import numpy as np
import ml_dtypes


def mxq(x, axis, fmt="e4m3"):
    dtype, down = {"e4m3": (ml_dtypes.float8_e4m3fn, 7), "e5m2": (ml_dtypes.float8_e5m2, 14)}[fmt]
    v = np.moveaxis(np.asarray(x, np.float32).astype(ml_dtypes.bfloat16).astype(np.float64), axis, -1)
    blocks = v.reshape(v.shape[:-1] + (-1, 32))
    amax = np.abs(blocks).max(-1, keepdims=True)
    byte = np.maximum(np.where(amax > 0, np.frexp(amax)[1] - 1 + 127, 0) - down, 1)
    scale = np.exp2(byte - 127.0)
    codes = (blocks / scale).astype(np.float32).astype(dtype).astype(np.float64)
    return np.moveaxis((codes * scale).reshape(v.shape), -1, axis)


WIDE = False


def mx_kscale(k):
    if not WIDE:
        return np.ones(k)
    levels = np.array([10, -10, 5, -5, 0])
    if k % 512:
        return np.exp2(np.random.permutation(np.resize(levels, k // 32))).repeat(32)
    a = np.empty((k // 512, 16))
    for p in range(k // 512):
        a[p, :8] = np.random.permutation(np.resize(levels, 8))
        for g in range(8):
            far = levels[np.abs(levels - a[p, g]) >= 10]
            a[p, g + 8] = far[np.random.randint(len(far))]
    return np.exp2(a.ravel()).repeat(32)


def f64(x):
    return np.asarray(x).astype(np.float64)


def striped(idx):
    return np.tile(idx.reshape(-1, 16).T, (8, 1)).astype(np.uint16)


def unstriped(offs):
    return offs[:16].T.reshape(-1).astype(np.int64)


E2M1 = np.array([0.0, 0.5, 1.0, 1.5, 2.0, 3.0, 4.0, 6.0, -0.0, -0.5, -1.0, -1.5, -2.0, -3.0, -4.0, -6.0])


def pack_weight(w, fmt):
    k, n = w.shape
    w = f64(np.asarray(w, np.float32).astype(ml_dtypes.bfloat16)).reshape(k // 32, 32, n)
    amax = np.abs(w).max(1)
    if fmt == "e4m3":
        byte = np.frexp(amax)[1] - 1 + 127 - 7
    else:
        mant, ex = np.frexp(amax / 6.0)
        byte = np.where(mant > 0.5, ex, ex - 1) + 127
    byte = np.clip(np.where(amax > 0, byte, 1), 1, 254)
    scaled = (w * np.exp2(127.0 - byte)[:, None, :]).reshape(k, n).astype(np.float32)
    by_word = np.ascontiguousarray(scaled.reshape(k // 512, 128, 4, n).transpose(0, 1, 3, 2))
    if fmt == "e4m3":
        words = by_word.astype(ml_dtypes.float8_e4m3fn).view(np.uint8)
    else:
        c = by_word.astype(ml_dtypes.float4_e2m1fn).view(np.uint8) & 0xF
        words = (c[..., 0::2] | (c[..., 1::2] << 4)).reshape(k // 512, 128, 2 * n)
    return np.ascontiguousarray(words), np.ascontiguousarray(byte.astype(np.uint8).reshape(k // 512, 16, n))


def unpack_weight(words, scales, fmt):
    g, _, n = scales.shape
    words = np.ascontiguousarray(words).reshape(g, 128, n, -1)
    if fmt == "e4m3":
        vals = words.view(ml_dtypes.float8_e4m3fn).astype(np.float64)
    else:
        nib = np.empty((g, 128, n, 4), np.uint8)
        nib[..., 0::2] = words & 0xF
        nib[..., 1::2] = words >> 4
        vals = E2M1[nib]
    vals = vals * np.repeat(np.exp2(scales.astype(np.float64) - 127.0), 8, axis=1)[..., None]
    return vals.transpose(0, 1, 3, 2).reshape(g * 512, n)


def gelu(v):
    return 0.5 * v * (1.0 + np.tanh(np.sqrt(2.0 / np.pi) * (v + 0.044715 * v**3)))


T, S, P, K, H, N = 4096, 1024, 512, 1024, 1024, 512

def setup_inputs():
    n = np.random.standard_normal
    s = mx_kscale(K)[:, None]
    u = mx_kscale(H)[:, None]
    tab_words, tab_scales = pack_weight(n((K, T)) * s, "e4m3")
    wg_words, wg_scales = pack_weight(n((K, H)) / np.sqrt(K) / s, "e2m1")
    duel = np.random.permutation(S)
    return {
        "tab_words": tab_words,
        "tab_scales": tab_scales,
        "offs": striped(np.random.permutation(T)[:S]),
        "pos1": striped(duel[:P]),
        "pos2": striped(duel[P:]),
        "w1": (n((K, H)) / np.sqrt(K) / s * u.T).astype(np.float32),
        "wg_words": wg_words,
        "wg_scales": wg_scales,
        "w2": (n((H, N)) / np.sqrt(H) / u).astype(np.float32),
        "c": (0.5 * n(N)).astype(np.float32),
    }

def reference(tab_words, tab_scales, offs, pos1, pos2, w1, wg_words, wg_scales, w2, c):
    v = unpack_weight(tab_words, tab_scales, "e4m3")[:, unstriped(offs)]
    wg = unpack_weight(wg_words, wg_scales, "e2m1")
    w1q = mxq(f64(w1), 0, "e4m3")
    h = (w1q.T @ v) * (wg.T @ v)
    a = h[:, unstriped(pos1)]
    b = h[:, unstriped(pos2)]
    z = mxq(a - b, 0, "e4m3")
    w2q = mxq(f64(w2), 0, "e4m3")
    y = (w2q.T @ z) + f64(c)[:, None]
    return 1.0 / (1.0 + np.exp(-y))

@@ -1,0 +1,332 @@
+from contextlib import ExitStack
+
+import concourse.mybir as mybir
+from concourse.masks import make_identity
+
+T, S, PAIRS, K, H, N = 4096, 1024, 512, 1024, 1024, 512
+FLOPS = 2 * (2 * K * H * S + H * N * PAIRS)
+
+F32 = mybir.dt.float32
+BF16 = mybir.dt.bfloat16
+I32 = mybir.dt.int32
+U32 = mybir.dt.uint32
+U16 = mybir.dt.uint16
+U8 = mybir.dt.uint8
+FP8X4 = mybir.dt.float8_e4m3fn_x4
+FP4X4 = mybir.dt.float4_e2m1fn_x4
+MULT = mybir.AluOpType.mult
+ADD = mybir.AluOpType.add
+SUB = mybir.AluOpType.subtract
+SIGMOID = mybir.ActivationFunctionType.Sigmoid
+
+P = 128
+TILES = H // P
+SPLIT_FROM = 7
+
+
+def tile_list_pairwise_document_ranking_kernel(
+    tc, tab_words, tab_scales, offs, pos1, pos2, w1, wg_words, wg_scales, w2, c, out
+):
+    nc = tc.nc
+    with ExitStack() as ctx:
+        keep = ctx.enter_context(tc.tile_pool(name="keep", bufs=1))
+        ring2 = ctx.enter_context(tc.tile_pool(name="ring2", bufs=2))
+        ring3 = ctx.enter_context(tc.tile_pool(name="ring3", bufs=3))
+        psum = ctx.enter_context(tc.psum_pool(name="psum", bufs=2))
+
+        offs_t = keep.tile([P, S // 16], U16, name="offs_t")
+        pos1_t = keep.tile([P, PAIRS // 16], U16, name="pos1_t")
+        pos2_t = keep.tile([P, PAIRS // 16], U16, name="pos2_t")
+        tab_sc = keep.tile([P, 2, T], U8, name="tab_sc", tag="slot_e", align_bytes=64)
+        wg_sc = keep.tile([P, 2, H], U8, name="wg_sc", align_bytes=64)
+        v_sc = [keep.tile([P, S], U8, name="v_sc%d" % a, align_bytes=64) for a in range(2)]
+        ident = keep.tile([P, P], F32, name="ident")
+        c_t = keep.tile([P, N // P], F32, name="c_t")
+
+        ident_made = keep.tile([P, P], F32, name="ident_made", tag="slot_b", align_bytes=64)
+        make_identity(nc, ident_made[:])
+        nc.vector.memset(tab_sc[:].bitcast(I32), 0)
+        nc.vector.memset(wg_sc[:].bitcast(I32), 0)
+        for q in range(4):
+            nc.scalar.dma_start(
+                out=tab_sc[32 * q : 32 * q + 4, :, :].bitcast(I32),
+                in_=tab_scales[:, 4 * q : 4 * q + 4, :].rearrange("a r t -> r a t").bitcast(I32),
+            )
+        for q in range(4):
+            nc.gpsimd.dma_start(
+                out=wg_sc[32 * q : 32 * q + 4, :, :].bitcast(I32),
+                in_=wg_scales[:, 4 * q : 4 * q + 4, :].rearrange("a r t -> r a t").bitcast(I32),
+            )
+        with nc.allow_non_contiguous_dma(reason="one bias value for each partition"):
+            nc.gpsimd.dma_start(out=c_t[:], in_=c.rearrange("(t p) -> p t", p=P))
+        nc.vector.tensor_copy(ident[:], ident_made[:])
+        warm = keep.tile([P, 1], F32, name="warm")
+        nc.scalar.activation(warm[:], ident[:, 0:1], SIGMOID)
+
+        w1_raw = {}
+
+        def load_w1(first, count, passes, tag):
+            raw = keep.tile(
+                [P, len(passes), 4, count * P], F32, name="w1_raw_%d_%d" % (first, passes[0]), tag=tag, align_bytes=64
+            )
+            for k, a in enumerate(passes):
+                nc.sync.dma_start(
+                    out=raw[:, k, :, :],
+                    in_=w1[512 * a : 512 * (a + 1), first * P : (first + count) * P].rearrange(
+                        "(p j) c -> p j c", j=4
+                    ),
+                )
+                for i in range(first, first + count):
+                    w1_raw[(i, a)] = raw[:, k, :, (i - first) * P : (i - first + 1) * P]
+
+        tab = {}
+
+        def load_tab(a, tag):
+            words = keep.tile([P, T], I32, name="tab%d" % a, tag=tag, align_bytes=64)
+            nc.sync.dma_start(out=words[:], in_=tab_words[a].rearrange("p t i -> p (t i)").bitcast(I32))
+            tab[a] = words
+
+        w2_raw = []
+
+        def load_w2(tag):
+            raw = keep.tile([P, 2, 4, N], F32, name="w2_raw", tag=tag, align_bytes=64)
+            for b in range(2):
+                nc.sync.dma_start(
+                    out=raw[:, b, :, :], in_=w2[512 * b : 512 * (b + 1), :].rearrange("(p j) n -> p j n", j=4)
+                )
+                w2_raw.append(raw[:, b, :, :])
+
+        def interleave(dst, src):
+            nc.scalar.copy(
+                out=dst.rearrange("p (c i) t -> p c t i", i=4),
+                in_=src.rearrange("p t (c i) -> p c t i", i=4),
+            )
+
+        v_words = {}
+
+        def gather_scales():
+            for a in range(2):
+                nc.vector.tensor_copy(v_sc[a][:], tab_sc[:, a, :].indirect(offs_t[:]))
+
+        def gather_words(a, halves):
+            width = S // halves
+            for h in range(halves):
+                words = keep.tile(
+                    [P, width], U32, name="v_words_%d_%d" % (a, h), tag="slot_e" if a == 0 else "", align_bytes=64
+                )
+                nc.vector.tensor_copy(
+                    words[:],
+                    tab[a][:].bitcast(U32).indirect(offs_t[:, h * width // 16 : (h + 1) * width // 16]),
+                )
+                for d in range(width // 512):
+                    v_words[(a, h * (width // 512) + d)] = words[:, 512 * d : 512 * (d + 1)]
+
+        w1_q = {}
+
+        def prep_w1(i):
+            grouped = ring2.tile([P, 2, P, 4], BF16, name="w1_grouped", align_bytes=64)
+            for a in range(2):
+                interleave(grouped[:, a, :, :], w1_raw[(i, a)])
+            codes = ring3.tile([P, 2 * P], U32, name="w1_codes", align_bytes=64)
+            scales = ring3.tile([P, 2 * P], U8, name="w1_scales", align_bytes=64)
+            nc.vector.quantize_mx(
+                out=codes[:].bitcast(FP8X4),
+                scales=scales[:],
+                in_=grouped[:].rearrange("p a c t -> p (a c t)"),
+            )
+            w1_q[i] = (codes, scales)
+
+        w2_q = {}
+
+        def prep_w2(b):
+            grouped = keep.tile([P, N, 4], BF16, name="w2_grouped%d" % b, align_bytes=64)
+            for h in range(2):
+                interleave(grouped[:, 256 * h : 256 * (h + 1), :], w2_raw[b][:, :, 256 * h : 256 * (h + 1)])
+            codes = keep.tile([P, N], U32, name="w2_codes%d" % b, align_bytes=64)
+            scales = keep.tile([P, N], U8, name="w2_scales%d" % b, align_bytes=64)
+            nc.vector.quantize_mx(
+                out=codes[:].bitcast(FP8X4), scales=scales[:], in_=grouped[:].rearrange("p c t -> p (c t)")
+            )
+            w2_q[b] = (codes, scales)
+
+        windows = {}
+        g_banks = {}
+        a_banks = {}
+
+        def gate_pass(i, d, a):
+            if a == 0:
+                g_banks[(i, d)] = psum.tile([P, 512], F32, name="g_bank", tag="g")
+            nc.tensor.matmul_mx(
+                out=g_banks[(i, d)][:],
+                lhsT=wg[:, a, 2 * P * i : 2 * P * (i + 1)].bitcast(FP4X4),
+                lhsT_scale=wg_sc[:, a, P * i : P * (i + 1)],
+                rhs=v_words[(a, d)].bitcast(FP8X4),
+                rhs_scale=v_sc[a][:, 512 * d : 512 * (d + 1)],
+                start=(a == 0),
+                stop=(a == 1),
+            )
+            if a == 1:
+                nc.scalar.copy(out=windows[i][:, S + 512 * d : S + 512 * (d + 1)], in_=g_banks[(i, d)][:])
+
+        def first_pass(i, d, a):
+            codes, scales = w1_q[i]
+            if a == 0:
+                a_banks[(i, d)] = psum.tile([P, 512], F32, name="a_bank", tag="a", bufs=4)
+            nc.tensor.matmul_mx(
+                out=a_banks[(i, d)][:],
+                lhsT=codes[:, P * a : P * (a + 1)].bitcast(FP8X4),
+                lhsT_scale=scales[:, P * a : P * (a + 1)],
+                rhs=v_words[(a, d)].bitcast(FP8X4),
+                rhs_scale=v_sc[a][:, 512 * d : 512 * (d + 1)],
+                start=(a == 0),
+                stop=(a == 1),
+            )
+
+        def products(i):
+            windows[i] = ring3.tile([P, 2 * S], F32, name="window")
+            for a in range(2):
+                for d in range(2):
+                    gate_pass(i, d, a)
+                    first_pass(i, d, a)
+
+        def features(i):
+            window = windows[i]
+            for d in range(2):
+                nc.vector.tensor_tensor(
+                    window[:, 512 * d : 512 * (d + 1)],
+                    a_banks[(i, d)][:],
+                    window[:, S + 512 * d : S + 512 * (d + 1)],
+                    MULT,
+                )
+
+        pieces = {0: [(0, 4)], 1: [(0, 2), (2, 2)]}
+        z_turned = {
+            (b, j0): keep.tile([P, nj, 2, 2 * P], BF16, name="z_turned_%d_%d" % (b, j0), align_bytes=64)
+            for b in range(2)
+            for (j0, nj) in pieces[b]
+        }
+
+        def turned_out(i, bank, bank_j0, j0, nj):
+            b, tau = divmod(i, 4)
+            nc.scalar.copy(
+                out=z_turned[(b, j0)][:, :, :, 64 * tau : 64 * (tau + 1)].rearrange("j b u (m e) -> j b u m e", e=2),
+                in_=bank[:, j0 - bank_j0 : j0 - bank_j0 + nj, :].rearrange("j b (m u e) -> j b u m e", u=2, e=2),
+            )
+
+        def pairs_whole(i):
+            window = windows[i]
+            first = ring2.tile([P, PAIRS], F32, name="first")
+            nc.vector.tensor_copy(first[:], window[:].indirect(pos1_t[:]))
+            second = ring2.tile([P, PAIRS], F32, name="second")
+            nc.vector.tensor_scalar(second[:], window[:].indirect(pos2_t[:]), -1.0, 0.0, MULT, ADD)
+            bank = psum.tile([P, 4, P], F32, name="zt_bank", tag="zt")
+            for jb in range(4):
+                cols = slice(P * jb, P * (jb + 1))
+                nc.tensor.matmul(bank[:, jb, :], first[:, cols], ident[:], start=True, stop=False, is_transpose=True)
+                nc.tensor.matmul(bank[:, jb, :], second[:, cols], ident[:], start=False, stop=True, is_transpose=True)
+            for j0, nj in pieces[i // 4]:
+                turned_out(i, bank, 0, j0, nj)
+
+        def pairs_half(i, h):
+            window = windows[i]
+            cols16 = slice(16 * h, 16 * (h + 1))
+            second = keep.tile([P, 256], F32, name="second_half", tag="second_half")
+            nc.vector.tensor_copy(second[:], window[:].indirect(pos2_t[:, cols16]))
+            diff = ring2.tile([P, 256], F32, name="diff_half")
+            nc.vector.tensor_tensor(diff[:], window[:].indirect(pos1_t[:, cols16]), second[:], SUB)
+            bank = psum.tile([P, 2, P], F32, name="zt_bank_half", tag="zt")
+            for jb in range(2):
+                nc.tensor.transpose(bank[:, jb, :], diff[:, P * jb : P * (jb + 1)], ident[:])
+            turned_out(i, bank, 2 * h, 2 * h, 2)
+
+        z_q = {}
+
+        def quantise_z(b, j0, nj, copy):
+            words = z_turned[(b, j0)][:].bitcast(F32)
+            grouped = keep.tile([P, nj * P, 4], BF16, name="z_grouped_%d_%d" % (b, j0), align_bytes=64)
+            grouped_words = grouped[:].bitcast(F32)
+            for g in range(nj // 2):
+                bank = psum.tile([P, 2, 2, P], F32, name="back_bank", tag="zt")
+                for jb in range(2):
+                    for u in range(2):
+                        nc.tensor.transpose(bank[:, jb, u, :], words[:, 2 * g + jb, u, :], ident[:])
+                copy(
+                    out=grouped_words[:, 256 * g : 256 * (g + 1), :].rearrange("p (b j) u -> p b j u", b=2),
+                    in_=bank[:].rearrange("p b u j -> p b j u"),
+                )
+            codes = keep.tile([P, nj * P], U32, name="z_codes_%d_%d" % (b, j0), align_bytes=64)
+            scales = keep.tile([P, nj * P], U8, name="z_scales_%d_%d" % (b, j0), align_bytes=64)
+            nc.vector.quantize_mx(
+                out=codes[:].bitcast(FP8X4), scales=scales[:], in_=grouped[:].rearrange("p c t -> p (c t)")
+            )
+            for g in range(nj // 2):
+                cols = slice(256 * g, 256 * (g + 1))
+                z_q[(b, j0 // 2 + g)] = (codes[:, cols], scales[:, cols])
+
+        out_view = out.rearrange("(t p) j -> p t j", p=P)
+
+        def scores(h, group):
+            for first in range(0, N // P, group):
+                result = keep.tile([P, group, 256], F32, name="result_%d_%d" % (h, first))
+                for k in range(group):
+                    nt = first + k
+                    bank = psum.tile([P, 256], F32, name="y_bank", tag="a", bufs=4)
+                    for b in range(2):
+                        w_codes, w_scales = w2_q[b]
+                        z_codes, z_scales = z_q[(b, h)]
+                        nc.tensor.matmul_mx(
+                            out=bank[:],
+                            lhsT=w_codes[:, P * nt : P * (nt + 1)].bitcast(FP8X4),
+                            lhsT_scale=w_scales[:, P * nt : P * (nt + 1)],
+                            rhs=z_codes.bitcast(FP8X4),
+                            rhs_scale=z_scales,
+                            start=(b == 0),
+                            stop=(b == 1),
+                        )
+                    nc.scalar.activation(result[:, k, :], bank[:], SIGMOID, bias=c_t[:, nt : nt + 1])
+                nc.sync.dma_start(
+                    out=out_view[:, first : first + group, 256 * h : 256 * (h + 1)], in_=result[:]
+                )
+
+        nc.sync.dma_start(offs_t[:], offs)
+        nc.sync.dma_start(pos1_t[:], pos1)
+        nc.sync.dma_start(pos2_t[:], pos2)
+        load_tab(0, "slot_a")
+        load_w1(0, 1, [0], "slot_c")
+        load_w1(0, 1, [1], "slot_d")
+        gather_scales()
+        load_tab(1, "slot_b")
+        gather_words(0, 1)
+        prep_w1(0)
+        wg = keep.tile([P, 2, 2 * H], U8, name="wg", tag="slot_c", align_bytes=64)
+        nc.sync.dma_start(out=wg[:].bitcast(I32), in_=wg_words.rearrange("a p n -> p a n").bitcast(I32))
+        load_w1(1, 1, [0, 1], "slot_d")
+        gather_words(1, 2)
+        load_w1(2, 2, [0, 1], "slot_b")
+        products(0)
+        prep_w1(1)
+        load_w1(4, 4, [0, 1], "slot_d")
+        products(1)
+        prep_w1(2)
+        for i in range(TILES):
+            features(i)
+            if i + 2 < TILES:
+                products(i + 2)
+            if i + 3 < TILES:
+                prep_w1(i + 3)
+            if i == 0:
+                load_w2("slot_b")
+            if i < SPLIT_FROM:
+                pairs_whole(i)
+            else:
+                pairs_half(i, 0)
+            if i == 3:
+                quantise_z(0, 0, 4, nc.scalar.copy)
+            if i in (4, 5):
+                prep_w2(i - 4)
+        quantise_z(1, 0, 2, nc.scalar.copy)
+        for i in range(SPLIT_FROM, TILES):
+            pairs_half(i, 1)
+        quantise_z(1, 2, 2, nc.vector.tensor_copy)
+        scores(0, 2)
+        scores(1, 1)

@@ -41,7 +41,6 @@ def tile_list_pairwise_document_ranking_kernel(
         wg_sc = keep.tile([P, 2, H], U8, name="wg_sc", align_bytes=64)
         v_sc = [keep.tile([P, S], U8, name="v_sc%d" % a, align_bytes=64) for a in range(2)]
         ident = keep.tile([P, P], F32, name="ident")
-        c_t = keep.tile([P, N // P], F32, name="c_t")
 
         ident_made = keep.tile([P, P], F32, name="ident_made", tag="slot_b", align_bytes=64)
         make_identity(nc, ident_made[:])
@@ -57,8 +56,6 @@ def tile_list_pairwise_document_ranking_kernel(
                 out=wg_sc[32 * q : 32 * q + 4, :, :].bitcast(I32),
                 in_=wg_scales[:, 4 * q : 4 * q + 4, :].rearrange("a r t -> r a t").bitcast(I32),
             )
-        with nc.allow_non_contiguous_dma(reason="one bias value for each partition"):
-            nc.gpsimd.dma_start(out=c_t[:], in_=c.rearrange("(t p) -> p t", p=P))
         nc.vector.tensor_copy(ident[:], ident_made[:])
         warm = keep.tile([P, 1], F32, name="warm")
         nc.scalar.activation(warm[:], ident[:, 0:1], SIGMOID)
@@ -98,8 +95,8 @@ def tile_list_pairwise_document_ranking_kernel(
 
         def interleave(dst, src):
             nc.scalar.copy(
-                out=dst.rearrange("p (c i) t -> p c t i", i=4),
-                in_=src.rearrange("p t (c i) -> p c t i", i=4),
+                out=dst.rearrange("p (c i) t -> p c t i", i=2),
+                in_=src.rearrange("p t (c i) -> p c t i", i=2),
             )
 
         v_words = {}
@@ -184,10 +181,12 @@ def tile_list_pairwise_document_ranking_kernel(
 
         def products(i):
             windows[i] = ring3.tile([P, 2 * S], F32, name="window")
-            for a in range(2):
-                for d in range(2):
-                    gate_pass(i, d, a)
-                    first_pass(i, d, a)
+            if i == 0:
+                steps = [(one, d, a) for a in range(2) for d in range(2) for one in (gate_pass, first_pass)]
+            else:
+                steps = [(one, d, a) for one in (gate_pass, first_pass) for d in range(2) for a in range(2)]
+            for one, d, a in steps:
+                one(i, d, a)
 
         def features(i):
             window = windows[i]
@@ -324,6 +323,9 @@ def tile_list_pairwise_document_ranking_kernel(
                 quantise_z(0, 0, 4, nc.scalar.copy)
             if i in (4, 5):
                 prep_w2(i - 4)
+        c_t = keep.tile([P, N // P], F32, name="c_t", tag="slot_d", align_bytes=64)
+        with nc.allow_non_contiguous_dma(reason="one bias value for each partition"):
+            nc.sync.dma_start(out=c_t[:], in_=c.rearrange("(t p) -> p t", p=P))
         quantise_z(1, 0, 2, nc.scalar.copy)
         for i in range(SPLIT_FROM, TILES):
             pairs_half(i, 1)

@@ -20,6 +20,7 @@ SUB = mybir.AluOpType.subtract
 SIGMOID = mybir.ActivationFunctionType.Sigmoid
 
 P = 128
+KIB = 1024
 TILES = H // P
 SPLIT_FROM = 7
 
@@ -30,6 +31,7 @@ def tile_list_pairwise_document_ranking_kernel(
     nc = tc.nc
     with ExitStack() as ctx:
         keep = ctx.enter_context(tc.tile_pool(name="keep", bufs=1))
+        staged = ctx.enter_context(tc.tile_pool(name="staged", bufs=1))
         ring2 = ctx.enter_context(tc.tile_pool(name="ring2", bufs=2))
         ring3 = ctx.enter_context(tc.tile_pool(name="ring3", bufs=3))
         psum = ctx.enter_context(tc.psum_pool(name="psum", bufs=2))
@@ -37,56 +39,52 @@ def tile_list_pairwise_document_ranking_kernel(
         offs_t = keep.tile([P, S // 16], U16, name="offs_t")
         pos1_t = keep.tile([P, PAIRS // 16], U16, name="pos1_t")
         pos2_t = keep.tile([P, PAIRS // 16], U16, name="pos2_t")
-        tab_sc = keep.tile([P, 2, T], U8, name="tab_sc", tag="slot_e", align_bytes=64)
-        wg_sc = keep.tile([P, 2, H], U8, name="wg_sc", align_bytes=64)
+        tab_sc = keep.tile([P, T], U8, name="tab_sc", tag="slot_e", align_bytes=64)
         v_sc = [keep.tile([P, S], U8, name="v_sc%d" % a, align_bytes=64) for a in range(2)]
         ident = keep.tile([P, P], F32, name="ident")
 
-        ident_made = keep.tile([P, P], F32, name="ident_made", tag="slot_b", align_bytes=64)
-        make_identity(nc, ident_made[:])
+        wg_sc = keep.tile([P, 2, H], U8, name="wg_sc", align_bytes=64)
+        ident_made = staged.tile([P, 26 * KIB // 4], F32, name="ident_made", offset=0, align_bytes=64)
+        tab = [keep.tile([P, T], I32, name="tab0", align_bytes=64)]
+        make_identity(nc, ident_made[:, 0:P])
         nc.vector.memset(tab_sc[:].bitcast(I32), 0)
         nc.vector.memset(wg_sc[:].bitcast(I32), 0)
+        nc.vector.memset(v_sc[1][:].bitcast(I32), 0)
+        nc.vector.tensor_copy(ident[:], ident_made[:, 0:P])
         for q in range(4):
             nc.scalar.dma_start(
-                out=tab_sc[32 * q : 32 * q + 4, :, :].bitcast(I32),
-                in_=tab_scales[:, 4 * q : 4 * q + 4, :].rearrange("a r t -> r a t").bitcast(I32),
+                out=tab_sc[32 * q : 32 * q + 8, :].bitcast(I32),
+                in_=tab_scales[:, 4 * q : 4 * q + 4, :].bitcast(I32),
             )
         for q in range(4):
             nc.gpsimd.dma_start(
                 out=wg_sc[32 * q : 32 * q + 4, :, :].bitcast(I32),
                 in_=wg_scales[:, 4 * q : 4 * q + 4, :].rearrange("a r t -> r a t").bitcast(I32),
             )
-        nc.vector.tensor_copy(ident[:], ident_made[:])
         warm = keep.tile([P, 1], F32, name="warm")
         nc.scalar.activation(warm[:], ident[:, 0:1], SIGMOID)
 
         w1_raw = {}
 
-        def load_w1(first, count, passes, tag):
-            raw = keep.tile(
-                [P, len(passes), 4, count * P], F32, name="w1_raw_%d_%d" % (first, passes[0]), tag=tag, align_bytes=64
-            )
-            for k, a in enumerate(passes):
+        def load_w1(first, count, offset):
+            raw = staged.tile([P, 2, 4, count * P], F32, name="w1_raw_%d" % first, offset=offset, align_bytes=64)
+            for a in range(2):
                 nc.sync.dma_start(
-                    out=raw[:, k, :, :],
+                    out=raw[:, a, :, :],
                     in_=w1[512 * a : 512 * (a + 1), first * P : (first + count) * P].rearrange(
                         "(p j) c -> p j c", j=4
                     ),
                 )
                 for i in range(first, first + count):
-                    w1_raw[(i, a)] = raw[:, k, :, (i - first) * P : (i - first + 1) * P]
-
-        tab = {}
-
-        def load_tab(a, tag):
-            words = keep.tile([P, T], I32, name="tab%d" % a, tag=tag, align_bytes=64)
-            nc.sync.dma_start(out=words[:], in_=tab_words[a].rearrange("p t i -> p (t i)").bitcast(I32))
-            tab[a] = words
+                    w1_raw[(i, a)] = raw[:, a, :, (i - first) * P : (i - first + 1) * P]
 
         w2_raw = []
 
-        def load_w2(tag):
-            raw = keep.tile([P, 2, 4, N], F32, name="w2_raw", tag=tag, align_bytes=64)
+        def load_tab(a):
+            nc.sync.dma_start(out=tab[a][:], in_=tab_words[a].rearrange("p t i -> p (t i)").bitcast(I32))
+
+        def load_w2(offset):
+            raw = staged.tile([P, 2, 4, N], F32, name="w2_raw", offset=offset, align_bytes=64)
             for b in range(2):
                 nc.sync.dma_start(
                     out=raw[:, b, :, :], in_=w2[512 * b : 512 * (b + 1), :].rearrange("(p j) n -> p j n", j=4)
@@ -102,8 +100,12 @@ def tile_list_pairwise_document_ranking_kernel(
         v_words = {}
 
         def gather_scales():
-            for a in range(2):
-                nc.vector.tensor_copy(v_sc[a][:], tab_sc[:, a, :].indirect(offs_t[:]))
+            nc.vector.tensor_copy(v_sc[0][:], tab_sc[:].indirect(offs_t[:]))
+            for q in range(4):
+                nc.scalar.dma_start(
+                    out=v_sc[1][32 * q : 32 * q + 4, :].bitcast(I32),
+                    in_=v_sc[0][32 * q + 4 : 32 * q + 8, :].bitcast(I32),
+                )
 
         def gather_words(a, halves):
             width = S // halves
@@ -290,21 +292,21 @@ def tile_list_pairwise_document_ranking_kernel(
         nc.sync.dma_start(offs_t[:], offs)
         nc.sync.dma_start(pos1_t[:], pos1)
         nc.sync.dma_start(pos2_t[:], pos2)
-        load_tab(0, "slot_a")
-        load_w1(0, 1, [0], "slot_c")
-        load_w1(0, 1, [1], "slot_d")
+        load_tab(0)
+        load_w1(0, 1, 22 * KIB)
+        tab.append(staged.tile([P, T], I32, name="tab1", offset=0, align_bytes=64))
+        load_tab(1)
+        wg = staged.tile([P, 2, 2 * H], U8, name="wg", offset=16 * KIB, align_bytes=64)
+        nc.sync.dma_start(out=wg[:].bitcast(I32), in_=wg_words.rearrange("a p n -> p a n").bitcast(I32))
         gather_scales()
-        load_tab(1, "slot_b")
         gather_words(0, 1)
         prep_w1(0)
-        wg = keep.tile([P, 2, 2 * H], U8, name="wg", tag="slot_c", align_bytes=64)
-        nc.sync.dma_start(out=wg[:].bitcast(I32), in_=wg_words.rearrange("a p n -> p a n").bitcast(I32))
-        load_w1(1, 1, [0, 1], "slot_d")
+        load_w1(1, 1, 20 * KIB)
+        load_w1(2, 2, 24 * KIB)
         gather_words(1, 2)
-        load_w1(2, 2, [0, 1], "slot_b")
+        load_w1(4, 4, 0)
         products(0)
         prep_w1(1)
-        load_w1(4, 4, [0, 1], "slot_d")
         products(1)
         prep_w1(2)
         for i in range(TILES):
@@ -314,7 +316,7 @@ def tile_list_pairwise_document_ranking_kernel(
             if i + 3 < TILES:
                 prep_w1(i + 3)
             if i == 0:
-                load_w2("slot_b")
+                load_w2(24 * KIB)
             if i < SPLIT_FROM:
                 pairs_whole(i)
             else:
@@ -323,7 +325,7 @@ def tile_list_pairwise_document_ranking_kernel(
                 quantise_z(0, 0, 4, nc.scalar.copy)
             if i in (4, 5):
                 prep_w2(i - 4)
-        c_t = keep.tile([P, N // P], F32, name="c_t", tag="slot_d", align_bytes=64)
+        c_t = staged.tile([P, N // P], F32, name="c_t", offset=0, align_bytes=64)
         with nc.allow_non_contiguous_dma(reason="one bias value for each partition"):
             nc.sync.dma_start(out=c_t[:], in_=c.rearrange("(t p) -> p t", p=P))
         quantise_z(1, 0, 2, nc.scalar.copy)

@@ -21,8 +21,7 @@ SIGMOID = mybir.ActivationFunctionType.Sigmoid
 
 P = 128
 KIB = 1024
-TILES = H // P
-SPLIT_FROM = 7
+HALF = PAIRS // 2
 
 
 def tile_list_pairwise_document_ranking_kernel(
@@ -32,9 +31,15 @@ def tile_list_pairwise_document_ranking_kernel(
     with ExitStack() as ctx:
         keep = ctx.enter_context(tc.tile_pool(name="keep", bufs=1))
         staged = ctx.enter_context(tc.tile_pool(name="staged", bufs=1))
-        ring2 = ctx.enter_context(tc.tile_pool(name="ring2", bufs=2))
-        ring3 = ctx.enter_context(tc.tile_pool(name="ring3", bufs=3))
-        psum = ctx.enter_context(tc.psum_pool(name="psum", bufs=2))
+        weave = ctx.enter_context(tc.tile_pool(name="weave", bufs=1))
+        psum = ctx.enter_context(tc.psum_pool(name="psum", bufs=1))
+
+        def bank_tile(name, shape, bank):
+            return psum.tile(shape, F32, name=name, offset=2 * KIB * bank)
+
+        GATE_BANK, SUM_BANK, TURN_BANK = 0, 2, 6
+        WINDOW_PLACE = [32 * KIB, 40 * KIB, 56 * KIB, 48 * KIB, 43 * KIB, 60 * KIB, 32 * KIB, 64 * KIB]
+        GATE_PLACE = {4: 32 * KIB, 5: 36 * KIB, 6: 72 * KIB, 7: 68 * KIB}
 
         offs_t = keep.tile([P, S // 16], U16, name="offs_t")
         pos1_t = keep.tile([P, PAIRS // 16], U16, name="pos1_t")
@@ -42,70 +47,63 @@ def tile_list_pairwise_document_ranking_kernel(
         tab_sc = keep.tile([P, T], U8, name="tab_sc", tag="slot_e", align_bytes=64)
         v_sc = [keep.tile([P, S], U8, name="v_sc%d" % a, align_bytes=64) for a in range(2)]
         ident = keep.tile([P, P], F32, name="ident")
-
         wg_sc = keep.tile([P, 2, H], U8, name="wg_sc", align_bytes=64)
-        ident_made = staged.tile([P, 26 * KIB // 4], F32, name="ident_made", offset=0, align_bytes=64)
-        tab = [keep.tile([P, T], I32, name="tab0", align_bytes=64)]
-        make_identity(nc, ident_made[:, 0:P])
+        zeros = staged.tile([P, 48 * KIB // 4], I32, name="zeros", offset=0, align_bytes=64)
+        tab = [staged.tile([P, T], I32, name="tab0", offset=48 * KIB, align_bytes=64)]
+        make_identity(nc, ident[:])
         nc.vector.memset(tab_sc[:].bitcast(I32), 0)
         nc.vector.memset(wg_sc[:].bitcast(I32), 0)
-        nc.vector.memset(v_sc[1][:].bitcast(I32), 0)
-        nc.vector.tensor_copy(ident[:], ident_made[:, 0:P])
-        for q in range(4):
-            nc.scalar.dma_start(
-                out=tab_sc[32 * q : 32 * q + 8, :].bitcast(I32),
-                in_=tab_scales[:, 4 * q : 4 * q + 4, :].bitcast(I32),
-            )
+        nc.vector.memset(zeros[:, 0 : S // 4], 0)
+        nc.vector.tensor_copy(v_sc[1][:].bitcast(I32), zeros[:, 0 : S // 4])
+        scale_rows = tab_scales.bitcast(I32).rearrange("a (q r) t -> r q a t", r=4)
+        for r in range(4):
+            nc.scalar.dma_start(out=tab_sc[r:P:16, :].bitcast(I32), in_=scale_rows[r])
         for q in range(4):
             nc.gpsimd.dma_start(
                 out=wg_sc[32 * q : 32 * q + 4, :, :].bitcast(I32),
                 in_=wg_scales[:, 4 * q : 4 * q + 4, :].rearrange("a r t -> r a t").bitcast(I32),
             )
-        warm = keep.tile([P, 1], F32, name="warm")
-        nc.scalar.activation(warm[:], ident[:, 0:1], SIGMOID)
+
+        def load_tab(a):
+            nc.sync.dma_start(out=tab[a][:, 0:T], in_=tab_words[a].rearrange("p t i -> p (t i)").bitcast(I32))
 
         w1_raw = {}
 
         def load_w1(first, count, offset):
-            raw = staged.tile([P, 2, 4, count * P], F32, name="w1_raw_%d" % first, offset=offset, align_bytes=64)
             for a in range(2):
+                raw = staged.tile(
+                    [P, 4, count * P], F32, name="w1_raw_%d_%d" % (first, a),
+                    offset=offset + a * count * 2 * KIB, align_bytes=64,
+                )
                 nc.sync.dma_start(
-                    out=raw[:, a, :, :],
+                    out=raw[:],
                     in_=w1[512 * a : 512 * (a + 1), first * P : (first + count) * P].rearrange(
                         "(p j) c -> p j c", j=4
                     ),
                 )
                 for i in range(first, first + count):
-                    w1_raw[(i, a)] = raw[:, a, :, (i - first) * P : (i - first + 1) * P]
+                    if i < 4:
+                        cols = raw[:, :, (i - first) * P : (i - first + 1) * P]
+                        w1_raw[(i, a)] = cols.rearrange("p j (g i) -> p g j i", i=4)
+                    else:
+                        w1_raw[(i, a)] = raw[:].rearrange("p j (q t e) -> p t q j e", t=4, e=8)[:, i - 4]
 
         w2_raw = []
 
-        def load_tab(a):
-            nc.sync.dma_start(out=tab[a][:], in_=tab_words[a].rearrange("p t i -> p (t i)").bitcast(I32))
-
         def load_w2(offset):
-            raw = staged.tile([P, 2, 4, N], F32, name="w2_raw", offset=offset, align_bytes=64)
-            for b in range(2):
-                nc.sync.dma_start(
-                    out=raw[:, b, :, :], in_=w2[512 * b : 512 * (b + 1), :].rearrange("(p j) n -> p j n", j=4)
-                )
-                w2_raw.append(raw[:, b, :, :])
-
-        def interleave(dst, src):
-            nc.scalar.copy(
-                out=dst.rearrange("p (c i) t -> p c t i", i=2),
-                in_=src.rearrange("p t (c i) -> p c t i", i=2),
-            )
+            natural = staged.tile([P, 4, N], F32, name="w2_raw0", offset=offset, align_bytes=64)
+            nc.sync.dma_start(out=natural[:], in_=w2[0:512, :].rearrange("(p j) n -> p j n", j=4))
+            dealt = staged.tile([P, 4, N], F32, name="w2_raw1", offset=offset + 8 * KIB, align_bytes=64)
+            rows = w2[512:1024, :].rearrange("(q t e) n -> t q e n", t=4, e=8)
+            for t in range(4):
+                nc.sync.dma_start(out=dealt[:, t, :], in_=rows[t])
+            w2_raw.extend([natural, dealt])
 
         v_words = {}
 
         def gather_scales():
             nc.vector.tensor_copy(v_sc[0][:], tab_sc[:].indirect(offs_t[:]))
-            for q in range(4):
-                nc.scalar.dma_start(
-                    out=v_sc[1][32 * q : 32 * q + 4, :].bitcast(I32),
-                    in_=v_sc[0][32 * q + 4 : 32 * q + 8, :].bitcast(I32),
-                )
+            nc.scalar.dma_start(out=v_sc[1][0:112, :].bitcast(I32), in_=v_sc[0][16:128, :].bitcast(I32))
 
         def gather_words(a, halves):
             width = S // halves
@@ -115,66 +113,110 @@ def tile_list_pairwise_document_ranking_kernel(
                 )
                 nc.vector.tensor_copy(
                     words[:],
-                    tab[a][:].bitcast(U32).indirect(offs_t[:, h * width // 16 : (h + 1) * width // 16]),
+                    tab[a][:, 0:T].bitcast(U32).indirect(offs_t[:, h * width // 16 : (h + 1) * width // 16]),
                 )
                 for d in range(width // 512):
                     v_words[(a, h * (width // 512) + d)] = words[:, 512 * d : 512 * (d + 1)]
 
+        def quantise(name, grouped, width, place=None):
+            if place is None:
+                codes = keep.tile([P, width], U32, name="codes_" + name, align_bytes=64)
+            else:
+                codes = weave.tile([P, width], U32, name="codes_" + name, offset=place, align_bytes=64)
+            scales = keep.tile([P, width], U8, name="scales_" + name, align_bytes=64)
+            nc.vector.quantize_mx(out=codes[:].bitcast(FP8X4), scales=scales[:], in_=grouped)
+            return codes, scales
+
         w1_q = {}
 
+        def round_w1(copy, dst, i, a):
+            if i < 4:
+                view = dst.rearrange("p (g i) j -> p g j i", i=4)
+            else:
+                view = dst.rearrange("p (q e) j -> p q j e", e=8)
+            copy(out=view, in_=w1_raw[(i, a)])
+
+        def prep_w1_first():
+            early = keep.tile([P, P, 4], BF16, name="w1_grouped_0_0", align_bytes=64)
+            late = staged.tile([P, P, 4], BF16, name="w1_grouped_0_1", offset=36 * KIB, align_bytes=64)
+            for a, grouped, copy in ((0, early, nc.scalar.copy), (1, late, nc.vector.tensor_copy)):
+                round_w1(copy, grouped[:], 0, a)
+                pool, place = ((staged, 37 * KIB), (weave, w1_place(1)))[a]
+                codes = pool.tile([P, P], U32, name="codes_w1_0_%d" % a, offset=place, align_bytes=64)
+                scales = keep.tile([P, P], U8, name="scales_w1_0_%d" % a, align_bytes=64)
+                nc.vector.quantize_mx(
+                    out=codes[:].bitcast(FP8X4), scales=scales[:], in_=grouped[:].rearrange("p c j -> p (c j)")
+                )
+                w1_q[(0, a)] = (codes[:], scales[:])
+
+        def w1_place(i):
+            return 2 * KIB * i if i < 4 else WINDOW_PLACE[1] + 2 * KIB * (i - 4)
+
+        W2_PLACE = [47 * KIB, 32 * KIB]
+
+        def pool_round(out, in_):
+            nc.gpsimd.tensor_scalar(out, in_, 1.0, 0.0, MULT, ADD)
+
         def prep_w1(i):
-            grouped = ring2.tile([P, 2, P, 4], BF16, name="w1_grouped", align_bytes=64)
+            reach = 4 if i < 3 else 2
+            span = weave.tile([P, reach, P, 4], BF16, name="w1_grouped_%d" % i, offset=w1_place(i), align_bytes=64)
+            grouped = span[:, 0:2, :, :]
             for a in range(2):
-                interleave(grouped[:, a, :, :], w1_raw[(i, a)])
-            codes = ring3.tile([P, 2 * P], U32, name="w1_codes", align_bytes=64)
-            scales = ring3.tile([P, 2 * P], U8, name="w1_scales", align_bytes=64)
-            nc.vector.quantize_mx(
-                out=codes[:].bitcast(FP8X4),
-                scales=scales[:],
-                in_=grouped[:].rearrange("p a c t -> p (a c t)"),
-            )
-            w1_q[i] = (codes, scales)
+                if a == 0 and i in (4, 5):
+                    pool_round(
+                        grouped[:, a, :, :].rearrange("p (q e) j -> p q e j", e=8),
+                        w1_raw[(i, a)].rearrange("p q j e -> p q e j"),
+                    )
+                else:
+                    round_w1(nc.scalar.copy, grouped[:, a, :, :], i, a)
+            codes, scales = quantise("w1_%d" % i, grouped.rearrange("p a c j -> p (a c j)"), 2 * P)
+            for a in range(2):
+                w1_q[(i, a)] = (codes[:, P * a : P * (a + 1)], scales[:, P * a : P * (a + 1)])
 
         w2_q = {}
 
-        def prep_w2(b):
-            grouped = keep.tile([P, N, 4], BF16, name="w2_grouped%d" % b, align_bytes=64)
-            for h in range(2):
-                interleave(grouped[:, 256 * h : 256 * (h + 1), :], w2_raw[b][:, :, 256 * h : 256 * (h + 1)])
-            codes = keep.tile([P, N], U32, name="w2_codes%d" % b, align_bytes=64)
-            scales = keep.tile([P, N], U8, name="w2_scales%d" % b, align_bytes=64)
-            nc.vector.quantize_mx(
-                out=codes[:].bitcast(FP8X4), scales=scales[:], in_=grouped[:].rearrange("p c t -> p (c t)")
+        def round_w2(b):
+            grouped = weave.tile([P, N, 4], BF16, name="w2_grouped%d" % b, offset=W2_PLACE[b], align_bytes=64)
+            if b == 0:
+                pool_round(grouped[:, 0:384, :], w2_raw[b][:, :, 0:384].rearrange("p j c -> p c j"))
+            for cols in ([slice(384, N)], [slice(0, 256), slice(256, N)])[b]:
+                nc.scalar.copy(
+                    out=grouped[:, cols, :].rearrange("p (g i) j -> p g j i", i=4),
+                    in_=w2_raw[b][:, :, cols].rearrange("p j (g i) -> p g j i", i=4),
+                )
+            return grouped[:].rearrange("p c j -> p (c j)")
+
+        gate_w = {}
+
+        def deal_wg():
+            words = staged.tile([P, 2, 4, 2 * P], U8, name="wg_dealt", offset=33 * KIB, align_bytes=64)
+            nc.vector.tensor_copy(
+                words[:].bitcast(I32).rearrange("p a t (q w) -> p a t q w", w=4),
+                wg[:, :, H : 2 * H].bitcast(I32).rearrange("p a (q t w) -> p a t q w", t=4, w=4),
             )
-            w2_q[b] = (codes, scales)
+            scales = staged.tile([P, 2, 4, P], U8, name="wg_sc_dealt", offset=35 * KIB, align_bytes=64)
+            nc.vector.tensor_copy(
+                scales[:].bitcast(I32).rearrange("p a t (q w) -> p a t q w", w=2),
+                wg_sc[:, :, 512:H].bitcast(I32).rearrange("p a (q t w) -> p a t q w", t=4, w=2),
+            )
+            for a in range(2):
+                for t in range(4):
+                    gate_w[(t, a)] = (wg[:, a, 2 * P * t : 2 * P * (t + 1)], wg_sc[:, a, P * t : P * (t + 1)])
+                    gate_w[(4 + t, a)] = (words[:, a, t, :], scales[:, a, t, :])
 
         windows = {}
-        g_banks = {}
         a_banks = {}
+        gates = {}
 
-        def gate_pass(i, d, a):
-            if a == 0:
-                g_banks[(i, d)] = psum.tile([P, 512], F32, name="g_bank", tag="g")
-            nc.tensor.matmul_mx(
-                out=g_banks[(i, d)][:],
-                lhsT=wg[:, a, 2 * P * i : 2 * P * (i + 1)].bitcast(FP4X4),
-                lhsT_scale=wg_sc[:, a, P * i : P * (i + 1)],
-                rhs=v_words[(a, d)].bitcast(FP8X4),
-                rhs_scale=v_sc[a][:, 512 * d : 512 * (d + 1)],
-                start=(a == 0),
-                stop=(a == 1),
-            )
-            if a == 1:
-                nc.scalar.copy(out=windows[i][:, S + 512 * d : S + 512 * (d + 1)], in_=g_banks[(i, d)][:])
+        def placed(name, width, offset):
+            return weave.tile([P, width], F32, name=name, offset=offset, align_bytes=64)[:]
 
-        def first_pass(i, d, a):
-            codes, scales = w1_q[i]
-            if a == 0:
-                a_banks[(i, d)] = psum.tile([P, 512], F32, name="a_bank", tag="a", bufs=4)
+        def first_stage_pass(bank, weights, fmt, d, a):
+            codes, scales = weights
             nc.tensor.matmul_mx(
-                out=a_banks[(i, d)][:],
-                lhsT=codes[:, P * a : P * (a + 1)].bitcast(FP8X4),
-                lhsT_scale=scales[:, P * a : P * (a + 1)],
+                out=bank[:],
+                lhsT=codes.bitcast(fmt),
+                lhsT_scale=scales,
                 rhs=v_words[(a, d)].bitcast(FP8X4),
                 rhs_scale=v_sc[a][:, 512 * d : 512 * (d + 1)],
                 start=(a == 0),
@@ -182,155 +224,215 @@ def tile_list_pairwise_document_ranking_kernel(
             )
 
         def products(i):
-            windows[i] = ring3.tile([P, 2 * S], F32, name="window")
-            if i == 0:
-                steps = [(one, d, a) for a in range(2) for d in range(2) for one in (gate_pass, first_pass)]
-            else:
-                steps = [(one, d, a) for one in (gate_pass, first_pass) for d in range(2) for a in range(2)]
-            for one, d, a in steps:
-                one(i, d, a)
+            if i < 4:
+                windows[i] = weave.tile([P, 2 * S], F32, name="window_%d" % i, offset=WINDOW_PLACE[i], align_bytes=64)
+            for d in range(2):
+                bank = bank_tile("g_bank_%d_%d" % (i, d), [P, 512], GATE_BANK + d)
+                for a in range(2):
+                    first_stage_pass(bank, gate_w[(i, a)], FP4X4, d, a)
+                if i < 4:
+                    gates[(i, d)] = windows[i][:, S + 512 * d : S + 512 * (d + 1)]
+                else:
+                    gates[(i, d)] = placed("gate_%d_%d" % (i, d), 512, GATE_PLACE[i] + 2 * KIB * d)
+                nc.scalar.copy(out=gates[(i, d)], in_=bank[:])
+            for d in range(2):
+                bank = GATE_BANK + d if i == 0 else SUM_BANK + 2 * (i % 2) + d
+                a_banks[(i, d)] = bank_tile("a_bank_%d_%d" % (i, d), [P, 512], bank)
+                for a in range(2):
+                    first_stage_pass(a_banks[(i, d)], w1_q[(i, a)], FP8X4, d, a)
 
         def features(i):
-            window = windows[i]
+            if i >= 4:
+                windows[i] = weave.tile([P, S], F32, name="window_%d" % i, offset=WINDOW_PLACE[i], align_bytes=64)
             for d in range(2):
-                nc.vector.tensor_tensor(
-                    window[:, 512 * d : 512 * (d + 1)],
-                    a_banks[(i, d)][:],
-                    window[:, S + 512 * d : S + 512 * (d + 1)],
-                    MULT,
-                )
+                nc.vector.tensor_tensor(windows[i][:, 512 * d : 512 * (d + 1)], a_banks[(i, d)][:], gates[(i, d)], MULT)
 
-        pieces = {0: [(0, 4)], 1: [(0, 2), (2, 2)]}
-        z_turned = {
-            (b, j0): keep.tile([P, nj, 2, 2 * P], BF16, name="z_turned_%d_%d" % (b, j0), align_bytes=64)
-            for b in range(2)
-            for (j0, nj) in pieces[b]
-        }
+        z_turned = keep.tile([P, 4, 2, 2 * P], BF16, name="z_turned", align_bytes=64)
 
-        def turned_out(i, bank, bank_j0, j0, nj):
-            b, tau = divmod(i, 4)
-            nc.scalar.copy(
-                out=z_turned[(b, j0)][:, :, :, 64 * tau : 64 * (tau + 1)].rearrange("j b u (m e) -> j b u m e", e=2),
-                in_=bank[:, j0 - bank_j0 : j0 - bank_j0 + nj, :].rearrange("j b (m u e) -> j b u m e", u=2, e=2),
-            )
+        def pick_first(i, dst):
+            nc.vector.tensor_copy(dst, windows[i][:, 0:S].indirect(pos1_t[:]))
 
-        def pairs_whole(i):
-            window = windows[i]
-            first = ring2.tile([P, PAIRS], F32, name="first")
-            nc.vector.tensor_copy(first[:], window[:].indirect(pos1_t[:]))
-            second = ring2.tile([P, PAIRS], F32, name="second")
-            nc.vector.tensor_scalar(second[:], window[:].indirect(pos2_t[:]), -1.0, 0.0, MULT, ADD)
-            bank = psum.tile([P, 4, P], F32, name="zt_bank", tag="zt")
+        def pick_negated_second(i, dst):
+            nc.vector.tensor_scalar(dst, windows[i][:].indirect(pos2_t[:]), -1.0, 0.0, MULT, ADD)
+
+        def pick_tiles(tiles, firsts, seconds):
+            for i, dst in zip(tiles, firsts):
+                pick_first(i, dst)
+            for i, dst in zip(tiles, seconds):
+                pick_negated_second(i, dst)
+            return list(zip(firsts, seconds))
+
+        def turn(i, first, second):
+            bank = bank_tile("zt_bank_%d" % i, [P, 4, P], TURN_BANK + i % 2)
             for jb in range(4):
                 cols = slice(P * jb, P * (jb + 1))
                 nc.tensor.matmul(bank[:, jb, :], first[:, cols], ident[:], start=True, stop=False, is_transpose=True)
                 nc.tensor.matmul(bank[:, jb, :], second[:, cols], ident[:], start=False, stop=True, is_transpose=True)
-            for j0, nj in pieces[i // 4]:
-                turned_out(i, bank, 0, j0, nj)
-
-        def pairs_half(i, h):
-            window = windows[i]
-            cols16 = slice(16 * h, 16 * (h + 1))
-            second = keep.tile([P, 256], F32, name="second_half", tag="second_half")
-            nc.vector.tensor_copy(second[:], window[:].indirect(pos2_t[:, cols16]))
-            diff = ring2.tile([P, 256], F32, name="diff_half")
-            nc.vector.tensor_tensor(diff[:], window[:].indirect(pos1_t[:, cols16]), second[:], SUB)
-            bank = psum.tile([P, 2, P], F32, name="zt_bank_half", tag="zt")
-            for jb in range(2):
-                nc.tensor.transpose(bank[:, jb, :], diff[:, P * jb : P * (jb + 1)], ident[:])
-            turned_out(i, bank, 2 * h, 2 * h, 2)
+            nc.scalar.copy(
+                out=z_turned[:, :, :, 64 * i : 64 * (i + 1)].rearrange("j b u (m e) -> j b u m e", e=2),
+                in_=bank[:].rearrange("j b (m u e) -> j b u m e", u=2, e=2),
+            )
 
         z_q = {}
 
-        def quantise_z(b, j0, nj, copy):
-            words = z_turned[(b, j0)][:].bitcast(F32)
-            grouped = keep.tile([P, nj * P, 4], BF16, name="z_grouped_%d_%d" % (b, j0), align_bytes=64)
-            grouped_words = grouped[:].bitcast(F32)
-            for g in range(nj // 2):
-                bank = psum.tile([P, 2, 2, P], F32, name="back_bank", tag="zt")
+        def turn_z_back():
+            words = z_turned[:].bitcast(F32)
+            grouped = weave.tile([P, PAIRS, 4], BF16, name="z_grouped_0", offset=51 * KIB, align_bytes=64)[:]
+            grouped_words = grouped.bitcast(F32)
+            for g in range(2):
+                bank = bank_tile("back_bank_%d" % g, [P, 2, 2, P], TURN_BANK + g)
                 for jb in range(2):
                     for u in range(2):
                         nc.tensor.transpose(bank[:, jb, u, :], words[:, 2 * g + jb, u, :], ident[:])
-                copy(
+                nc.scalar.copy(
                     out=grouped_words[:, 256 * g : 256 * (g + 1), :].rearrange("p (b j) u -> p b j u", b=2),
                     in_=bank[:].rearrange("p b u j -> p b j u"),
                 )
-            codes = keep.tile([P, nj * P], U32, name="z_codes_%d_%d" % (b, j0), align_bytes=64)
-            scales = keep.tile([P, nj * P], U8, name="z_scales_%d_%d" % (b, j0), align_bytes=64)
-            nc.vector.quantize_mx(
-                out=codes[:].bitcast(FP8X4), scales=scales[:], in_=grouped[:].rearrange("p c t -> p (c t)")
+            return grouped
+
+        def quantise_z_natural(grouped):
+            place = GATE_PLACE[5] + 2 * KIB
+            codes, scales = quantise("z_0", grouped.rearrange("p c t -> p (c t)"), PAIRS, place)
+            for h in range(2):
+                cols = slice(HALF * h, HALF * (h + 1))
+                z_q[(0, h)] = (codes[:, cols], scales[:, cols])
+
+        Z_PLACE = [26 * KIB, 28 * KIB]
+        z_grouped = [
+            weave.tile([P, HALF, 4], BF16, name="z_grouped_1_%d" % h, offset=Z_PLACE[h], align_bytes=64)
+            for h in range(2)
+        ]
+
+        def pick_second(i, dst, cols16):
+            nc.vector.tensor_copy(dst, windows[i][:].indirect(pos2_t[:, cols16]))
+
+        def pick_difference(i, dst, second, cols16):
+            nc.vector.tensor_tensor(dst, windows[i][:].indirect(pos1_t[:, cols16]), second, SUB)
+
+        def round_planes(copy, h, u, planes):
+            copy(out=z_grouped[h][:, :, 2 * u : 2 * u + 2], in_=planes.rearrange("p t j -> p j t"))
+
+        def quantise_z_dealt(h):
+            codes, scales = quantise("z_1_%d" % h, z_grouped[h][:].rearrange("p c t -> p (c t)"), HALF)
+            z_q[(1, h)] = (codes[:], scales[:])
+
+        y_banks = {}
+
+        def second_stage_pass(h, nt, b):
+            if b == 0:
+                early = (GATE_BANK, GATE_BANK + 1, TURN_BANK + 1, TURN_BANK)
+                bank = early[nt] if h == 0 else SUM_BANK + nt
+                y_banks[(h, nt)] = bank_tile("y_bank_%d_%d" % (h, nt), [P, HALF], bank)
+            w_codes, w_scales = w2_q[b]
+            z_codes, z_scales = z_q[(b, h)]
+            nc.tensor.matmul_mx(
+                out=y_banks[(h, nt)][:],
+                lhsT=w_codes[:, P * nt : P * (nt + 1)].bitcast(FP8X4),
+                lhsT_scale=w_scales[:, P * nt : P * (nt + 1)],
+                rhs=z_codes.bitcast(FP8X4),
+                rhs_scale=z_scales,
+                start=(b == 0),
+                stop=(b == 1),
             )
-            for g in range(nj // 2):
-                cols = slice(256 * g, 256 * (g + 1))
-                z_q[(b, j0 // 2 + g)] = (codes[:, cols], scales[:, cols])
 
         out_view = out.rearrange("(t p) j -> p t j", p=P)
 
         def scores(h, group):
             for first in range(0, N // P, group):
-                result = keep.tile([P, group, 256], F32, name="result_%d_%d" % (h, first))
+                result = keep.tile([P, group, HALF], F32, name="result_%d_%d" % (h, first))
                 for k in range(group):
                     nt = first + k
-                    bank = psum.tile([P, 256], F32, name="y_bank", tag="a", bufs=4)
-                    for b in range(2):
-                        w_codes, w_scales = w2_q[b]
-                        z_codes, z_scales = z_q[(b, h)]
-                        nc.tensor.matmul_mx(
-                            out=bank[:],
-                            lhsT=w_codes[:, P * nt : P * (nt + 1)].bitcast(FP8X4),
-                            lhsT_scale=w_scales[:, P * nt : P * (nt + 1)],
-                            rhs=z_codes.bitcast(FP8X4),
-                            rhs_scale=z_scales,
-                            start=(b == 0),
-                            stop=(b == 1),
-                        )
-                    nc.scalar.activation(result[:, k, :], bank[:], SIGMOID, bias=c_t[:, nt : nt + 1])
+                    second_stage_pass(h, nt, 1)
+                    nc.scalar.activation(result[:, k, :], y_banks[(h, nt)][:], SIGMOID, bias=c_t[:, nt : nt + 1])
                 nc.sync.dma_start(
-                    out=out_view[:, first : first + group, 256 * h : 256 * (h + 1)], in_=result[:]
+                    out=out_view[:, first : first + group, HALF * h : HALF * (h + 1)], in_=result[:]
                 )
 
         nc.sync.dma_start(offs_t[:], offs)
         nc.sync.dma_start(pos1_t[:], pos1)
         nc.sync.dma_start(pos2_t[:], pos2)
         load_tab(0)
-        load_w1(0, 1, 22 * KIB)
-        tab.append(staged.tile([P, T], I32, name="tab1", offset=0, align_bytes=64))
+        tab.append(staged.tile([P, 40 * KIB // 4], I32, name="tab1", offset=0, align_bytes=64))
         load_tab(1)
-        wg = staged.tile([P, 2, 2 * H], U8, name="wg", offset=16 * KIB, align_bytes=64)
+        wg = staged.tile([P, 2, 2 * H], U8, name="wg", offset=40 * KIB, align_bytes=64)
         nc.sync.dma_start(out=wg[:].bitcast(I32), in_=wg_words.rearrange("a p n -> p a n").bitcast(I32))
+        load_w1(0, 1, 44 * KIB)
         gather_scales()
         gather_words(0, 1)
-        prep_w1(0)
-        load_w1(1, 1, 20 * KIB)
-        load_w1(2, 2, 24 * KIB)
+        load_w1(1, 1, 48 * KIB)
+        load_w1(2, 2, 52 * KIB)
         gather_words(1, 2)
         load_w1(4, 4, 0)
+        load_w2(16 * KIB)
+        c_t = staged.tile([P, N // P], F32, name="c_t", offset=32 * KIB, align_bytes=64)
+        with nc.allow_non_contiguous_dma(reason="one bias value for each partition"):
+            nc.sync.dma_start(out=c_t[:], in_=c.rearrange("(t p) -> p t", p=P))
+        deal_wg()
+        prep_w1_first()
         products(0)
         prep_w1(1)
         products(1)
         prep_w1(2)
-        for i in range(TILES):
-            features(i)
-            if i + 2 < TILES:
-                products(i + 2)
-            if i + 3 < TILES:
-                prep_w1(i + 3)
-            if i == 0:
-                load_w2(24 * KIB)
-            if i < SPLIT_FROM:
-                pairs_whole(i)
-            else:
-                pairs_half(i, 0)
-            if i == 3:
-                quantise_z(0, 0, 4, nc.scalar.copy)
-            if i in (4, 5):
-                prep_w2(i - 4)
-        c_t = staged.tile([P, N // P], F32, name="c_t", offset=0, align_bytes=64)
-        with nc.allow_non_contiguous_dma(reason="one bias value for each partition"):
-            nc.sync.dma_start(out=c_t[:], in_=c.rearrange("(t p) -> p t", p=P))
-        quantise_z(1, 0, 2, nc.scalar.copy)
-        for i in range(SPLIT_FROM, TILES):
-            pairs_half(i, 1)
-        quantise_z(1, 2, 2, nc.vector.tensor_copy)
-        scores(0, 2)
-        scores(1, 1)
+
+        features(0)
+        first_0 = keep.tile([P, PAIRS], F32, name="first_0")
+        picked = pick_tiles([0], [first_0[:]], [placed("second_0", PAIRS, w1_place(1))])
+        prep_w1(3)
+        products(2)
+        features(1)
+        products(3)
+        picked += pick_tiles([1], [placed("first_1", PAIRS, w1_place(2))], [placed("second_1", PAIRS, w1_place(3))])
+        for i in range(2):
+            turn(i, *picked[i])
+
+        features(2)
+        prep_w1(4)
+        products(4)
+        features(3)
+        prep_w1(5)
+        products(5)
+        prep_w1(6)
+        prep_w1(7)
+        second_3 = keep.tile([P, PAIRS], F32, name="second_3")
+        picked += pick_tiles(
+            [2, 3],
+            [windows[3][:, S : S + PAIRS], placed("first_3", PAIRS, w1_place(4))],
+            [placed("second_2", PAIRS, w1_place(5)), second_3[:]],
+        )
+        for i in range(2, 4):
+            turn(i, *picked[i])
+        z_back = turn_z_back()
+        w2_q[0] = quantise("w2_0", round_w2(0), N)
+
+        features(4)
+        products(6)
+        features(5)
+        products(7)
+        quantise_z_natural(z_back)
+        w2_q[1] = quantise("w2_1", round_w2(1), N)
+        whole = slice(0, PAIRS // 16)
+        seconds = [placed("second_4", PAIRS, GATE_PLACE[5]), placed("second_5", PAIRS, W2_PLACE[0])]
+        for t in range(2):
+            pick_second(4 + t, seconds[t], whole)
+        planes = keep.tile([P, 2, PAIRS], F32, name="planes_low")
+        for t in range(2):
+            pick_difference(4 + t, planes[:, t, :], seconds[t], whole)
+        for h in range(2):
+            round_planes(nc.scalar.copy, h, 0, planes[:, :, HALF * h : HALF * (h + 1)])
+
+        features(6)
+        features(7)
+        for h in range(2):
+            for nt in range(N // P):
+                second_stage_pass(h, nt, 0)
+        for h in range(2):
+            cols16 = slice(16 * h, 16 * (h + 1))
+            seconds = [placed("second_%d_%d" % (6 + t, h), HALF, GATE_PLACE[7] + KIB * t) for t in range(2)]
+            planes = keep.tile([P, 2, HALF], F32, name="planes_high_%d" % h)
+            for t in range(2):
+                pick_second(6 + t, seconds[t], cols16)
+            for t in range(2):
+                pick_difference(6 + t, planes[:, t, :], seconds[t], cols16)
+            round_planes(nc.vector.tensor_copy, h, 1, planes[:])
+            quantise_z_dealt(h)
+            scores(h, 2 - h)

@@ -21,7 +21,7 @@ SIGMOID = mybir.ActivationFunctionType.Sigmoid
 
 P = 128
 KIB = 1024
-HALF = PAIRS // 2
+PIECES = [(0, 256), (256, 128), (384, 128)]
 
 
 def tile_list_pairwise_document_ranking_kernel(
@@ -44,33 +44,26 @@ def tile_list_pairwise_document_ranking_kernel(
         offs_t = keep.tile([P, S // 16], U16, name="offs_t")
         pos1_t = keep.tile([P, PAIRS // 16], U16, name="pos1_t")
         pos2_t = keep.tile([P, PAIRS // 16], U16, name="pos2_t")
-        tab_sc = keep.tile([P, T], U8, name="tab_sc", tag="slot_e", align_bytes=64)
+        tab_sc = staged.tile([P, T + 2 * H], U8, name="tab_sc", offset=64 * KIB, align_bytes=64)
         v_sc = [keep.tile([P, S], U8, name="v_sc%d" % a, align_bytes=64) for a in range(2)]
         ident = keep.tile([P, P], F32, name="ident")
-        wg_sc = keep.tile([P, 2, H], U8, name="wg_sc", align_bytes=64)
         zeros = staged.tile([P, 48 * KIB // 4], I32, name="zeros", offset=0, align_bytes=64)
         tab = [staged.tile([P, T], I32, name="tab0", offset=48 * KIB, align_bytes=64)]
         make_identity(nc, ident[:])
-        nc.vector.memset(tab_sc[:].bitcast(I32), 0)
-        nc.vector.memset(wg_sc[:].bitcast(I32), 0)
+        nc.vector.memset(tab_sc[:, 0:T].bitcast(I32), 0)
         nc.vector.memset(zeros[:, 0 : S // 4], 0)
         nc.vector.tensor_copy(v_sc[1][:].bitcast(I32), zeros[:, 0 : S // 4])
         scale_rows = tab_scales.bitcast(I32).rearrange("a (q r) t -> r q a t", r=4)
         for r in range(4):
-            nc.scalar.dma_start(out=tab_sc[r:P:16, :].bitcast(I32), in_=scale_rows[r])
-        for q in range(4):
-            nc.gpsimd.dma_start(
-                out=wg_sc[32 * q : 32 * q + 4, :, :].bitcast(I32),
-                in_=wg_scales[:, 4 * q : 4 * q + 4, :].rearrange("a r t -> r a t").bitcast(I32),
-            )
+            nc.scalar.dma_start(out=tab_sc[r:P:16, 0:T].bitcast(I32), in_=scale_rows[r])
 
         def load_tab(a):
             nc.sync.dma_start(out=tab[a][:, 0:T], in_=tab_words[a].rearrange("p t i -> p (t i)").bitcast(I32))
 
         w1_raw = {}
 
-        def load_w1(first, count, offset):
-            for a in range(2):
+        def load_w1(first, count, offset, passes=(0, 1)):
+            for a in passes:
                 raw = staged.tile(
                     [P, 4, count * P], F32, name="w1_raw_%d_%d" % (first, a),
                     offset=offset + a * count * 2 * KIB, align_bytes=64,
@@ -86,7 +79,7 @@ def tile_list_pairwise_document_ranking_kernel(
                         cols = raw[:, :, (i - first) * P : (i - first + 1) * P]
                         w1_raw[(i, a)] = cols.rearrange("p j (g i) -> p g j i", i=4)
                     else:
-                        w1_raw[(i, a)] = raw[:].rearrange("p j (q t e) -> p t q j e", t=4, e=8)[:, i - 4]
+                        w1_raw[(i, a)] = raw[:].rearrange("p j (q t h i) -> p t q h j i", t=4, h=2, i=4)[:, i - 4]
 
         w2_raw = []
 
@@ -102,15 +95,16 @@ def tile_list_pairwise_document_ranking_kernel(
         v_words = {}
 
         def gather_scales():
-            nc.vector.tensor_copy(v_sc[0][:], tab_sc[:].indirect(offs_t[:]))
+            nc.vector.tensor_copy(v_sc[0][:], tab_sc[:, 0:T].indirect(offs_t[:]))
             nc.scalar.dma_start(out=v_sc[1][0:112, :].bitcast(I32), in_=v_sc[0][16:128, :].bitcast(I32))
 
         def gather_words(a, halves):
             width = S // halves
             for h in range(halves):
-                words = keep.tile(
-                    [P, width], U32, name="v_words_%d_%d" % (a, h), tag="slot_e" if a == 0 else "", align_bytes=64
-                )
+                if a == 0:
+                    words = staged.tile([P, width], U32, name="v_words_0", offset=64 * KIB, align_bytes=64)
+                else:
+                    words = keep.tile([P, width], U32, name="v_words_1_%d" % h, align_bytes=64)
                 nc.vector.tensor_copy(
                     words[:],
                     tab[a][:, 0:T].bitcast(U32).indirect(offs_t[:, h * width // 16 : (h + 1) * width // 16]),
@@ -133,7 +127,7 @@ def tile_list_pairwise_document_ranking_kernel(
             if i < 4:
                 view = dst.rearrange("p (g i) j -> p g j i", i=4)
             else:
-                view = dst.rearrange("p (q e) j -> p q j e", e=8)
+                view = dst.rearrange("p (q h i) j -> p q h j i", h=2, i=4)
             copy(out=view, in_=w1_raw[(i, a)])
 
         def prep_w1_first():
@@ -152,7 +146,7 @@ def tile_list_pairwise_document_ranking_kernel(
         def w1_place(i):
             return 2 * KIB * i if i < 4 else WINDOW_PLACE[1] + 2 * KIB * (i - 4)
 
-        W2_PLACE = [47 * KIB, 32 * KIB]
+        W2_PLACE = [47 * KIB, 30 * KIB]
 
         def pool_round(out, in_):
             nc.gpsimd.tensor_scalar(out, in_, 1.0, 0.0, MULT, ADD)
@@ -165,7 +159,7 @@ def tile_list_pairwise_document_ranking_kernel(
                 if a == 0 and i in (4, 5):
                     pool_round(
                         grouped[:, a, :, :].rearrange("p (q e) j -> p q e j", e=8),
-                        w1_raw[(i, a)].rearrange("p q j e -> p q e j"),
+                        w1_raw[(i, a)].rearrange("p q h j i -> p q (h i) j"),
                     )
                 else:
                     round_w1(nc.scalar.copy, grouped[:, a, :, :], i, a)
@@ -293,14 +287,12 @@ def tile_list_pairwise_document_ranking_kernel(
         def quantise_z_natural(grouped):
             place = GATE_PLACE[5] + 2 * KIB
             codes, scales = quantise("z_0", grouped.rearrange("p c t -> p (c t)"), PAIRS, place)
-            for h in range(2):
-                cols = slice(HALF * h, HALF * (h + 1))
-                z_q[(0, h)] = (codes[:, cols], scales[:, cols])
+            for h, (j0, width) in enumerate(PIECES):
+                z_q[(0, h)] = (codes[:, j0 : j0 + width], scales[:, j0 : j0 + width])
 
-        Z_PLACE = [26 * KIB, 28 * KIB]
         z_grouped = [
-            weave.tile([P, HALF, 4], BF16, name="z_grouped_1_%d" % h, offset=Z_PLACE[h], align_bytes=64)
-            for h in range(2)
+            keep.tile([P, width, 4], BF16, name="z_grouped_1_%d" % h, align_bytes=64)
+            for h, (j0, width) in enumerate(PIECES)
         ]
 
         def pick_second(i, dst, cols16):
@@ -313,7 +305,7 @@ def tile_list_pairwise_document_ranking_kernel(
             copy(out=z_grouped[h][:, :, 2 * u : 2 * u + 2], in_=planes.rearrange("p t j -> p j t"))
 
         def quantise_z_dealt(h):
-            codes, scales = quantise("z_1_%d" % h, z_grouped[h][:].rearrange("p c t -> p (c t)"), HALF)
+            codes, scales = quantise("z_1_%d" % h, z_grouped[h][:].rearrange("p c t -> p (c t)"), PIECES[h][1])
             z_q[(1, h)] = (codes[:], scales[:])
 
         y_banks = {}
@@ -321,8 +313,8 @@ def tile_list_pairwise_document_ranking_kernel(
         def second_stage_pass(h, nt, b):
             if b == 0:
                 early = (GATE_BANK, GATE_BANK + 1, TURN_BANK + 1, TURN_BANK)
-                bank = early[nt] if h == 0 else SUM_BANK + nt
-                y_banks[(h, nt)] = bank_tile("y_bank_%d_%d" % (h, nt), [P, HALF], bank)
+                bank = SUM_BANK + nt if h == 1 else early[nt]
+                y_banks[(h, nt)] = bank_tile("y_bank_%d_%d" % (h, nt), [P, PIECES[h][1]], bank)
             w_codes, w_scales = w2_q[b]
             z_codes, z_scales = z_q[(b, h)]
             nc.tensor.matmul_mx(
@@ -338,14 +330,15 @@ def tile_list_pairwise_document_ranking_kernel(
         out_view = out.rearrange("(t p) j -> p t j", p=P)
 
         def scores(h, group):
+            j0, width = PIECES[h]
             for first in range(0, N // P, group):
-                result = keep.tile([P, group, HALF], F32, name="result_%d_%d" % (h, first))
+                result = keep.tile([P, group, width], F32, name="result_%d_%d" % (h, first))
                 for k in range(group):
                     nt = first + k
                     second_stage_pass(h, nt, 1)
                     nc.scalar.activation(result[:, k, :], y_banks[(h, nt)][:], SIGMOID, bias=c_t[:, nt : nt + 1])
                 nc.sync.dma_start(
-                    out=out_view[:, first : first + group, HALF * h : HALF * (h + 1)], in_=result[:]
+                    out=out_view[:, first : first + group, j0 : j0 + width], in_=result[:]
                 )
 
         nc.sync.dma_start(offs_t[:], offs)
@@ -356,9 +349,17 @@ def tile_list_pairwise_document_ranking_kernel(
         load_tab(1)
         wg = staged.tile([P, 2, 2 * H], U8, name="wg", offset=40 * KIB, align_bytes=64)
         nc.sync.dma_start(out=wg[:].bitcast(I32), in_=wg_words.rearrange("a p n -> p a n").bitcast(I32))
-        load_w1(0, 1, 44 * KIB)
+        load_w1(0, 1, 44 * KIB, (0,))
         gather_scales()
+        wg_sc = staged.tile([P, 2, H], U8, name="wg_sc", offset=68 * KIB, align_bytes=64)
+        nc.vector.memset(wg_sc[:].bitcast(I32), 0)
+        for q in range(4):
+            nc.scalar.dma_start(
+                out=wg_sc[32 * q : 32 * q + 4, :, :].bitcast(I32),
+                in_=wg_scales[:, 4 * q : 4 * q + 4, :].rearrange("a r t -> r a t").bitcast(I32),
+            )
         gather_words(0, 1)
+        load_w1(0, 1, 58 * KIB, (1,))
         load_w1(1, 1, 48 * KIB)
         load_w1(2, 2, 52 * KIB)
         gather_words(1, 2)
@@ -411,28 +412,34 @@ def tile_list_pairwise_document_ranking_kernel(
         quantise_z_natural(z_back)
         w2_q[1] = quantise("w2_1", round_w2(1), N)
         whole = slice(0, PAIRS // 16)
-        seconds = [placed("second_4", PAIRS, GATE_PLACE[5]), placed("second_5", PAIRS, W2_PLACE[0])]
+        firsts = [placed("first_4", PAIRS, GATE_PLACE[5]), placed("first_5", PAIRS, W2_PLACE[0])]
+        seconds = [placed("second_4", PAIRS, 51 * KIB), placed("second_5", PAIRS, W2_PLACE[1])]
+        for t in range(2):
+            pick_first(4 + t, firsts[t])
         for t in range(2):
             pick_second(4 + t, seconds[t], whole)
         planes = keep.tile([P, 2, PAIRS], F32, name="planes_low")
         for t in range(2):
-            pick_difference(4 + t, planes[:, t, :], seconds[t], whole)
-        for h in range(2):
-            round_planes(nc.scalar.copy, h, 0, planes[:, :, HALF * h : HALF * (h + 1)])
+            nc.gpsimd.tensor_tensor(planes[:, t, :], firsts[t], seconds[t], SUB)
+        for h, (j0, width) in enumerate(PIECES):
+            round_planes(nc.scalar.copy, h, 0, planes[:, :, j0 : j0 + width])
 
         features(6)
         features(7)
         for h in range(2):
             for nt in range(N // P):
                 second_stage_pass(h, nt, 0)
-        for h in range(2):
-            cols16 = slice(16 * h, 16 * (h + 1))
-            seconds = [placed("second_%d_%d" % (6 + t, h), HALF, GATE_PLACE[7] + KIB * t) for t in range(2)]
-            planes = keep.tile([P, 2, HALF], F32, name="planes_high_%d" % h)
+        for h, (j0, width) in enumerate(PIECES):
+            cols16 = slice(j0 // 16, (j0 + width) // 16)
+            seconds = [placed("second_%d_%d" % (6 + t, h), width, GATE_PLACE[7] + KIB * t) for t in range(2)]
+            planes = keep.tile([P, 2, width], F32, name="planes_high_%d" % h)
             for t in range(2):
                 pick_second(6 + t, seconds[t], cols16)
             for t in range(2):
                 pick_difference(6 + t, planes[:, t, :], seconds[t], cols16)
             round_planes(nc.vector.tensor_copy, h, 1, planes[:])
             quantise_z_dealt(h)
-            scores(h, 2 - h)
+            if h == 2:
+                for nt in range(N // P):
+                    second_stage_pass(h, nt, 0)
+            scores(h, 1 if h == 2 else 2)

@@ -44,26 +44,33 @@ def tile_list_pairwise_document_ranking_kernel(
         offs_t = keep.tile([P, S // 16], U16, name="offs_t")
         pos1_t = keep.tile([P, PAIRS // 16], U16, name="pos1_t")
         pos2_t = keep.tile([P, PAIRS // 16], U16, name="pos2_t")
-        tab_sc = staged.tile([P, T + 2 * H], U8, name="tab_sc", offset=64 * KIB, align_bytes=64)
+        tab_sc = staged.tile([P, T], U8, name="tab_sc", offset=64 * KIB, align_bytes=64)
         v_sc = [keep.tile([P, S], U8, name="v_sc%d" % a, align_bytes=64) for a in range(2)]
         ident = keep.tile([P, P], F32, name="ident")
         zeros = staged.tile([P, 48 * KIB // 4], I32, name="zeros", offset=0, align_bytes=64)
         tab = [staged.tile([P, T], I32, name="tab0", offset=48 * KIB, align_bytes=64)]
         make_identity(nc, ident[:])
         nc.vector.memset(tab_sc[:, 0:T].bitcast(I32), 0)
+        wg_sc = keep.tile([P, 2, H], U8, name="wg_sc", align_bytes=64)
+        nc.vector.memset(wg_sc[:].bitcast(I32), 0)
         nc.vector.memset(zeros[:, 0 : S // 4], 0)
         nc.vector.tensor_copy(v_sc[1][:].bitcast(I32), zeros[:, 0 : S // 4])
         scale_rows = tab_scales.bitcast(I32).rearrange("a (q r) t -> r q a t", r=4)
         for r in range(4):
             nc.scalar.dma_start(out=tab_sc[r:P:16, 0:T].bitcast(I32), in_=scale_rows[r])
+        for q, queue in enumerate((nc.gpsimd, nc.gpsimd, nc.scalar, nc.scalar)):
+            queue.dma_start(
+                out=wg_sc[32 * q : 32 * q + 4, :, :].bitcast(I32),
+                in_=wg_scales[:, 4 * q : 4 * q + 4, :].rearrange("a r t -> r a t").bitcast(I32),
+            )
 
         def load_tab(a):
             nc.sync.dma_start(out=tab[a][:, 0:T], in_=tab_words[a].rearrange("p t i -> p (t i)").bitcast(I32))
 
         w1_raw = {}
 
-        def load_w1(first, count, offset, passes=(0, 1)):
-            for a in passes:
+        def load_w1(first, count, offset):
+            for a in range(2):
                 raw = staged.tile(
                     [P, 4, count * P], F32, name="w1_raw_%d_%d" % (first, a),
                     offset=offset + a * count * 2 * KIB, align_bytes=64,
@@ -135,7 +142,7 @@ def tile_list_pairwise_document_ranking_kernel(
             late = staged.tile([P, P, 4], BF16, name="w1_grouped_0_1", offset=36 * KIB, align_bytes=64)
             for a, grouped, copy in ((0, early, nc.scalar.copy), (1, late, nc.vector.tensor_copy)):
                 round_w1(copy, grouped[:], 0, a)
-                pool, place = ((staged, 37 * KIB), (weave, w1_place(1)))[a]
+                pool, place = ((staged, 38 * KIB), (weave, w1_place(1)))[a]
                 codes = pool.tile([P, P], U32, name="codes_w1_0_%d" % a, offset=place, align_bytes=64)
                 scales = keep.tile([P, P], U8, name="scales_w1_0_%d" % a, align_bytes=64)
                 nc.vector.quantize_mx(
@@ -183,19 +190,20 @@ def tile_list_pairwise_document_ranking_kernel(
         gate_w = {}
 
         def deal_wg():
-            words = staged.tile([P, 2, 4, 2 * P], U8, name="wg_dealt", offset=33 * KIB, align_bytes=64)
+            words = staged.tile([P, 2, 4, 2 * P], U8, name="wg_dealt", offset=34 * KIB + 512, align_bytes=64)
             nc.vector.tensor_copy(
                 words[:].bitcast(I32).rearrange("p a t (q w) -> p a t q w", w=4),
-                wg[:, :, H : 2 * H].bitcast(I32).rearrange("p a (q t w) -> p a t q w", t=4, w=4),
+                wg_rest[:, :, H - 2 * P : 2 * (H - P)].bitcast(I32).rearrange("p a (q t w) -> p a t q w", t=4, w=4),
             )
-            scales = staged.tile([P, 2, 4, P], U8, name="wg_sc_dealt", offset=35 * KIB, align_bytes=64)
+            scales = staged.tile([P, 2, 4, P], U8, name="wg_sc_dealt", offset=36 * KIB + 512, align_bytes=64)
             nc.vector.tensor_copy(
                 scales[:].bitcast(I32).rearrange("p a t (q w) -> p a t q w", w=2),
                 wg_sc[:, :, 512:H].bitcast(I32).rearrange("p a (q t w) -> p a t q w", t=4, w=2),
             )
             for a in range(2):
                 for t in range(4):
-                    gate_w[(t, a)] = (wg[:, a, 2 * P * t : 2 * P * (t + 1)], wg_sc[:, a, P * t : P * (t + 1)])
+                    natural = wg_first[:, a, :] if t == 0 else wg_rest[:, a, 2 * P * (t - 1) : 2 * P * t]
+                    gate_w[(t, a)] = (natural, wg_sc[:, a, P * t : P * (t + 1)])
                     gate_w[(4 + t, a)] = (words[:, a, t, :], scales[:, a, t, :])
 
         windows = {}
@@ -347,19 +355,14 @@ def tile_list_pairwise_document_ranking_kernel(
         load_tab(0)
         tab.append(staged.tile([P, 40 * KIB // 4], I32, name="tab1", offset=0, align_bytes=64))
         load_tab(1)
-        wg = staged.tile([P, 2, 2 * H], U8, name="wg", offset=40 * KIB, align_bytes=64)
-        nc.sync.dma_start(out=wg[:].bitcast(I32), in_=wg_words.rearrange("a p n -> p a n").bitcast(I32))
-        load_w1(0, 1, 44 * KIB, (0,))
+        wg_rows = wg_words.bitcast(I32).rearrange("a p n -> p a n")
+        wg_first = staged.tile([P, 2, 2 * P], U8, name="wg_first", offset=40 * KIB, align_bytes=64)
+        nc.sync.dma_start(out=wg_first[:].bitcast(I32), in_=wg_rows[:, :, 0 : P // 2])
+        load_w1(0, 1, 44 * KIB)
         gather_scales()
-        wg_sc = staged.tile([P, 2, H], U8, name="wg_sc", offset=68 * KIB, align_bytes=64)
-        nc.vector.memset(wg_sc[:].bitcast(I32), 0)
-        for q in range(4):
-            nc.scalar.dma_start(
-                out=wg_sc[32 * q : 32 * q + 4, :, :].bitcast(I32),
-                in_=wg_scales[:, 4 * q : 4 * q + 4, :].rearrange("a r t -> r a t").bitcast(I32),
-            )
         gather_words(0, 1)
-        load_w1(0, 1, 58 * KIB, (1,))
+        wg_rest = staged.tile([P, 2, 2 * (H - P)], U8, name="wg_rest", offset=60 * KIB, align_bytes=64)
+        nc.sync.dma_start(out=wg_rest[:].bitcast(I32), in_=wg_rows[:, :, P // 2 : H // 2])
         load_w1(1, 1, 48 * KIB)
         load_w1(2, 2, 52 * KIB)
         gather_words(1, 2)
@@ -368,8 +371,8 @@ def tile_list_pairwise_document_ranking_kernel(
         c_t = staged.tile([P, N // P], F32, name="c_t", offset=32 * KIB, align_bytes=64)
         with nc.allow_non_contiguous_dma(reason="one bias value for each partition"):
             nc.sync.dma_start(out=c_t[:], in_=c.rearrange("(t p) -> p t", p=P))
-        deal_wg()
         prep_w1_first()
+        deal_wg()
         products(0)
         prep_w1(1)
         products(1)

@@ -21,6 +21,7 @@ SIGMOID = mybir.ActivationFunctionType.Sigmoid
 
 P = 128
 KIB = 1024
+SHARED = 256
 PIECES = [(0, 256), (256, 128), (384, 128)]
 
 
@@ -38,7 +39,7 @@ def tile_list_pairwise_document_ranking_kernel(
             return psum.tile(shape, F32, name=name, offset=2 * KIB * bank)
 
         GATE_BANK, SUM_BANK, TURN_BANK = 0, 2, 6
-        WINDOW_PLACE = [32 * KIB, 40 * KIB, 56 * KIB, 48 * KIB, 43 * KIB, 60 * KIB, 32 * KIB, 64 * KIB]
+        WINDOW_PLACE = [32 * KIB, 40 * KIB, 56 * KIB, 48 * KIB, 43 * KIB, 60 * KIB, 43 * KIB, 60 * KIB]
         GATE_PLACE = {4: 32 * KIB, 5: 36 * KIB, 6: 72 * KIB, 7: 68 * KIB}
 
         offs_t = keep.tile([P, S // 16], U16, name="offs_t")
@@ -58,8 +59,8 @@ def tile_list_pairwise_document_ranking_kernel(
         scale_rows = tab_scales.bitcast(I32).rearrange("a (q r) t -> r q a t", r=4)
         for r in range(4):
             nc.scalar.dma_start(out=tab_sc[r:P:16, 0:T].bitcast(I32), in_=scale_rows[r])
-        for q, queue in enumerate((nc.gpsimd, nc.gpsimd, nc.scalar, nc.scalar)):
-            queue.dma_start(
+        for q in range(4):
+            nc.gpsimd.dma_start(
                 out=wg_sc[32 * q : 32 * q + 4, :, :].bitcast(I32),
                 in_=wg_scales[:, 4 * q : 4 * q + 4, :].rearrange("a r t -> r a t").bitcast(I32),
             )
@@ -84,9 +85,9 @@ def tile_list_pairwise_document_ranking_kernel(
                 for i in range(first, first + count):
                     if i < 4:
                         cols = raw[:, :, (i - first) * P : (i - first + 1) * P]
-                        w1_raw[(i, a)] = cols.rearrange("p j (g i) -> p g j i", i=4)
+                        w1_raw[(i, a)] = cols.rearrange("p j (g i) -> p g j i", i=2)
                     else:
-                        w1_raw[(i, a)] = raw[:].rearrange("p j (q t h i) -> p t q h j i", t=4, h=2, i=4)[:, i - 4]
+                        w1_raw[(i, a)] = raw[:].rearrange("p j (q t h i) -> p t q h j i", t=4, h=4, i=2)[:, i - 4]
 
         w2_raw = []
 
@@ -132,9 +133,9 @@ def tile_list_pairwise_document_ranking_kernel(
 
         def round_w1(copy, dst, i, a):
             if i < 4:
-                view = dst.rearrange("p (g i) j -> p g j i", i=4)
+                view = dst.rearrange("p (g i) j -> p g j i", i=2)
             else:
-                view = dst.rearrange("p (q h i) j -> p q h j i", h=2, i=4)
+                view = dst.rearrange("p (q h i) j -> p q h j i", h=4, i=2)
             copy(out=view, in_=w1_raw[(i, a)])
 
         def prep_w1_first():
@@ -153,7 +154,7 @@ def tile_list_pairwise_document_ranking_kernel(
         def w1_place(i):
             return 2 * KIB * i if i < 4 else WINDOW_PLACE[1] + 2 * KIB * (i - 4)
 
-        W2_PLACE = [47 * KIB, 30 * KIB]
+        W2_PLACE = [47 * KIB, 32 * KIB]
 
         def pool_round(out, in_):
             nc.gpsimd.tensor_scalar(out, in_, 1.0, 0.0, MULT, ADD)
@@ -182,8 +183,8 @@ def tile_list_pairwise_document_ranking_kernel(
                 pool_round(grouped[:, 0:384, :], w2_raw[b][:, :, 0:384].rearrange("p j c -> p c j"))
             for cols in ([slice(384, N)], [slice(0, 256), slice(256, N)])[b]:
                 nc.scalar.copy(
-                    out=grouped[:, cols, :].rearrange("p (g i) j -> p g j i", i=4),
-                    in_=w2_raw[b][:, :, cols].rearrange("p j (g i) -> p g j i", i=4),
+                    out=grouped[:, cols, :].rearrange("p (g i) j -> p g j i", i=2),
+                    in_=w2_raw[b][:, :, cols].rearrange("p j (g i) -> p g j i", i=2),
                 )
             return grouped[:].rearrange("p c j -> p (c j)")
 
@@ -193,7 +194,7 @@ def tile_list_pairwise_document_ranking_kernel(
             words = staged.tile([P, 2, 4, 2 * P], U8, name="wg_dealt", offset=34 * KIB + 512, align_bytes=64)
             nc.vector.tensor_copy(
                 words[:].bitcast(I32).rearrange("p a t (q w) -> p a t q w", w=4),
-                wg_rest[:, :, H - 2 * P : 2 * (H - P)].bitcast(I32).rearrange("p a (q t w) -> p a t q w", t=4, w=4),
+                wg[:, :, H : 2 * H].bitcast(I32).rearrange("p a (q t w) -> p a t q w", t=4, w=4),
             )
             scales = staged.tile([P, 2, 4, P], U8, name="wg_sc_dealt", offset=36 * KIB + 512, align_bytes=64)
             nc.vector.tensor_copy(
@@ -202,13 +203,13 @@ def tile_list_pairwise_document_ranking_kernel(
             )
             for a in range(2):
                 for t in range(4):
-                    natural = wg_first[:, a, :] if t == 0 else wg_rest[:, a, 2 * P * (t - 1) : 2 * P * t]
-                    gate_w[(t, a)] = (natural, wg_sc[:, a, P * t : P * (t + 1)])
+                    gate_w[(t, a)] = (wg[:, a, 2 * P * t : 2 * P * (t + 1)], wg_sc[:, a, P * t : P * (t + 1)])
                     gate_w[(4 + t, a)] = (words[:, a, t, :], scales[:, a, t, :])
 
         windows = {}
         a_banks = {}
         gates = {}
+        shared_sums = {}
 
         def placed(name, width, offset):
             return weave.tile([P, width], F32, name=name, offset=offset, align_bytes=64)[:]
@@ -242,12 +243,20 @@ def tile_list_pairwise_document_ranking_kernel(
                 a_banks[(i, d)] = bank_tile("a_bank_%d_%d" % (i, d), [P, 512], bank)
                 for a in range(2):
                     first_stage_pass(a_banks[(i, d)], w1_q[(i, a)], FP8X4, d, a)
+            if i >= 6:
+                shared_sums[i] = keep.tile([P, SHARED], F32, name="shared_sums_%d" % i)[:]
+                nc.scalar.copy(out=shared_sums[i], in_=a_banks[(i, 1)][:, 512 - SHARED : 512])
 
         def features(i):
             if i >= 4:
                 windows[i] = weave.tile([P, S], F32, name="window_%d" % i, offset=WINDOW_PLACE[i], align_bytes=64)
-            for d in range(2):
-                nc.vector.tensor_tensor(windows[i][:, 512 * d : 512 * (d + 1)], a_banks[(i, d)][:], gates[(i, d)], MULT)
+            own = 512 - SHARED if i >= 6 else 512
+            nc.vector.tensor_tensor(windows[i][:, 0:512], a_banks[(i, 0)][:], gates[(i, 0)], MULT)
+            nc.vector.tensor_tensor(
+                windows[i][:, 512 : 512 + own], a_banks[(i, 1)][:, 0:own], gates[(i, 1)][:, 0:own], MULT
+            )
+            if i >= 6:
+                nc.gpsimd.tensor_tensor(windows[i][:, 512 + own : S], shared_sums[i], gates[(i, 1)][:, own:512], MULT)
 
         z_turned = keep.tile([P, 4, 2, 2 * P], BF16, name="z_turned", align_bytes=64)
 
@@ -279,7 +288,7 @@ def tile_list_pairwise_document_ranking_kernel(
 
         def turn_z_back():
             words = z_turned[:].bitcast(F32)
-            grouped = weave.tile([P, PAIRS, 4], BF16, name="z_grouped_0", offset=51 * KIB, align_bytes=64)[:]
+            grouped = weave.tile([P, PAIRS, 4], BF16, name="z_grouped_0", offset=28 * KIB, align_bytes=64)[:]
             grouped_words = grouped.bitcast(F32)
             for g in range(2):
                 bank = bank_tile("back_bank_%d" % g, [P, 2, 2, P], TURN_BANK + g)
@@ -355,14 +364,11 @@ def tile_list_pairwise_document_ranking_kernel(
         load_tab(0)
         tab.append(staged.tile([P, 40 * KIB // 4], I32, name="tab1", offset=0, align_bytes=64))
         load_tab(1)
-        wg_rows = wg_words.bitcast(I32).rearrange("a p n -> p a n")
-        wg_first = staged.tile([P, 2, 2 * P], U8, name="wg_first", offset=40 * KIB, align_bytes=64)
-        nc.sync.dma_start(out=wg_first[:].bitcast(I32), in_=wg_rows[:, :, 0 : P // 2])
+        wg = staged.tile([P, 2, 2 * H], U8, name="wg", offset=40 * KIB, align_bytes=64)
+        nc.sync.dma_start(out=wg[:].bitcast(I32), in_=wg_words.rearrange("a p n -> p a n").bitcast(I32))
         load_w1(0, 1, 44 * KIB)
         gather_scales()
         gather_words(0, 1)
-        wg_rest = staged.tile([P, 2, 2 * (H - P)], U8, name="wg_rest", offset=60 * KIB, align_bytes=64)
-        nc.sync.dma_start(out=wg_rest[:].bitcast(I32), in_=wg_rows[:, :, P // 2 : H // 2])
         load_w1(1, 1, 48 * KIB)
         load_w1(2, 2, 52 * KIB)
         gather_words(1, 2)
@@ -413,22 +419,20 @@ def tile_list_pairwise_document_ranking_kernel(
         features(5)
         products(7)
         quantise_z_natural(z_back)
-        w2_q[1] = quantise("w2_1", round_w2(1), N)
+        w2_rounded = round_w2(1)
         whole = slice(0, PAIRS // 16)
-        firsts = [placed("first_4", PAIRS, GATE_PLACE[5]), placed("first_5", PAIRS, W2_PLACE[0])]
-        seconds = [placed("second_4", PAIRS, 51 * KIB), placed("second_5", PAIRS, W2_PLACE[1])]
-        for t in range(2):
-            pick_first(4 + t, firsts[t])
+        seconds = [placed("second_4", PAIRS, GATE_PLACE[5]), placed("second_5", PAIRS, W2_PLACE[0])]
         for t in range(2):
             pick_second(4 + t, seconds[t], whole)
-        planes = keep.tile([P, 2, PAIRS], F32, name="planes_low")
+        planes = weave.tile([P, 2, PAIRS], F32, name="planes_low", offset=28 * KIB, align_bytes=64)
         for t in range(2):
-            nc.gpsimd.tensor_tensor(planes[:, t, :], firsts[t], seconds[t], SUB)
+            pick_difference(4 + t, planes[:, t, :], seconds[t], whole)
         for h, (j0, width) in enumerate(PIECES):
             round_planes(nc.scalar.copy, h, 0, planes[:, :, j0 : j0 + width])
 
         features(6)
         features(7)
+        w2_q[1] = quantise("w2_1", w2_rounded, N, GATE_PLACE[7] + 2 * KIB)
         for h in range(2):
             for nt in range(N // P):
                 second_stage_pass(h, nt, 0)

@@ -21,7 +21,7 @@ SIGMOID = mybir.ActivationFunctionType.Sigmoid
 
 P = 128
 KIB = 1024
-SHARED = 256
+SHARED = 320
 PIECES = [(0, 256), (256, 128), (384, 128)]
 
 
@@ -38,7 +38,7 @@ def tile_list_pairwise_document_ranking_kernel(
         def bank_tile(name, shape, bank):
             return psum.tile(shape, F32, name=name, offset=2 * KIB * bank)
 
-        GATE_BANK, SUM_BANK, TURN_BANK = 0, 2, 6
+        GATE_BANK, SUM_BANK, TURN_BANK = 6, 2, 0
         WINDOW_PLACE = [32 * KIB, 40 * KIB, 56 * KIB, 48 * KIB, 43 * KIB, 60 * KIB, 43 * KIB, 60 * KIB]
         GATE_PLACE = {4: 32 * KIB, 5: 36 * KIB, 6: 72 * KIB, 7: 68 * KIB}
 
@@ -160,7 +160,7 @@ def tile_list_pairwise_document_ranking_kernel(
             nc.gpsimd.tensor_scalar(out, in_, 1.0, 0.0, MULT, ADD)
 
         def prep_w1(i):
-            reach = 4 if i < 3 else 2
+            reach = {1: 12, 2: 4}.get(i, 2)
             span = weave.tile([P, reach, P, 4], BF16, name="w1_grouped_%d" % i, offset=w1_place(i), align_bytes=64)
             grouped = span[:, 0:2, :, :]
             for a in range(2):
@@ -191,20 +191,25 @@ def tile_list_pairwise_document_ranking_kernel(
         gate_w = {}
 
         def deal_wg():
-            words = staged.tile([P, 2, 4, 2 * P], U8, name="wg_dealt", offset=34 * KIB + 512, align_bytes=64)
-            nc.vector.tensor_copy(
+            words = weave.tile([P, 2, 4, 2 * P], U8, name="wg_dealt", offset=10 * KIB, align_bytes=64)
+            nc.gpsimd.tensor_copy(
                 words[:].bitcast(I32).rearrange("p a t (q w) -> p a t q w", w=4),
-                wg[:, :, H : 2 * H].bitcast(I32).rearrange("p a (q t w) -> p a t q w", t=4, w=4),
+                wg_rest[:, :, H - 2 * P : 2 * (H - P)].bitcast(I32).rearrange("p a (q t w) -> p a t q w", t=4, w=4),
             )
-            scales = staged.tile([P, 2, 4, P], U8, name="wg_sc_dealt", offset=36 * KIB + 512, align_bytes=64)
-            nc.vector.tensor_copy(
+            scales = weave.tile([P, 2, 4, P], U8, name="wg_sc_dealt", offset=12 * KIB, align_bytes=64)
+            nc.gpsimd.tensor_copy(
                 scales[:].bitcast(I32).rearrange("p a t (q w) -> p a t q w", w=2),
                 wg_sc[:, :, 512:H].bitcast(I32).rearrange("p a (q t w) -> p a t q w", t=4, w=2),
             )
             for a in range(2):
                 for t in range(4):
-                    gate_w[(t, a)] = (wg[:, a, 2 * P * t : 2 * P * (t + 1)], wg_sc[:, a, P * t : P * (t + 1)])
                     gate_w[(4 + t, a)] = (words[:, a, t, :], scales[:, a, t, :])
+
+        def natural_wg():
+            for a in range(2):
+                for t in range(4):
+                    words = wg_first[:, a, :] if t == 0 else wg_rest[:, a, 2 * P * (t - 1) : 2 * P * t]
+                    gate_w[(t, a)] = (words, wg_sc[:, a, P * t : P * (t + 1)])
 
         windows = {}
         a_banks = {}
@@ -230,7 +235,7 @@ def tile_list_pairwise_document_ranking_kernel(
             if i < 4:
                 windows[i] = weave.tile([P, 2 * S], F32, name="window_%d" % i, offset=WINDOW_PLACE[i], align_bytes=64)
             for d in range(2):
-                bank = bank_tile("g_bank_%d_%d" % (i, d), [P, 512], GATE_BANK + d)
+                bank = bank_tile("g_bank_%d_%d" % (i, d), [P, 512], (TURN_BANK if i == 0 else GATE_BANK) + d)
                 for a in range(2):
                     first_stage_pass(bank, gate_w[(i, a)], FP4X4, d, a)
                 if i < 4:
@@ -364,12 +369,15 @@ def tile_list_pairwise_document_ranking_kernel(
         load_tab(0)
         tab.append(staged.tile([P, 40 * KIB // 4], I32, name="tab1", offset=0, align_bytes=64))
         load_tab(1)
-        wg = staged.tile([P, 2, 2 * H], U8, name="wg", offset=40 * KIB, align_bytes=64)
-        nc.sync.dma_start(out=wg[:].bitcast(I32), in_=wg_words.rearrange("a p n -> p a n").bitcast(I32))
+        wg_rows = wg_words.bitcast(I32).rearrange("a p n -> p a n")
+        wg_first = staged.tile([P, 2, 2 * P], U8, name="wg_first", offset=40 * KIB, align_bytes=64)
+        nc.sync.dma_start(out=wg_first[:].bitcast(I32), in_=wg_rows[:, :, 0 : P // 2])
         load_w1(0, 1, 44 * KIB)
         gather_scales()
         gather_words(0, 1)
         load_w1(1, 1, 48 * KIB)
+        wg_rest = staged.tile([P, 2, 2 * (H - P)], U8, name="wg_rest", offset=60 * KIB, align_bytes=64)
+        nc.sync.dma_start(out=wg_rest[:].bitcast(I32), in_=wg_rows[:, :, P // 2 : H // 2])
         load_w1(2, 2, 52 * KIB)
         gather_words(1, 2)
         load_w1(4, 4, 0)
@@ -378,7 +386,7 @@ def tile_list_pairwise_document_ranking_kernel(
         with nc.allow_non_contiguous_dma(reason="one bias value for each partition"):
             nc.sync.dma_start(out=c_t[:], in_=c.rearrange("(t p) -> p t", p=P))
         prep_w1_first()
-        deal_wg()
+        natural_wg()
         products(0)
         prep_w1(1)
         products(1)
@@ -387,6 +395,7 @@ def tile_list_pairwise_document_ranking_kernel(
         features(0)
         first_0 = keep.tile([P, PAIRS], F32, name="first_0")
         picked = pick_tiles([0], [first_0[:]], [placed("second_0", PAIRS, w1_place(1))])
+        deal_wg()
         prep_w1(3)
         products(2)
         features(1)

@@ -21,8 +21,27 @@ SIGMOID = mybir.ActivationFunctionType.Sigmoid
 
 P = 128
 KIB = 1024
+BANK = 512
+NATURAL = 4
+SHARED_FROM = 6
 SHARED = 320
+W2_SHARED = 384
 PIECES = [(0, 256), (256, 128), (384, 128)]
+
+TURN_BANK, SUM_BANK, GATE_BANK = 0, 2, 6
+
+ZEROS_SPAN = 48 * KIB
+TABLE_1_SPAN = 40 * KIB
+TABLE_0_AT = 48 * KIB
+TABLE_SCALES_AT = 64 * KIB
+
+ROUNDED_NATURAL_AT = 0
+Z_NATURAL_AT = 28 * KIB
+WG_DEALT_AT = 37 * KIB
+ROUNDED_DEALT_AT = 40 * KIB
+WINDOW_AT = [76 * KIB, 37 * KIB, 56 * KIB, 48 * KIB, 43 * KIB, 60 * KIB, 43 * KIB, 60 * KIB]
+GATE_AT = {4: 76 * KIB, 5: 80 * KIB, 6: 72 * KIB, 7: 68 * KIB}
+W2_ROUNDED_AT = [47 * KIB, 76 * KIB]
 
 
 def tile_list_pairwise_document_ranking_kernel(
@@ -31,312 +50,301 @@ def tile_list_pairwise_document_ranking_kernel(
     nc = tc.nc
     with ExitStack() as ctx:
         keep = ctx.enter_context(tc.tile_pool(name="keep", bufs=1))
-        staged = ctx.enter_context(tc.tile_pool(name="staged", bufs=1))
-        weave = ctx.enter_context(tc.tile_pool(name="weave", bufs=1))
+        loads = ctx.enter_context(tc.tile_pool(name="loads", bufs=1))
+        work = ctx.enter_context(tc.tile_pool(name="work", bufs=1))
         psum = ctx.enter_context(tc.psum_pool(name="psum", bufs=1))
 
         def bank_tile(name, shape, bank):
             return psum.tile(shape, F32, name=name, offset=2 * KIB * bank)
 
-        GATE_BANK, SUM_BANK, TURN_BANK = 6, 2, 0
-        WINDOW_PLACE = [32 * KIB, 40 * KIB, 56 * KIB, 48 * KIB, 43 * KIB, 60 * KIB, 43 * KIB, 60 * KIB]
-        GATE_PLACE = {4: 32 * KIB, 5: 36 * KIB, 6: 72 * KIB, 7: 68 * KIB}
+        def placed(name, width, offset):
+            return work.tile([P, width], F32, name=name, offset=offset, align_bytes=64)[:]
 
         offs_t = keep.tile([P, S // 16], U16, name="offs_t")
         pos1_t = keep.tile([P, PAIRS // 16], U16, name="pos1_t")
         pos2_t = keep.tile([P, PAIRS // 16], U16, name="pos2_t")
-        tab_sc = staged.tile([P, T], U8, name="tab_sc", offset=64 * KIB, align_bytes=64)
+        tab_sc = loads.tile([P, T], U8, name="tab_sc", offset=TABLE_SCALES_AT, align_bytes=64)
         v_sc = [keep.tile([P, S], U8, name="v_sc%d" % a, align_bytes=64) for a in range(2)]
         ident = keep.tile([P, P], F32, name="ident")
-        zeros = staged.tile([P, 48 * KIB // 4], I32, name="zeros", offset=0, align_bytes=64)
-        tab = [staged.tile([P, T], I32, name="tab0", offset=48 * KIB, align_bytes=64)]
+        zeros = loads.tile([P, ZEROS_SPAN // 4], I32, name="zeros", offset=0, align_bytes=64)
+        tab = [loads.tile([P, T], I32, name="tab0", offset=TABLE_0_AT, align_bytes=64)]
         make_identity(nc, ident[:])
-        nc.vector.memset(tab_sc[:, 0:T].bitcast(I32), 0)
+
+        nc.vector.memset(tab_sc[:].bitcast(I32), 0)
         wg_sc = keep.tile([P, 2, H], U8, name="wg_sc", align_bytes=64)
         nc.vector.memset(wg_sc[:].bitcast(I32), 0)
         nc.vector.memset(zeros[:, 0 : S // 4], 0)
         nc.vector.tensor_copy(v_sc[1][:].bitcast(I32), zeros[:, 0 : S // 4])
         scale_rows = tab_scales.bitcast(I32).rearrange("a (q r) t -> r q a t", r=4)
         for r in range(4):
-            nc.scalar.dma_start(out=tab_sc[r:P:16, 0:T].bitcast(I32), in_=scale_rows[r])
+            nc.scalar.dma_start(out=tab_sc[r:P:16, :].bitcast(I32), in_=scale_rows[r])
         for q in range(4):
             nc.gpsimd.dma_start(
                 out=wg_sc[32 * q : 32 * q + 4, :, :].bitcast(I32),
                 in_=wg_scales[:, 4 * q : 4 * q + 4, :].rearrange("a r t -> r a t").bitcast(I32),
             )
 
-        def load_tab(a):
+        def load_table(a):
             nc.sync.dma_start(out=tab[a][:, 0:T], in_=tab_words[a].rearrange("p t i -> p (t i)").bitcast(I32))
+
+        def load_wg(name, first, count, offset):
+            words = loads.tile([P, 2, 2 * count], U8, name=name, offset=offset, align_bytes=64)
+            rows = wg_words.bitcast(I32).rearrange("a p n -> p a n")
+            nc.sync.dma_start(out=words[:].bitcast(I32), in_=rows[:, :, first // 2 : (first + count) // 2])
+            return words
 
         w1_raw = {}
 
         def load_w1(first, count, offset):
             for a in range(2):
-                raw = staged.tile(
+                raw = loads.tile(
                     [P, 4, count * P], F32, name="w1_raw_%d_%d" % (first, a),
                     offset=offset + a * count * 2 * KIB, align_bytes=64,
                 )
-                nc.sync.dma_start(
-                    out=raw[:],
-                    in_=w1[512 * a : 512 * (a + 1), first * P : (first + count) * P].rearrange(
-                        "(p j) c -> p j c", j=4
-                    ),
-                )
-                for i in range(first, first + count):
-                    if i < 4:
-                        cols = raw[:, :, (i - first) * P : (i - first + 1) * P]
-                        w1_raw[(i, a)] = cols.rearrange("p j (g i) -> p g j i", i=2)
-                    else:
-                        w1_raw[(i, a)] = raw[:].rearrange("p j (q t h i) -> p t q h j i", t=4, h=4, i=2)[:, i - 4]
-
-        w2_raw = []
+                cols = w1[512 * a : 512 * (a + 1), first * P : (first + count) * P]
+                nc.sync.dma_start(out=raw[:], in_=cols.rearrange("(p j) c -> p j c", j=4))
+                if first < NATURAL:
+                    w1_raw[(first, a)] = raw[:].rearrange("p j (g i) -> p g j i", i=2)
+                else:
+                    dealt = raw[:].rearrange("p j (q t g i) -> p t q g j i", t=4, g=4, i=2)
+                    for t in range(count):
+                        w1_raw[(first + t, a)] = dealt[:, t]
 
         def load_w2(offset):
-            natural = staged.tile([P, 4, N], F32, name="w2_raw0", offset=offset, align_bytes=64)
-            nc.sync.dma_start(out=natural[:], in_=w2[0:512, :].rearrange("(p j) n -> p j n", j=4))
-            dealt = staged.tile([P, 4, N], F32, name="w2_raw1", offset=offset + 8 * KIB, align_bytes=64)
+            natural = loads.tile([P, 4, N], F32, name="w2_raw0", offset=offset, align_bytes=64)
+            nc.sync.dma_start(out=natural[:], in_=w2[0:512, :].rearrange("(p t) n -> p t n", t=4))
+            dealt = loads.tile([P, 4, N], F32, name="w2_raw1", offset=offset + 8 * KIB, align_bytes=64)
             rows = w2[512:1024, :].rearrange("(q t e) n -> t q e n", t=4, e=8)
             for t in range(4):
                 nc.sync.dma_start(out=dealt[:, t, :], in_=rows[t])
-            w2_raw.extend([natural, dealt])
+            return natural, dealt
+
+        def gather_scales():
+            nc.vector.tensor_copy(v_sc[0][:], tab_sc[:].indirect(offs_t[:]))
+            nc.scalar.dma_start(out=v_sc[1][0 : P - 16, :].bitcast(I32), in_=v_sc[0][16:P, :].bitcast(I32))
 
         v_words = {}
 
-        def gather_scales():
-            nc.vector.tensor_copy(v_sc[0][:], tab_sc[:, 0:T].indirect(offs_t[:]))
-            nc.scalar.dma_start(out=v_sc[1][0:112, :].bitcast(I32), in_=v_sc[0][16:128, :].bitcast(I32))
+        def gather_first_pass():
+            words = loads.tile([P, S], U32, name="v_words_0", offset=TABLE_SCALES_AT, align_bytes=64)
+            nc.vector.tensor_copy(words[:], tab[0][:, 0:T].bitcast(U32).indirect(offs_t[:]))
+            for d in range(2):
+                v_words[(0, d)] = words[:, BANK * d : BANK * (d + 1)]
 
-        def gather_words(a, halves):
-            width = S // halves
-            for h in range(halves):
-                if a == 0:
-                    words = staged.tile([P, width], U32, name="v_words_0", offset=64 * KIB, align_bytes=64)
-                else:
-                    words = keep.tile([P, width], U32, name="v_words_1_%d" % h, align_bytes=64)
-                nc.vector.tensor_copy(
-                    words[:],
-                    tab[a][:, 0:T].bitcast(U32).indirect(offs_t[:, h * width // 16 : (h + 1) * width // 16]),
-                )
-                for d in range(width // 512):
-                    v_words[(a, h * (width // 512) + d)] = words[:, 512 * d : 512 * (d + 1)]
+        def gather_second_pass():
+            for d in range(2):
+                words = keep.tile([P, BANK], U32, name="v_words_1_%d" % d, align_bytes=64)
+                entries = offs_t[:, BANK * d // 16 : BANK * (d + 1) // 16]
+                nc.vector.tensor_copy(words[:], tab[1][:, 0:T].bitcast(U32).indirect(entries))
+                v_words[(1, d)] = words[:]
 
-        def quantise(name, grouped, width, place=None):
-            if place is None:
-                codes = keep.tile([P, width], U32, name="codes_" + name, align_bytes=64)
-            else:
-                codes = weave.tile([P, width], U32, name="codes_" + name, offset=place, align_bytes=64)
+        def quantise(name, rounded, width, pool=keep, offset=None):
+            codes = pool.tile([P, width], U32, name="codes_" + name, offset=offset, align_bytes=64)
             scales = keep.tile([P, width], U8, name="scales_" + name, align_bytes=64)
-            nc.vector.quantize_mx(out=codes[:].bitcast(FP8X4), scales=scales[:], in_=grouped)
+            nc.vector.quantize_mx(out=codes[:].bitcast(FP8X4), scales=scales[:], in_=rounded)
             return codes, scales
+
+        def gpsimd_round(out, in_):
+            nc.gpsimd.tensor_scalar(out, in_, 1.0, 0.0, MULT, ADD)
+
+        def rounded_w1_at(i):
+            return ROUNDED_NATURAL_AT + 2 * KIB * i if i < NATURAL else ROUNDED_DEALT_AT + 2 * KIB * (i - NATURAL)
+
+        def round_w1(copy, dst, i, a):
+            if i < NATURAL:
+                view = dst.rearrange("p (g i) j -> p g j i", i=2)
+            else:
+                view = dst.rearrange("p (q g i) j -> p q g j i", g=4, i=2)
+            copy(out=view, in_=w1_raw[(i, a)])
 
         w1_q = {}
 
-        def round_w1(copy, dst, i, a):
-            if i < 4:
-                view = dst.rearrange("p (g i) j -> p g j i", i=2)
-            else:
-                view = dst.rearrange("p (q h i) j -> p q h j i", h=4, i=2)
-            copy(out=view, in_=w1_raw[(i, a)])
-
-        def prep_w1_first():
-            early = keep.tile([P, P, 4], BF16, name="w1_grouped_0_0", align_bytes=64)
-            late = staged.tile([P, P, 4], BF16, name="w1_grouped_0_1", offset=36 * KIB, align_bytes=64)
-            for a, grouped, copy in ((0, early, nc.scalar.copy), (1, late, nc.vector.tensor_copy)):
-                round_w1(copy, grouped[:], 0, a)
-                pool, place = ((staged, 38 * KIB), (weave, w1_place(1)))[a]
-                codes = pool.tile([P, P], U32, name="codes_w1_0_%d" % a, offset=place, align_bytes=64)
-                scales = keep.tile([P, P], U8, name="scales_w1_0_%d" % a, align_bytes=64)
-                nc.vector.quantize_mx(
-                    out=codes[:].bitcast(FP8X4), scales=scales[:], in_=grouped[:].rearrange("p c j -> p (c j)")
-                )
+        def prepare_first_w1():
+            early = keep.tile([P, P, 4], BF16, name="w1_rounded_0_0", align_bytes=64)
+            late = loads.tile([P, P, 4], BF16, name="w1_rounded_0_1", offset=TABLE_1_SPAN - 4 * KIB, align_bytes=64)
+            passes = (
+                (early, nc.scalar.copy, loads, TABLE_1_SPAN - 2 * KIB),
+                (late, nc.vector.tensor_copy, work, rounded_w1_at(1)),
+            )
+            for a, (rounded, copy, pool, offset) in enumerate(passes):
+                round_w1(copy, rounded[:], 0, a)
+                codes, scales = quantise("w1_0_%d" % a, rounded[:].rearrange("p c j -> p (c j)"), P, pool, offset)
                 w1_q[(0, a)] = (codes[:], scales[:])
 
-        def w1_place(i):
-            return 2 * KIB * i if i < 4 else WINDOW_PLACE[1] + 2 * KIB * (i - 4)
-
-        W2_PLACE = [47 * KIB, 32 * KIB]
-
-        def pool_round(out, in_):
-            nc.gpsimd.tensor_scalar(out, in_, 1.0, 0.0, MULT, ADD)
-
-        def prep_w1(i):
-            reach = {1: 12, 2: 4}.get(i, 2)
-            span = weave.tile([P, reach, P, 4], BF16, name="w1_grouped_%d" % i, offset=w1_place(i), align_bytes=64)
-            grouped = span[:, 0:2, :, :]
+        def prepare_w1(i):
+            reach = 4 if i < NATURAL - 1 else 2
+            span = work.tile([P, reach, P, 4], BF16, name="w1_rounded_%d" % i, offset=rounded_w1_at(i), align_bytes=64)
+            rounded = span[:, 0:2, :, :]
             for a in range(2):
-                if a == 0 and i in (4, 5):
-                    pool_round(
-                        grouped[:, a, :, :].rearrange("p (q e) j -> p q e j", e=8),
-                        w1_raw[(i, a)].rearrange("p q h j i -> p q (h i) j"),
+                if (i, a) == (NATURAL, 0):
+                    gpsimd_round(
+                        rounded[:, a, :, :].rearrange("p (q e) j -> p q e j", e=8),
+                        w1_raw[(i, a)].rearrange("p q g j i -> p q (g i) j"),
                     )
                 else:
-                    round_w1(nc.scalar.copy, grouped[:, a, :, :], i, a)
-            codes, scales = quantise("w1_%d" % i, grouped.rearrange("p a c j -> p (a c j)"), 2 * P)
+                    round_w1(nc.scalar.copy, rounded[:, a, :, :], i, a)
+            codes, scales = quantise("w1_%d" % i, rounded.rearrange("p a c j -> p (a c j)"), 2 * P)
             for a in range(2):
                 w1_q[(i, a)] = (codes[:, P * a : P * (a + 1)], scales[:, P * a : P * (a + 1)])
 
         w2_q = {}
 
         def round_w2(b):
-            grouped = weave.tile([P, N, 4], BF16, name="w2_grouped%d" % b, offset=W2_PLACE[b], align_bytes=64)
+            rounded = work.tile([P, N, 4], BF16, name="w2_rounded%d" % b, offset=W2_ROUNDED_AT[b], align_bytes=64)
             if b == 0:
-                pool_round(grouped[:, 0:384, :], w2_raw[b][:, :, 0:384].rearrange("p j c -> p c j"))
-            for cols in ([slice(384, N)], [slice(0, 256), slice(256, N)])[b]:
+                gpsimd_round(rounded[:, 0:W2_SHARED, :], w2_raw[b][:, :, 0:W2_SHARED].rearrange("p t n -> p n t"))
+                parts = [slice(W2_SHARED, N)]
+            else:
+                parts = [slice(0, N // 2), slice(N // 2, N)]
+            for cols in parts:
                 nc.scalar.copy(
-                    out=grouped[:, cols, :].rearrange("p (g i) j -> p g j i", i=2),
-                    in_=w2_raw[b][:, :, cols].rearrange("p j (g i) -> p g j i", i=2),
+                    out=rounded[:, cols, :].rearrange("p (g i) t -> p g t i", i=2),
+                    in_=w2_raw[b][:, :, cols].rearrange("p t (g i) -> p g t i", i=2),
                 )
-            return grouped[:].rearrange("p c j -> p (c j)")
+            return rounded[:].rearrange("p n t -> p (n t)")
 
         gate_w = {}
 
+        def name_natural_wg():
+            for a in range(2):
+                for i in range(NATURAL):
+                    words = wg_first[:, a, :] if i == 0 else wg_rest[:, a, 2 * P * (i - 1) : 2 * P * i]
+                    gate_w[(i, a)] = (words, wg_sc[:, a, P * i : P * (i + 1)])
+
         def deal_wg():
-            words = weave.tile([P, 2, 4, 2 * P], U8, name="wg_dealt", offset=10 * KIB, align_bytes=64)
+            words = work.tile([P, 2, 4, 2 * P], U8, name="wg_dealt", offset=WG_DEALT_AT, align_bytes=64)
             nc.gpsimd.tensor_copy(
                 words[:].bitcast(I32).rearrange("p a t (q w) -> p a t q w", w=4),
-                wg_rest[:, :, H - 2 * P : 2 * (H - P)].bitcast(I32).rearrange("p a (q t w) -> p a t q w", t=4, w=4),
+                wg_high[:].bitcast(I32).rearrange("p a (q t w) -> p a t q w", t=4, w=4),
             )
-            scales = weave.tile([P, 2, 4, P], U8, name="wg_sc_dealt", offset=12 * KIB, align_bytes=64)
+            scales = work.tile([P, 2, 4, P], U8, name="wg_sc_dealt", offset=WG_DEALT_AT + 2 * KIB, align_bytes=64)
             nc.gpsimd.tensor_copy(
                 scales[:].bitcast(I32).rearrange("p a t (q w) -> p a t q w", w=2),
-                wg_sc[:, :, 512:H].bitcast(I32).rearrange("p a (q t w) -> p a t q w", t=4, w=2),
+                wg_sc[:, :, H // 2 : H].bitcast(I32).rearrange("p a (q t w) -> p a t q w", t=4, w=2),
             )
             for a in range(2):
                 for t in range(4):
-                    gate_w[(4 + t, a)] = (words[:, a, t, :], scales[:, a, t, :])
-
-        def natural_wg():
-            for a in range(2):
-                for t in range(4):
-                    words = wg_first[:, a, :] if t == 0 else wg_rest[:, a, 2 * P * (t - 1) : 2 * P * t]
-                    gate_w[(t, a)] = (words, wg_sc[:, a, P * t : P * (t + 1)])
+                    gate_w[(NATURAL + t, a)] = (words[:, a, t, :], scales[:, a, t, :])
 
         windows = {}
-        a_banks = {}
+        w1_sums = {}
         gates = {}
         shared_sums = {}
 
-        def placed(name, width, offset):
-            return weave.tile([P, width], F32, name=name, offset=offset, align_bytes=64)[:]
-
-        def first_stage_pass(bank, weights, fmt, d, a):
-            codes, scales = weights
-            nc.tensor.matmul_mx(
-                out=bank[:],
-                lhsT=codes.bitcast(fmt),
-                lhsT_scale=scales,
-                rhs=v_words[(a, d)].bitcast(FP8X4),
-                rhs_scale=v_sc[a][:, 512 * d : 512 * (d + 1)],
-                start=(a == 0),
-                stop=(a == 1),
-            )
+        def first_stage_sum(bank, weights, fmt, i, d):
+            for a in range(2):
+                codes, scales = weights[(i, a)]
+                nc.tensor.matmul_mx(
+                    out=bank[:],
+                    lhsT=codes.bitcast(fmt),
+                    lhsT_scale=scales,
+                    rhs=v_words[(a, d)].bitcast(FP8X4),
+                    rhs_scale=v_sc[a][:, BANK * d : BANK * (d + 1)],
+                    start=(a == 0),
+                    stop=(a == 1),
+                )
 
         def products(i):
-            if i < 4:
-                windows[i] = weave.tile([P, 2 * S], F32, name="window_%d" % i, offset=WINDOW_PLACE[i], align_bytes=64)
+            gate_bank = TURN_BANK if i == 0 else GATE_BANK
+            sum_bank = GATE_BANK if i == 0 else SUM_BANK + 2 * (i % 2)
+            if i < NATURAL:
+                windows[i] = work.tile([P, 2 * S], F32, name="window_%d" % i, offset=WINDOW_AT[i], align_bytes=64)
             for d in range(2):
-                bank = bank_tile("g_bank_%d_%d" % (i, d), [P, 512], (TURN_BANK if i == 0 else GATE_BANK) + d)
-                for a in range(2):
-                    first_stage_pass(bank, gate_w[(i, a)], FP4X4, d, a)
-                if i < 4:
-                    gates[(i, d)] = windows[i][:, S + 512 * d : S + 512 * (d + 1)]
+                bank = bank_tile("g_bank_%d_%d" % (i, d), [P, BANK], gate_bank + d)
+                first_stage_sum(bank, gate_w, FP4X4, i, d)
+                if i < NATURAL:
+                    gates[(i, d)] = windows[i][:, S + BANK * d : S + BANK * (d + 1)]
                 else:
-                    gates[(i, d)] = placed("gate_%d_%d" % (i, d), 512, GATE_PLACE[i] + 2 * KIB * d)
+                    gates[(i, d)] = placed("gate_%d_%d" % (i, d), BANK, GATE_AT[i] + 2 * KIB * d)
                 nc.scalar.copy(out=gates[(i, d)], in_=bank[:])
             for d in range(2):
-                bank = GATE_BANK + d if i == 0 else SUM_BANK + 2 * (i % 2) + d
-                a_banks[(i, d)] = bank_tile("a_bank_%d_%d" % (i, d), [P, 512], bank)
-                for a in range(2):
-                    first_stage_pass(a_banks[(i, d)], w1_q[(i, a)], FP8X4, d, a)
-            if i >= 6:
+                w1_sums[(i, d)] = bank_tile("a_bank_%d_%d" % (i, d), [P, BANK], sum_bank + d)
+                first_stage_sum(w1_sums[(i, d)], w1_q, FP8X4, i, d)
+            if i >= SHARED_FROM:
                 shared_sums[i] = keep.tile([P, SHARED], F32, name="shared_sums_%d" % i)[:]
-                nc.scalar.copy(out=shared_sums[i], in_=a_banks[(i, 1)][:, 512 - SHARED : 512])
+                nc.scalar.copy(out=shared_sums[i], in_=w1_sums[(i, 1)][:, BANK - SHARED : BANK])
 
         def features(i):
-            if i >= 4:
-                windows[i] = weave.tile([P, S], F32, name="window_%d" % i, offset=WINDOW_PLACE[i], align_bytes=64)
-            own = 512 - SHARED if i >= 6 else 512
-            nc.vector.tensor_tensor(windows[i][:, 0:512], a_banks[(i, 0)][:], gates[(i, 0)], MULT)
+            if i >= NATURAL:
+                windows[i] = work.tile([P, S], F32, name="window_%d" % i, offset=WINDOW_AT[i], align_bytes=64)
+            own = BANK - SHARED if i >= SHARED_FROM else BANK
+            nc.vector.tensor_tensor(windows[i][:, 0:BANK], w1_sums[(i, 0)][:], gates[(i, 0)], MULT)
             nc.vector.tensor_tensor(
-                windows[i][:, 512 : 512 + own], a_banks[(i, 1)][:, 0:own], gates[(i, 1)][:, 0:own], MULT
+                windows[i][:, BANK : BANK + own], w1_sums[(i, 1)][:, 0:own], gates[(i, 1)][:, 0:own], MULT
             )
-            if i >= 6:
-                nc.gpsimd.tensor_tensor(windows[i][:, 512 + own : S], shared_sums[i], gates[(i, 1)][:, own:512], MULT)
+            if i >= SHARED_FROM:
+                nc.gpsimd.tensor_tensor(windows[i][:, BANK + own : S], shared_sums[i], gates[(i, 1)][:, own:BANK], MULT)
+
+
+        def pick_natural(tiles, firsts, negated_seconds):
+            for i, dst in zip(tiles, firsts):
+                nc.vector.tensor_copy(dst, windows[i][:, 0:S].indirect(pos1_t[:]))
+            for i, dst in zip(tiles, negated_seconds):
+                nc.vector.tensor_scalar(dst, windows[i][:].indirect(pos2_t[:]), -1.0, 0.0, MULT, ADD)
+            return list(zip(firsts, negated_seconds))
 
         z_turned = keep.tile([P, 4, 2, 2 * P], BF16, name="z_turned", align_bytes=64)
 
-        def pick_first(i, dst):
-            nc.vector.tensor_copy(dst, windows[i][:, 0:S].indirect(pos1_t[:]))
-
-        def pick_negated_second(i, dst):
-            nc.vector.tensor_scalar(dst, windows[i][:].indirect(pos2_t[:]), -1.0, 0.0, MULT, ADD)
-
-        def pick_tiles(tiles, firsts, seconds):
-            for i, dst in zip(tiles, firsts):
-                pick_first(i, dst)
-            for i, dst in zip(tiles, seconds):
-                pick_negated_second(i, dst)
-            return list(zip(firsts, seconds))
-
-        def turn(i, first, second):
+        def turn(i, first, negated_second):
             bank = bank_tile("zt_bank_%d" % i, [P, 4, P], TURN_BANK + i % 2)
             for jb in range(4):
                 cols = slice(P * jb, P * (jb + 1))
-                nc.tensor.matmul(bank[:, jb, :], first[:, cols], ident[:], start=True, stop=False, is_transpose=True)
-                nc.tensor.matmul(bank[:, jb, :], second[:, cols], ident[:], start=False, stop=True, is_transpose=True)
+                for term, last in ((first, False), (negated_second, True)):
+                    nc.tensor.matmul(
+                        bank[:, jb, :], term[:, cols], ident[:], start=not last, stop=last, is_transpose=True
+                    )
             nc.scalar.copy(
                 out=z_turned[:, :, :, 64 * i : 64 * (i + 1)].rearrange("j b u (m e) -> j b u m e", e=2),
                 in_=bank[:].rearrange("j b (m u e) -> j b u m e", u=2, e=2),
             )
 
-        z_q = {}
-
         def turn_z_back():
             words = z_turned[:].bitcast(F32)
-            grouped = weave.tile([P, PAIRS, 4], BF16, name="z_grouped_0", offset=28 * KIB, align_bytes=64)[:]
-            grouped_words = grouped.bitcast(F32)
+            rounded = work.tile([P, PAIRS, 4], BF16, name="z_rounded_0", offset=Z_NATURAL_AT, align_bytes=64)[:]
+            rounded_words = rounded.bitcast(F32)
             for g in range(2):
                 bank = bank_tile("back_bank_%d" % g, [P, 2, 2, P], TURN_BANK + g)
                 for jb in range(2):
                     for u in range(2):
                         nc.tensor.transpose(bank[:, jb, u, :], words[:, 2 * g + jb, u, :], ident[:])
                 nc.scalar.copy(
-                    out=grouped_words[:, 256 * g : 256 * (g + 1), :].rearrange("p (b j) u -> p b j u", b=2),
+                    out=rounded_words[:, 256 * g : 256 * (g + 1), :].rearrange("p (b j) u -> p b j u", b=2),
                     in_=bank[:].rearrange("p b u j -> p b j u"),
                 )
-            return grouped
+            return rounded
 
-        def quantise_z_natural(grouped):
-            place = GATE_PLACE[5] + 2 * KIB
-            codes, scales = quantise("z_0", grouped.rearrange("p c t -> p (c t)"), PAIRS, place)
+        z_q = {}
+
+        def quantise_z_natural(rounded):
+            flat = rounded.rearrange("p j t -> p (j t)")
+            codes, scales = quantise("z_0", flat, PAIRS, work, GATE_AT[5] + 2 * KIB)
             for h, (j0, width) in enumerate(PIECES):
                 z_q[(0, h)] = (codes[:, j0 : j0 + width], scales[:, j0 : j0 + width])
 
-        z_grouped = [
-            keep.tile([P, width, 4], BF16, name="z_grouped_1_%d" % h, align_bytes=64)
+
+        z_dealt = [
+            keep.tile([P, width, 4], BF16, name="z_rounded_1_%d" % h, align_bytes=64)
             for h, (j0, width) in enumerate(PIECES)
         ]
 
-        def pick_second(i, dst, cols16):
-            nc.vector.tensor_copy(dst, windows[i][:].indirect(pos2_t[:, cols16]))
+        def pick_dealt(tiles, seconds, differences, j0, width):
+            entries = slice(j0 // 16, (j0 + width) // 16)
+            for i, second in zip(tiles, seconds):
+                nc.vector.tensor_copy(second, windows[i][:].indirect(pos2_t[:, entries]))
+            for t, (i, second) in enumerate(zip(tiles, seconds)):
+                nc.vector.tensor_tensor(differences[:, t, :], windows[i][:].indirect(pos1_t[:, entries]), second, SUB)
 
-        def pick_difference(i, dst, second, cols16):
-            nc.vector.tensor_tensor(dst, windows[i][:].indirect(pos1_t[:, cols16]), second, SUB)
-
-        def round_planes(copy, h, u, planes):
-            copy(out=z_grouped[h][:, :, 2 * u : 2 * u + 2], in_=planes.rearrange("p t j -> p j t"))
+        def round_differences(copy, h, u, differences):
+            copy(out=z_dealt[h][:, :, 2 * u : 2 * u + 2], in_=differences.rearrange("p t j -> p j t"))
 
         def quantise_z_dealt(h):
-            codes, scales = quantise("z_1_%d" % h, z_grouped[h][:].rearrange("p c t -> p (c t)"), PIECES[h][1])
+            codes, scales = quantise("z_1_%d" % h, z_dealt[h][:].rearrange("p j t -> p (j t)"), PIECES[h][1])
             z_q[(1, h)] = (codes[:], scales[:])
+
 
         y_banks = {}
 
         def second_stage_pass(h, nt, b):
-            if b == 0:
-                early = (GATE_BANK, GATE_BANK + 1, TURN_BANK + 1, TURN_BANK)
-                bank = SUM_BANK + nt if h == 1 else early[nt]
-                y_banks[(h, nt)] = bank_tile("y_bank_%d_%d" % (h, nt), [P, PIECES[h][1]], bank)
             w_codes, w_scales = w2_q[b]
             z_codes, z_scales = z_q[(b, h)]
             nc.tensor.matmul_mx(
@@ -349,9 +357,16 @@ def tile_list_pairwise_document_ranking_kernel(
                 stop=(b == 1),
             )
 
+        def open_scores(h):
+            free_early = (GATE_BANK, GATE_BANK + 1, TURN_BANK + 1, TURN_BANK)
+            for nt in range(N // P):
+                bank = SUM_BANK + nt if h == 1 else free_early[nt]
+                y_banks[(h, nt)] = bank_tile("y_bank_%d_%d" % (h, nt), [P, PIECES[h][1]], bank)
+                second_stage_pass(h, nt, 0)
+
         out_view = out.rearrange("(t p) j -> p t j", p=P)
 
-        def scores(h, group):
+        def close_scores(h, group):
             j0, width = PIECES[h]
             for first in range(0, N // P, group):
                 result = keep.tile([P, group, width], F32, name="result_%d_%d" % (h, first))
@@ -359,103 +374,94 @@ def tile_list_pairwise_document_ranking_kernel(
                     nt = first + k
                     second_stage_pass(h, nt, 1)
                     nc.scalar.activation(result[:, k, :], y_banks[(h, nt)][:], SIGMOID, bias=c_t[:, nt : nt + 1])
-                nc.sync.dma_start(
-                    out=out_view[:, first : first + group, j0 : j0 + width], in_=result[:]
-                )
+                nc.sync.dma_start(out=out_view[:, first : first + group, j0 : j0 + width], in_=result[:])
 
         nc.sync.dma_start(offs_t[:], offs)
+        load_table(0)
         nc.sync.dma_start(pos1_t[:], pos1)
         nc.sync.dma_start(pos2_t[:], pos2)
-        load_tab(0)
-        tab.append(staged.tile([P, 40 * KIB // 4], I32, name="tab1", offset=0, align_bytes=64))
-        load_tab(1)
-        wg_rows = wg_words.bitcast(I32).rearrange("a p n -> p a n")
-        wg_first = staged.tile([P, 2, 2 * P], U8, name="wg_first", offset=40 * KIB, align_bytes=64)
-        nc.sync.dma_start(out=wg_first[:].bitcast(I32), in_=wg_rows[:, :, 0 : P // 2])
-        load_w1(0, 1, 44 * KIB)
+        tab.append(loads.tile([P, TABLE_1_SPAN // 4], I32, name="tab1", offset=0, align_bytes=64))
+        load_table(1)
+        wg_first = load_wg("wg_first", 0, P, TABLE_1_SPAN)
+        load_w1(0, 1, TABLE_1_SPAN + 4 * KIB)
         gather_scales()
-        gather_words(0, 1)
-        load_w1(1, 1, 48 * KIB)
-        wg_rest = staged.tile([P, 2, 2 * (H - P)], U8, name="wg_rest", offset=60 * KIB, align_bytes=64)
-        nc.sync.dma_start(out=wg_rest[:].bitcast(I32), in_=wg_rows[:, :, P // 2 : H // 2])
-        load_w1(2, 2, 52 * KIB)
-        gather_words(1, 2)
-        load_w1(4, 4, 0)
-        load_w2(16 * KIB)
-        c_t = staged.tile([P, N // P], F32, name="c_t", offset=32 * KIB, align_bytes=64)
+        gather_first_pass()
+        load_w1(1, 1, TABLE_0_AT)
+        wg_rest = load_wg("wg_rest", P, H // 2 - P, TABLE_0_AT + 12 * KIB)
+        load_w1(2, 1, TABLE_0_AT + 4 * KIB)
+        load_w1(3, 1, TABLE_0_AT + 8 * KIB)
+        wg_high = load_wg("wg_high", H // 2, H // 2, TABLE_0_AT + 14 * KIB)
+        gather_second_pass()
+        load_w1(NATURAL, 4, 0)
+        w2_raw = load_w2(16 * KIB)
+        c_t = loads.tile([P, N // P], F32, name="c_t", offset=32 * KIB, align_bytes=64)
         with nc.allow_non_contiguous_dma(reason="one bias value for each partition"):
             nc.sync.dma_start(out=c_t[:], in_=c.rearrange("(t p) -> p t", p=P))
-        prep_w1_first()
-        natural_wg()
+
+        prepare_first_w1()
+        name_natural_wg()
         products(0)
-        prep_w1(1)
+        prepare_w1(1)
         products(1)
-        prep_w1(2)
+        prepare_w1(2)
 
         features(0)
         first_0 = keep.tile([P, PAIRS], F32, name="first_0")
-        picked = pick_tiles([0], [first_0[:]], [placed("second_0", PAIRS, w1_place(1))])
-        deal_wg()
-        prep_w1(3)
+        picked = pick_natural([0], [first_0[:]], [placed("second_0", PAIRS, rounded_w1_at(1))])
+        prepare_w1(3)
         products(2)
         features(1)
         products(3)
-        picked += pick_tiles([1], [placed("first_1", PAIRS, w1_place(2))], [placed("second_1", PAIRS, w1_place(3))])
-        for i in range(2):
+        picked += pick_natural(
+            [1], [placed("first_1", PAIRS, rounded_w1_at(2))], [placed("second_1", PAIRS, rounded_w1_at(3))]
+        )
+        deal_wg()
+        for i in (0, 1):
             turn(i, *picked[i])
 
         features(2)
-        prep_w1(4)
+        prepare_w1(4)
         products(4)
         features(3)
-        prep_w1(5)
+        prepare_w1(5)
         products(5)
-        prep_w1(6)
-        prep_w1(7)
+        prepare_w1(6)
+        prepare_w1(7)
         second_3 = keep.tile([P, PAIRS], F32, name="second_3")
-        picked += pick_tiles(
+        picked += pick_natural(
             [2, 3],
-            [windows[3][:, S : S + PAIRS], placed("first_3", PAIRS, w1_place(4))],
-            [placed("second_2", PAIRS, w1_place(5)), second_3[:]],
+            [windows[3][:, S : S + PAIRS], placed("first_3", PAIRS, rounded_w1_at(4))],
+            [placed("second_2", PAIRS, rounded_w1_at(5)), second_3[:]],
         )
-        for i in range(2, 4):
+        for i in (2, 3):
             turn(i, *picked[i])
-        z_back = turn_z_back()
+        z_natural = turn_z_back()
         w2_q[0] = quantise("w2_0", round_w2(0), N)
 
         features(4)
         products(6)
         features(5)
         products(7)
-        quantise_z_natural(z_back)
+        quantise_z_natural(z_natural)
         w2_rounded = round_w2(1)
-        whole = slice(0, PAIRS // 16)
-        seconds = [placed("second_4", PAIRS, GATE_PLACE[5]), placed("second_5", PAIRS, W2_PLACE[0])]
-        for t in range(2):
-            pick_second(4 + t, seconds[t], whole)
-        planes = weave.tile([P, 2, PAIRS], F32, name="planes_low", offset=28 * KIB, align_bytes=64)
-        for t in range(2):
-            pick_difference(4 + t, planes[:, t, :], seconds[t], whole)
+        seconds = [placed("second_4", PAIRS, GATE_AT[5]), placed("second_5", PAIRS, W2_ROUNDED_AT[0])]
+        differences = work.tile([P, 2, PAIRS], F32, name="differences_low", offset=Z_NATURAL_AT, align_bytes=64)
+        pick_dealt([4, 5], seconds, differences, 0, PAIRS)
         for h, (j0, width) in enumerate(PIECES):
-            round_planes(nc.scalar.copy, h, 0, planes[:, :, j0 : j0 + width])
+            round_differences(nc.scalar.copy, h, 0, differences[:, :, j0 : j0 + width])
 
         features(6)
         features(7)
-        w2_q[1] = quantise("w2_1", w2_rounded, N, GATE_PLACE[7] + 2 * KIB)
-        for h in range(2):
-            for nt in range(N // P):
-                second_stage_pass(h, nt, 0)
+        w2_q[1] = quantise("w2_1", w2_rounded, N, work, GATE_AT[7] + 2 * KIB)
+        open_scores(0)
+        open_scores(1)
+        last = len(PIECES) - 1
         for h, (j0, width) in enumerate(PIECES):
-            cols16 = slice(j0 // 16, (j0 + width) // 16)
-            seconds = [placed("second_%d_%d" % (6 + t, h), width, GATE_PLACE[7] + KIB * t) for t in range(2)]
-            planes = keep.tile([P, 2, width], F32, name="planes_high_%d" % h)
-            for t in range(2):
-                pick_second(6 + t, seconds[t], cols16)
-            for t in range(2):
-                pick_difference(6 + t, planes[:, t, :], seconds[t], cols16)
-            round_planes(nc.vector.tensor_copy, h, 1, planes[:])
+            seconds = [placed("second_%d_%d" % (6 + t, h), width, GATE_AT[7] + KIB * t) for t in range(2)]
+            differences = keep.tile([P, 2, width], F32, name="differences_high_%d" % h)
+            pick_dealt([6, 7], seconds, differences, j0, width)
+            round_differences(nc.vector.tensor_copy, h, 1, differences[:])
             quantise_z_dealt(h)
-            if h == 2:
-                for nt in range(N // P):
-                    second_stage_pass(h, nt, 0)
-            scores(h, 1 if h == 2 else 2)
+            if h == last:
+                open_scores(h)
+            close_scores(h, 1 if h == last else 2)

@@ -25,7 +25,6 @@ BANK = 512
 NATURAL = 4
 SHARED_FROM = 6
 SHARED = 320
-W2_SHARED = 384
 PIECES = [(0, 256), (256, 128), (384, 128)]
 
 TURN_BANK, SUM_BANK, GATE_BANK = 0, 2, 6
@@ -39,7 +38,7 @@ ROUNDED_NATURAL_AT = 0
 Z_NATURAL_AT = 28 * KIB
 WG_DEALT_AT = 37 * KIB
 ROUNDED_DEALT_AT = 40 * KIB
-WINDOW_AT = [76 * KIB, 37 * KIB, 56 * KIB, 48 * KIB, 43 * KIB, 60 * KIB, 43 * KIB, 60 * KIB]
+WINDOW_AT = [76 * KIB, 37 * KIB, 56 * KIB, 84 * KIB, 43 * KIB, 60 * KIB, 43 * KIB, 60 * KIB]
 GATE_AT = {4: 76 * KIB, 5: 80 * KIB, 6: 72 * KIB, 7: 68 * KIB}
 W2_ROUNDED_AT = [47 * KIB, 76 * KIB]
 
@@ -192,8 +191,8 @@ def tile_list_pairwise_document_ranking_kernel(
         def round_w2(b):
             rounded = work.tile([P, N, 4], BF16, name="w2_rounded%d" % b, offset=W2_ROUNDED_AT[b], align_bytes=64)
             if b == 0:
-                gpsimd_round(rounded[:, 0:W2_SHARED, :], w2_raw[b][:, :, 0:W2_SHARED].rearrange("p t n -> p n t"))
-                parts = [slice(W2_SHARED, N)]
+                gpsimd_round(rounded[:], w2_raw[b][:].rearrange("p t n -> p n t"))
+                parts = []
             else:
                 parts = [slice(0, N // 2), slice(N // 2, N)]
             for cols in parts:

@@ -23,24 +23,34 @@ P = 128
 KIB = 1024
 BANK = 512
 NATURAL = 4
-SHARED_FROM = 6
-SHARED = 320
+SHARED = (3, 5, 6, 7)
+GPSIMD_ROUNDS = [(i, 0) for i in range(1, 8)]
 PIECES = [(0, 256), (256, 128), (384, 128)]
 
-TURN_BANK, SUM_BANK, GATE_BANK = 0, 2, 6
+TURN_BANK = 0
+GATE_BANK = [0, 6, 6, 6, 6, 6, 6, 6]
+SUM_BANK = [6, 4, 2, 6, 0, 4, 2, 4]
+SCORE_BANKS = [(6, 7, 2, 3), (4, 5, 0, 1), (6, 7, 2, 3)]
 
 ZEROS_SPAN = 48 * KIB
 TABLE_1_SPAN = 40 * KIB
 TABLE_0_AT = 48 * KIB
 TABLE_SCALES_AT = 64 * KIB
 
-ROUNDED_NATURAL_AT = 0
-Z_NATURAL_AT = 28 * KIB
-WG_DEALT_AT = 37 * KIB
-ROUNDED_DEALT_AT = 40 * KIB
-WINDOW_AT = [76 * KIB, 37 * KIB, 56 * KIB, 84 * KIB, 43 * KIB, 60 * KIB, 43 * KIB, 60 * KIB]
-GATE_AT = {4: 76 * KIB, 5: 80 * KIB, 6: 72 * KIB, 7: 68 * KIB}
-W2_ROUNDED_AT = [47 * KIB, 76 * KIB]
+ROUNDED = {1: (0, 28), 2: (4, 14), 3: (18, 10), 4: (6, 2), 5: (8, 10), 6: (20, 2), 7: (22, 6)}
+WG_DEALT_AT = 2
+GATE_AT = {0: 28, 1: 32, 2: 36, 3: 40, 4: 48, 5: 10, 6: 44, 7: 52}
+CODES_AT = {1: 28, 2: 32, 3: 36, 4: 40, 5: 41, 6: 48, 7: 49}
+FIRST_AT = {3: 6, 4: 20}
+SECOND_AT = {0: 0, 1: 4, 2: 18, 3: 8, 4: 22}
+W2_ROUNDED_AT = [14, 24]
+WIDE_WINDOWS_AT = 56
+WINDOWS_AT = 72
+LAST_SUMS_AT = 88
+SECOND_5 = (92, 8)
+Z_NATURAL_AT = 100
+Z_DEALT_AT = 104
+HIGH = [(98, 4), (102, 1), (104, 1)]
 
 
 def tile_list_pairwise_document_ranking_kernel(
@@ -56,8 +66,13 @@ def tile_list_pairwise_document_ranking_kernel(
         def bank_tile(name, shape, bank):
             return psum.tile(shape, F32, name=name, offset=2 * KIB * bank)
 
-        def placed(name, width, offset):
-            return work.tile([P, width], F32, name=name, offset=offset, align_bytes=64)[:]
+        def placed(name, shape, dtype, kib):
+            return work.tile(shape, dtype, name=name, offset=kib * KIB, align_bytes=64)
+
+        def picks(name, kib):
+            if kib is None:
+                return keep.tile([P, PAIRS], F32, name=name)[:]
+            return placed(name, [P, PAIRS], F32, kib)[:]
 
         offs_t = keep.tile([P, S // 16], U16, name="offs_t")
         pos1_t = keep.tile([P, PAIRS // 16], U16, name="pos1_t")
@@ -103,11 +118,11 @@ def tile_list_pairwise_document_ranking_kernel(
                 cols = w1[512 * a : 512 * (a + 1), first * P : (first + count) * P]
                 nc.sync.dma_start(out=raw[:], in_=cols.rearrange("(p j) c -> p j c", j=4))
                 if first < NATURAL:
-                    w1_raw[(first, a)] = raw[:].rearrange("p j (g i) -> p g j i", i=2)
+                    tiles = raw[:].rearrange("p j (t q e) -> p t j q e", t=count, e=8)
                 else:
-                    dealt = raw[:].rearrange("p j (q t g i) -> p t q g j i", t=4, g=4, i=2)
-                    for t in range(count):
-                        w1_raw[(first + t, a)] = dealt[:, t]
+                    tiles = raw[:].rearrange("p j (q t e) -> p t j q e", t=count, e=8)
+                for t in range(count):
+                    w1_raw[(first + t, a)] = tiles[:, t]
 
         def load_w2(offset):
             natural = loads.tile([P, 4, N], F32, name="w2_raw0", offset=offset, align_bytes=64)
@@ -146,60 +161,50 @@ def tile_list_pairwise_document_ranking_kernel(
         def gpsimd_round(out, in_):
             nc.gpsimd.tensor_scalar(out, in_, 1.0, 0.0, MULT, ADD)
 
-        def rounded_w1_at(i):
-            return ROUNDED_NATURAL_AT + 2 * KIB * i if i < NATURAL else ROUNDED_DEALT_AT + 2 * KIB * (i - NATURAL)
-
-        def round_w1(copy, dst, i, a):
-            if i < NATURAL:
-                view = dst.rearrange("p (g i) j -> p g j i", i=2)
+        def round_w1(dst, i, a):
+            if (i, a) in GPSIMD_ROUNDS:
+                gpsimd_round(dst.rearrange("p (q e) j -> p q e j", e=8), w1_raw[(i, a)].rearrange("p j q e -> p q e j"))
             else:
-                view = dst.rearrange("p (q g i) j -> p q g j i", g=4, i=2)
-            copy(out=view, in_=w1_raw[(i, a)])
+                nc.scalar.copy(
+                    out=dst.rearrange("p (q g i) j -> p q g j i", g=4, i=2),
+                    in_=w1_raw[(i, a)].rearrange("p j q (g i) -> p q g j i", i=2),
+                )
 
+        w1_rounded = {}
         w1_q = {}
 
         def prepare_first_w1():
             early = keep.tile([P, P, 4], BF16, name="w1_rounded_0_0", align_bytes=64)
-            late = loads.tile([P, P, 4], BF16, name="w1_rounded_0_1", offset=TABLE_1_SPAN - 4 * KIB, align_bytes=64)
-            passes = (
-                (early, nc.scalar.copy, loads, TABLE_1_SPAN - 2 * KIB),
-                (late, nc.vector.tensor_copy, work, rounded_w1_at(1)),
-            )
-            for a, (rounded, copy, pool, offset) in enumerate(passes):
-                round_w1(copy, rounded[:], 0, a)
-                codes, scales = quantise("w1_0_%d" % a, rounded[:].rearrange("p c j -> p (c j)"), P, pool, offset)
+            late = placed("w1_rounded_0_1", [P, P, 4], BF16, ROUNDED[1][0])
+            for a, rounded in enumerate((early, late)):
+                round_w1(rounded[:], 0, a)
+                flat = rounded[:].rearrange("p c j -> p (c j)")
+                codes, scales = quantise("w1_0_%d" % a, flat, P, loads, TABLE_1_SPAN - (2 - a) * KIB)
                 w1_q[(0, a)] = (codes[:], scales[:])
 
-        def prepare_w1(i):
-            reach = 4 if i < NATURAL - 1 else 2
-            span = work.tile([P, reach, P, 4], BF16, name="w1_rounded_%d" % i, offset=rounded_w1_at(i), align_bytes=64)
-            rounded = span[:, 0:2, :, :]
-            for a in range(2):
-                if (i, a) == (NATURAL, 0):
-                    gpsimd_round(
-                        rounded[:, a, :, :].rearrange("p (q e) j -> p q e j", e=8),
-                        w1_raw[(i, a)].rearrange("p q g j i -> p q (g i) j"),
-                    )
-                else:
-                    round_w1(nc.scalar.copy, rounded[:, a, :, :], i, a)
-            codes, scales = quantise("w1_%d" % i, rounded.rearrange("p a c j -> p (a c j)"), 2 * P)
+        def round_tile(i, passes=(0, 1)):
+            if i not in w1_rounded:
+                start, span = ROUNDED[i]
+                w1_rounded[i] = placed("w1_rounded_%d" % i, [P, span, P, 4], BF16, start)[:, 0:2, :, :]
+            for a in passes:
+                round_w1(w1_rounded[i][:, a, :, :], i, a)
+
+        def quantise_tile(i):
+            flat = w1_rounded[i].rearrange("p a c j -> p (a c j)")
+            codes, scales = quantise("w1_%d" % i, flat, 2 * P, work, CODES_AT[i] * KIB)
             for a in range(2):
                 w1_q[(i, a)] = (codes[:, P * a : P * (a + 1)], scales[:, P * a : P * (a + 1)])
 
-        w2_q = {}
-
         def round_w2(b):
-            rounded = work.tile([P, N, 4], BF16, name="w2_rounded%d" % b, offset=W2_ROUNDED_AT[b], align_bytes=64)
+            rounded = placed("w2_rounded%d" % b, [P, N, 4], BF16, W2_ROUNDED_AT[b])
+            shared = N if b == 1 else N // 2
+            gpsimd_round(rounded[:, 0:shared, :], w2_raw[b][:, :, 0:shared].rearrange("p t n -> p n t"))
             if b == 0:
-                gpsimd_round(rounded[:], w2_raw[b][:].rearrange("p t n -> p n t"))
-                parts = []
-            else:
-                parts = [slice(0, N // 2), slice(N // 2, N)]
-            for cols in parts:
-                nc.scalar.copy(
-                    out=rounded[:, cols, :].rearrange("p (g i) t -> p g t i", i=2),
-                    in_=w2_raw[b][:, :, cols].rearrange("p t (g i) -> p g t i", i=2),
-                )
+                for cols in (slice(N // 2, 3 * N // 4), slice(3 * N // 4, N)):
+                    nc.scalar.copy(
+                        out=rounded[:, cols, :].rearrange("p (g i) t -> p g t i", i=2),
+                        in_=w2_raw[b][:, :, cols].rearrange("p t (g i) -> p g t i", i=2),
+                    )
             return rounded[:].rearrange("p n t -> p (n t)")
 
         gate_w = {}
@@ -210,28 +215,36 @@ def tile_list_pairwise_document_ranking_kernel(
                     words = wg_first[:, a, :] if i == 0 else wg_rest[:, a, 2 * P * (i - 1) : 2 * P * i]
                     gate_w[(i, a)] = (words, wg_sc[:, a, P * i : P * (i + 1)])
 
-        def deal_wg():
-            words = work.tile([P, 2, 4, 2 * P], U8, name="wg_dealt", offset=WG_DEALT_AT, align_bytes=64)
-            nc.gpsimd.tensor_copy(
-                words[:].bitcast(I32).rearrange("p a t (q w) -> p a t q w", w=4),
-                wg_high[:].bitcast(I32).rearrange("p a (q t w) -> p a t q w", t=4, w=4),
-            )
-            scales = work.tile([P, 2, 4, P], U8, name="wg_sc_dealt", offset=WG_DEALT_AT + 2 * KIB, align_bytes=64)
+        def deal_wg_scales():
+            scales = keep.tile([P, 2, 4, P], U8, name="wg_sc_dealt", align_bytes=64)
             nc.gpsimd.tensor_copy(
                 scales[:].bitcast(I32).rearrange("p a t (q w) -> p a t q w", w=2),
                 wg_sc[:, :, H // 2 : H].bitcast(I32).rearrange("p a (q t w) -> p a t q w", t=4, w=2),
+            )
+            return scales
+
+        def deal_wg_words(scales):
+            words = placed("wg_dealt", [P, 2, 4, 2 * P], U8, WG_DEALT_AT)
+            nc.gpsimd.tensor_copy(
+                words[:].bitcast(I32).rearrange("p a t (q w) -> p a t q w", w=4),
+                wg_high[:].bitcast(I32).rearrange("p a (q t w) -> p a t q w", t=4, w=4),
             )
             for a in range(2):
                 for t in range(4):
                     gate_w[(NATURAL + t, a)] = (words[:, a, t, :], scales[:, a, t, :])
 
-        windows = {}
+        wide = [placed("wide_window_%d" % u, [P, 2 * S], F32, WIDE_WINDOWS_AT + 8 * u) for u in range(2)]
+        for window in wide:
+            nc.vector.memset(window[:, S : 2 * S], 0.0)
+        windows = {i: wide[i % 2] for i in range(NATURAL)}
+        for t in range(4):
+            windows[NATURAL + t] = placed("window_%d" % (NATURAL + t), [P, S], F32, WINDOWS_AT + 4 * t)
         w1_sums = {}
         gates = {}
         shared_sums = {}
 
-        def first_stage_sum(bank, weights, fmt, i, d):
-            for a in range(2):
+        def first_stage_sum(bank, weights, fmt, i, d, passes=(0, 1)):
+            for a in passes:
                 codes, scales = weights[(i, a)]
                 nc.tensor.matmul_mx(
                     out=bank[:],
@@ -243,46 +256,62 @@ def tile_list_pairwise_document_ranking_kernel(
                     stop=(a == 1),
                 )
 
-        def products(i):
-            gate_bank = TURN_BANK if i == 0 else GATE_BANK
-            sum_bank = GATE_BANK if i == 0 else SUM_BANK + 2 * (i % 2)
-            if i < NATURAL:
-                windows[i] = work.tile([P, 2 * S], F32, name="window_%d" % i, offset=WINDOW_AT[i], align_bytes=64)
-            for d in range(2):
-                bank = bank_tile("g_bank_%d_%d" % (i, d), [P, BANK], gate_bank + d)
+        def halves(i):
+            return (1, 0) if i in SHARED else (0, 1)
+
+        def copy_gate(i, d, bank):
+            gates[(i, d)] = placed("gate_%d_%d" % (i, d), [P, BANK], F32, GATE_AT[i] + 2 * d)
+            nc.scalar.copy(out=gates[(i, d)][:], in_=bank[:])
+
+        def gate_sums(i):
+            for d in halves(i):
+                bank = bank_tile("g_bank_%d_%d" % (i, d), [P, BANK], GATE_BANK[i] + d)
                 first_stage_sum(bank, gate_w, FP4X4, i, d)
-                if i < NATURAL:
-                    gates[(i, d)] = windows[i][:, S + BANK * d : S + BANK * (d + 1)]
-                else:
-                    gates[(i, d)] = placed("gate_%d_%d" % (i, d), BANK, GATE_AT[i] + 2 * KIB * d)
-                nc.scalar.copy(out=gates[(i, d)], in_=bank[:])
+                copy_gate(i, d, bank)
+
+        def first_sums():
+            banks = [bank_tile("g_bank_0_%d" % d, [P, BANK], GATE_BANK[0] + d) for d in range(2)]
             for d in range(2):
-                w1_sums[(i, d)] = bank_tile("a_bank_%d_%d" % (i, d), [P, BANK], sum_bank + d)
-                first_stage_sum(w1_sums[(i, d)], w1_q, FP8X4, i, d)
-            if i >= SHARED_FROM:
-                shared_sums[i] = keep.tile([P, SHARED], F32, name="shared_sums_%d" % i)[:]
-                nc.scalar.copy(out=shared_sums[i], in_=w1_sums[(i, 1)][:, BANK - SHARED : BANK])
+                w1_sums[(0, d)] = bank_tile("a_bank_0_%d" % d, [P, BANK], SUM_BANK[0] + d)
+                first_stage_sum(banks[d], gate_w, FP4X4, 0, d, [0])
+            for d in range(2):
+                first_stage_sum(banks[d], gate_w, FP4X4, 0, d, [1])
+                copy_gate(0, d, banks[d])
+            first_stage_sum(w1_sums[(0, 0)], w1_q, FP8X4, 0, 0)
+            first_stage_sum(w1_sums[(0, 1)], w1_q, FP8X4, 0, 1)
 
-        def features(i):
-            if i >= NATURAL:
-                windows[i] = work.tile([P, S], F32, name="window_%d" % i, offset=WINDOW_AT[i], align_bytes=64)
-            own = BANK - SHARED if i >= SHARED_FROM else BANK
-            nc.vector.tensor_tensor(windows[i][:, 0:BANK], w1_sums[(i, 0)][:], gates[(i, 0)], MULT)
-            nc.vector.tensor_tensor(
-                windows[i][:, BANK : BANK + own], w1_sums[(i, 1)][:, 0:own], gates[(i, 1)][:, 0:own], MULT
-            )
-            if i >= SHARED_FROM:
-                nc.gpsimd.tensor_tensor(windows[i][:, BANK + own : S], shared_sums[i], gates[(i, 1)][:, own:BANK], MULT)
+        def weight_sums(i, d):
+            w1_sums[(i, d)] = bank_tile("a_bank_%d_%d" % (i, d), [P, BANK], SUM_BANK[i] + d)
+            first_stage_sum(w1_sums[(i, d)], w1_q, FP8X4, i, d)
+            if d == 1 and i in SHARED:
+                if i == 7:
+                    shared_sums[i] = placed("shared_sums_7", [P, BANK], F32, LAST_SUMS_AT)
+                else:
+                    shared_sums[i] = keep.tile([P, BANK], F32, name="shared_sums_%d" % i)
+                nc.scalar.copy(out=shared_sums[i][:], in_=w1_sums[(i, d)][:])
+
+        def both_weight_sums(i):
+            for d in halves(i):
+                weight_sums(i, d)
+
+        def features(i, d):
+            dst = windows[i][:, BANK * d : BANK * (d + 1)]
+            if d == 1 and i in SHARED:
+                nc.gpsimd.tensor_tensor(dst, shared_sums[i][:], gates[(i, d)][:], MULT)
+            else:
+                nc.vector.tensor_tensor(dst, w1_sums[(i, d)][:], gates[(i, d)][:], MULT)
 
 
-        def pick_natural(tiles, firsts, negated_seconds):
-            for i, dst in zip(tiles, firsts):
-                nc.vector.tensor_copy(dst, windows[i][:, 0:S].indirect(pos1_t[:]))
-            for i, dst in zip(tiles, negated_seconds):
-                nc.vector.tensor_scalar(dst, windows[i][:].indirect(pos2_t[:]), -1.0, 0.0, MULT, ADD)
-            return list(zip(firsts, negated_seconds))
+        picked = {}
 
-        z_turned = keep.tile([P, 4, 2, 2 * P], BF16, name="z_turned", align_bytes=64)
+        def pick_natural(i):
+            first = picks("first_%d" % i, FIRST_AT.get(i))
+            negated_second = picks("second_%d" % i, SECOND_AT.get(i))
+            nc.vector.tensor_copy(first, windows[i][:, 0:S].indirect(pos1_t[:]))
+            nc.vector.tensor_scalar(negated_second, windows[i][:].indirect(pos2_t[:]), -1.0, 0.0, MULT, ADD)
+            picked[i] = (first, negated_second)
+
+        z_turned = placed("z_turned", [P, 4, 2, 2 * P], BF16, Z_DEALT_AT)
 
         def turn(i, first, negated_second):
             bank = bank_tile("zt_bank_%d" % i, [P, 4, P], TURN_BANK + i % 2)
@@ -299,15 +328,15 @@ def tile_list_pairwise_document_ranking_kernel(
 
         def turn_z_back():
             words = z_turned[:].bitcast(F32)
-            rounded = work.tile([P, PAIRS, 4], BF16, name="z_rounded_0", offset=Z_NATURAL_AT, align_bytes=64)[:]
-            rounded_words = rounded.bitcast(F32)
+            rounded = []
             for g in range(2):
+                rounded.append(placed("z_rounded_0_%d" % g, [P, PAIRS // 2, 4], BF16, Z_NATURAL_AT + 2 * g)[:])
                 bank = bank_tile("back_bank_%d" % g, [P, 2, 2, P], TURN_BANK + g)
                 for jb in range(2):
                     for u in range(2):
                         nc.tensor.transpose(bank[:, jb, u, :], words[:, 2 * g + jb, u, :], ident[:])
                 nc.scalar.copy(
-                    out=rounded_words[:, 256 * g : 256 * (g + 1), :].rearrange("p (b j) u -> p b j u", b=2),
+                    out=rounded[g].bitcast(F32).rearrange("p (b j) u -> p b j u", b=2),
                     in_=bank[:].rearrange("p b u j -> p b j u"),
                 )
             return rounded
@@ -315,23 +344,25 @@ def tile_list_pairwise_document_ranking_kernel(
         z_q = {}
 
         def quantise_z_natural(rounded):
-            flat = rounded.rearrange("p j t -> p (j t)")
-            codes, scales = quantise("z_0", flat, PAIRS, work, GATE_AT[5] + 2 * KIB)
-            for h, (j0, width) in enumerate(PIECES):
-                z_q[(0, h)] = (codes[:, j0 : j0 + width], scales[:, j0 : j0 + width])
+            half = PAIRS // 2
+            for g in range(2):
+                flat = rounded[g].rearrange("p j t -> p (j t)")
+                codes, scales = quantise("z_0_%d" % g, flat, half, work, (SECOND_5[0] + g) * KIB)
+                for h, (j0, width) in enumerate(PIECES):
+                    if j0 // half == g:
+                        cols = slice(j0 - half * g, j0 - half * g + width)
+                        z_q[(0, h)] = (codes[:, cols], scales[:, cols])
 
 
         z_dealt = [
-            keep.tile([P, width, 4], BF16, name="z_rounded_1_%d" % h, align_bytes=64)
+            placed("z_rounded_1_%d" % h, [P, width, 4], BF16, Z_DEALT_AT + j0 // P)
             for h, (j0, width) in enumerate(PIECES)
         ]
 
-        def pick_dealt(tiles, seconds, differences, j0, width):
-            entries = slice(j0 // 16, (j0 + width) // 16)
-            for i, second in zip(tiles, seconds):
-                nc.vector.tensor_copy(second, windows[i][:].indirect(pos2_t[:, entries]))
-            for t, (i, second) in enumerate(zip(tiles, seconds)):
-                nc.vector.tensor_tensor(differences[:, t, :], windows[i][:].indirect(pos1_t[:, entries]), second, SUB)
+        def pick_plain(i, first, second):
+            nc.vector.tensor_copy(first, windows[i][:].indirect(pos1_t[:]))
+            nc.vector.tensor_copy(second, windows[i][:].indirect(pos2_t[:]))
+            picked[i] = (first, second)
 
         def round_differences(copy, h, u, differences):
             copy(out=z_dealt[h][:, :, 2 * u : 2 * u + 2], in_=differences.rearrange("p t j -> p j t"))
@@ -357,10 +388,8 @@ def tile_list_pairwise_document_ranking_kernel(
             )
 
         def open_scores(h):
-            free_early = (GATE_BANK, GATE_BANK + 1, TURN_BANK + 1, TURN_BANK)
             for nt in range(N // P):
-                bank = SUM_BANK + nt if h == 1 else free_early[nt]
-                y_banks[(h, nt)] = bank_tile("y_bank_%d_%d" % (h, nt), [P, PIECES[h][1]], bank)
+                y_banks[(h, nt)] = bank_tile("y_bank_%d_%d" % (h, nt), [P, PIECES[h][1]], SCORE_BANKS[h][nt])
                 second_stage_pass(h, nt, 0)
 
         out_view = out.rearrange("(t p) j -> p t j", p=P)
@@ -387,8 +416,7 @@ def tile_list_pairwise_document_ranking_kernel(
         gather_first_pass()
         load_w1(1, 1, TABLE_0_AT)
         wg_rest = load_wg("wg_rest", P, H // 2 - P, TABLE_0_AT + 12 * KIB)
-        load_w1(2, 1, TABLE_0_AT + 4 * KIB)
-        load_w1(3, 1, TABLE_0_AT + 8 * KIB)
+        load_w1(2, 2, TABLE_0_AT + 4 * KIB)
         wg_high = load_wg("wg_high", H // 2, H // 2, TABLE_0_AT + 14 * KIB)
         gather_second_pass()
         load_w1(NATURAL, 4, 0)
@@ -397,69 +425,97 @@ def tile_list_pairwise_document_ranking_kernel(
         with nc.allow_non_contiguous_dma(reason="one bias value for each partition"):
             nc.sync.dma_start(out=c_t[:], in_=c.rearrange("(t p) -> p t", p=P))
 
+        wg_scales_dealt = deal_wg_scales()
         prepare_first_w1()
         name_natural_wg()
-        products(0)
-        prepare_w1(1)
-        products(1)
-        prepare_w1(2)
+        first_sums()
+        round_tile(1)
 
-        features(0)
-        first_0 = keep.tile([P, PAIRS], F32, name="first_0")
-        picked = pick_natural([0], [first_0[:]], [placed("second_0", PAIRS, rounded_w1_at(1))])
-        prepare_w1(3)
-        products(2)
-        features(1)
-        products(3)
-        picked += pick_natural(
-            [1], [placed("first_1", PAIRS, rounded_w1_at(2))], [placed("second_1", PAIRS, rounded_w1_at(3))]
-        )
-        deal_wg()
-        for i in (0, 1):
-            turn(i, *picked[i])
+        for i in range(3):
+            features(i, 0)
+            features(i, 1)
+            quantise_tile(i + 1)
+            if i == 0:
+                gate_sums(1)
+            both_weight_sums(i + 1)
+            if i == 0:
+                round_tile(2)
+                gate_sums(2)
+                round_tile(3)
+                deal_wg_words(wg_scales_dealt)
+                gate_sums(3)
+            if i == 1:
+                round_tile(4, [0])
+                round_tile(5, [0])
+                gate_sums(4)
+            if i == 2:
+                round_tile(6, [0])
+                round_tile(7, [0])
+                features(3, 1)
+                round_tile(4, [1])
+                round_tile(5, [1])
+            pick_natural(i)
 
-        features(2)
-        prepare_w1(4)
-        products(4)
-        features(3)
-        prepare_w1(5)
-        products(5)
-        prepare_w1(6)
-        prepare_w1(7)
-        second_3 = keep.tile([P, PAIRS], F32, name="second_3")
-        picked += pick_natural(
-            [2, 3],
-            [windows[3][:, S : S + PAIRS], placed("first_3", PAIRS, rounded_w1_at(4))],
-            [placed("second_2", PAIRS, rounded_w1_at(5)), second_3[:]],
-        )
-        for i in (2, 3):
+        features(3, 0)
+        quantise_tile(4)
+        quantise_tile(5)
+        gate_sums(5)
+        w2_rounded = {}
+        weight_sums(4, 0)
+        weight_sums(5, 1)
+        weight_sums(4, 1)
+        weight_sums(5, 0)
+        round_tile(6, [1])
+        round_tile(7, [1])
+        w2_rounded[0] = round_w2(0)
+        features(5, 1)
+        gate_sums(6)
+        pick_natural(3)
+
+        features(4, 0)
+        features(4, 1)
+        features(5, 0)
+        quantise_tile(6)
+        quantise_tile(7)
+        w2_rounded[1] = round_w2(1)
+        both_weight_sums(6)
+        features(6, 1)
+        gate_sums(7)
+        both_weight_sums(7)
+        features(7, 1)
+        for i in range(NATURAL):
             turn(i, *picked[i])
         z_natural = turn_z_back()
-        w2_q[0] = quantise("w2_0", round_w2(0), N)
-
-        features(4)
-        products(6)
-        features(5)
-        products(7)
-        quantise_z_natural(z_natural)
-        w2_rounded = round_w2(1)
-        seconds = [placed("second_4", PAIRS, GATE_AT[5]), placed("second_5", PAIRS, W2_ROUNDED_AT[0])]
-        differences = work.tile([P, 2, PAIRS], F32, name="differences_low", offset=Z_NATURAL_AT, align_bytes=64)
-        pick_dealt([4, 5], seconds, differences, 0, PAIRS)
+        pick_plain(4, picks("first_4", FIRST_AT[4]), picks("second_4", SECOND_AT[4]))
+        second_5 = placed("second_5", [P, SECOND_5[1] * KIB // 4], F32, SECOND_5[0])
+        pick_plain(5, picks("first_5", None), second_5[:, 0:PAIRS])
+        low = placed("differences_low", [P, 2, PAIRS], F32, LAST_SUMS_AT)
+        for t in range(2):
+            nc.gpsimd.tensor_tensor(low[:, t, :], *picked[NATURAL + t], SUB)
         for h, (j0, width) in enumerate(PIECES):
-            round_differences(nc.scalar.copy, h, 0, differences[:, :, j0 : j0 + width])
+            round_differences(nc.scalar.copy, h, 0, low[:, :, j0 : j0 + width])
 
-        features(6)
-        features(7)
-        w2_q[1] = quantise("w2_1", w2_rounded, N, work, GATE_AT[7] + 2 * KIB)
+        seconds = {}
+        for i in (6, 7):
+            features(i, 0)
+        for i in (6, 7):
+            seconds[i] = picks("second_%d" % i, None)
+            nc.vector.tensor_copy(seconds[i], windows[i][:].indirect(pos2_t[:]))
+        w2_q = {}
+        for b in range(2):
+            w2_q[b] = quantise("w2_%d" % b, w2_rounded[b], N, work, (SECOND_5[0] + 2 + 2 * b) * KIB)
+        quantise_z_natural(z_natural)
         open_scores(0)
         open_scores(1)
         last = len(PIECES) - 1
         for h, (j0, width) in enumerate(PIECES):
-            seconds = [placed("second_%d_%d" % (6 + t, h), width, GATE_AT[7] + KIB * t) for t in range(2)]
-            differences = keep.tile([P, 2, width], F32, name="differences_high_%d" % h)
-            pick_dealt([6, 7], seconds, differences, j0, width)
-            round_differences(nc.vector.tensor_copy, h, 1, differences[:])
+            start, span = HIGH[h]
+            high = placed("differences_high_%d" % h, [P, span * KIB // (4 * width), width], F32, start)[:, 0:2, :]
+            entries = slice(j0 // 16, (j0 + width) // 16)
+            for t, i in enumerate((6, 7)):
+                firsts = windows[i][:].indirect(pos1_t[:, entries])
+                nc.vector.tensor_tensor(high[:, t, :], firsts, seconds[i][:, j0 : j0 + width], SUB)
+            round_differences(nc.vector.tensor_copy, h, 1, high)
             quantise_z_dealt(h)
             if h == last:
                 open_scores(h)

@@ -23,34 +23,37 @@ P = 128
 KIB = 1024
 BANK = 512
 NATURAL = 4
-SHARED = (3, 5, 6, 7)
-GPSIMD_ROUNDS = [(i, 0) for i in range(1, 8)]
+SHARED = (5, 6, 7)
+GPSIMD_ROUNDS = [(1, 0), (2, 0), (6, 0), (4, 1), (5, 1)]
+W2_SHARED = [128, 384]
+WARM_UPS = 4
 PIECES = [(0, 256), (256, 128), (384, 128)]
 
 TURN_BANK = 0
-GATE_BANK = [0, 6, 6, 6, 6, 6, 6, 6]
-SUM_BANK = [6, 4, 2, 6, 0, 4, 2, 4]
-SCORE_BANKS = [(6, 7, 2, 3), (4, 5, 0, 1), (6, 7, 2, 3)]
+GATE_BANK = [0, 6, 6, 6, 6, 0, 6, 6]
+SUM_BANK = [6, 4, 2, 4, 0, 2, 4, 2]
+SCORE_BANKS = [(6, 7, 4, 5), (2, 3, 0, 1), (6, 7, 4, 5)]
 
 ZEROS_SPAN = 48 * KIB
 TABLE_1_SPAN = 40 * KIB
 TABLE_0_AT = 48 * KIB
 TABLE_SCALES_AT = 64 * KIB
 
-ROUNDED = {1: (0, 28), 2: (4, 14), 3: (18, 10), 4: (6, 2), 5: (8, 10), 6: (20, 2), 7: (22, 6)}
+ROUNDED = {1: (0, 28), 2: (4, 10), 3: (14, 14), 4: (16, 2), 5: (18, 10), 6: (6, 2), 7: (8, 6)}
 WG_DEALT_AT = 2
-GATE_AT = {0: 28, 1: 32, 2: 36, 3: 40, 4: 48, 5: 10, 6: 44, 7: 52}
+GATE_AT = {0: 28, 1: 32, 2: 36, 3: 40, 4: 48, 5: 44, 6: 20, 7: 52}
 CODES_AT = {1: 28, 2: 32, 3: 36, 4: 40, 5: 41, 6: 48, 7: 49}
-FIRST_AT = {3: 6, 4: 20}
-SECOND_AT = {0: 0, 1: 4, 2: 18, 3: 8, 4: 22}
-W2_ROUNDED_AT = [14, 24]
+FIRST_AT = {3: 16, 4: 6}
+SECOND_AT = {0: 0, 1: 4, 2: 14, 3: 18, 4: 8}
+W2_ROUNDED_AT = [24, 10]
 WIDE_WINDOWS_AT = 56
 WINDOWS_AT = 72
 LAST_SUMS_AT = 88
 SECOND_5 = (92, 8)
 Z_NATURAL_AT = 100
-Z_DEALT_AT = 104
-HIGH = [(98, 4), (102, 1), (104, 1)]
+Z_DEALT_AT = 105
+HIGH = [(98, 4), (102, 1), (110, 1)]
+LAST_SECONDS = [[(109, 1), (104, 1)], [(109, 1), (104, 1)], [(109, 1), (104, 2)]]
 
 
 def tile_list_pairwise_document_ranking_kernel(
@@ -197,14 +200,17 @@ def tile_list_pairwise_document_ranking_kernel(
 
         def round_w2(b):
             rounded = placed("w2_rounded%d" % b, [P, N, 4], BF16, W2_ROUNDED_AT[b])
-            shared = N if b == 1 else N // 2
+            shared = W2_SHARED[b]
             gpsimd_round(rounded[:, 0:shared, :], w2_raw[b][:, :, 0:shared].rearrange("p t n -> p n t"))
-            if b == 0:
-                for cols in (slice(N // 2, 3 * N // 4), slice(3 * N // 4, N)):
-                    nc.scalar.copy(
-                        out=rounded[:, cols, :].rearrange("p (g i) t -> p g t i", i=2),
-                        in_=w2_raw[b][:, :, cols].rearrange("p t (g i) -> p g t i", i=2),
-                    )
+            return rounded
+
+        def finish_w2(b, rounded):
+            for first in range(W2_SHARED[b], N, P):
+                cols = slice(first, first + P)
+                nc.scalar.copy(
+                    out=rounded[:, cols, :].rearrange("p (g i) t -> p g t i", i=2),
+                    in_=w2_raw[b][:, :, cols].rearrange("p t (g i) -> p g t i", i=2),
+                )
             return rounded[:].rearrange("p n t -> p (n t)")
 
         gate_w = {}
@@ -227,7 +233,7 @@ def tile_list_pairwise_document_ranking_kernel(
             words = placed("wg_dealt", [P, 2, 4, 2 * P], U8, WG_DEALT_AT)
             nc.gpsimd.tensor_copy(
                 words[:].bitcast(I32).rearrange("p a t (q w) -> p a t q w", w=4),
-                wg_high[:].bitcast(I32).rearrange("p a (q t w) -> p a t q w", t=4, w=4),
+                wg_rest[:, :, H - 2 * P : 2 * H - 2 * P].bitcast(I32).rearrange("p a (q t w) -> p a t q w", t=4, w=4),
             )
             for a in range(2):
                 for t in range(4):
@@ -268,6 +274,15 @@ def tile_list_pairwise_document_ranking_kernel(
                 bank = bank_tile("g_bank_%d_%d" % (i, d), [P, BANK], GATE_BANK[i] + d)
                 first_stage_sum(bank, gate_w, FP4X4, i, d)
                 copy_gate(i, d, bank)
+
+        def warm_up():
+            words = v_words[(0, 0)]
+            for k in range(WARM_UPS):
+                unread = bank_tile("warm_up_%d" % k, [P, BANK], SUM_BANK[2] + k % 2)
+                nc.tensor.matmul_mx(
+                    out=unread[:], lhsT=words[:, 0:P].bitcast(FP8X4), lhsT_scale=v_sc[0][:, 0:P],
+                    rhs=words.bitcast(FP8X4), rhs_scale=v_sc[0][:, 0:BANK], start=True, stop=True,
+                )
 
         def first_sums():
             banks = [bank_tile("g_bank_0_%d" % d, [P, BANK], GATE_BANK[0] + d) for d in range(2)]
@@ -415,9 +430,8 @@ def tile_list_pairwise_document_ranking_kernel(
         gather_scales()
         gather_first_pass()
         load_w1(1, 1, TABLE_0_AT)
-        wg_rest = load_wg("wg_rest", P, H // 2 - P, TABLE_0_AT + 12 * KIB)
+        wg_rest = load_wg("wg_rest", P, H - P, TABLE_0_AT + 12 * KIB)
         load_w1(2, 2, TABLE_0_AT + 4 * KIB)
-        wg_high = load_wg("wg_high", H // 2, H // 2, TABLE_0_AT + 14 * KIB)
         gather_second_pass()
         load_w1(NATURAL, 4, 0)
         w2_raw = load_w2(16 * KIB)
@@ -439,37 +453,37 @@ def tile_list_pairwise_document_ranking_kernel(
                 gate_sums(1)
             both_weight_sums(i + 1)
             if i == 0:
+                deal_wg_words(wg_scales_dealt)
                 round_tile(2)
                 gate_sums(2)
                 round_tile(3)
-                deal_wg_words(wg_scales_dealt)
                 gate_sums(3)
             if i == 1:
-                round_tile(4, [0])
-                round_tile(5, [0])
                 gate_sums(4)
-            if i == 2:
+                gate_sums(5)
                 round_tile(6, [0])
                 round_tile(7, [0])
-                features(3, 1)
-                round_tile(4, [1])
-                round_tile(5, [1])
+            if i == 2:
+                round_tile(4)
+                round_tile(5)
             pick_natural(i)
+        for i in (0, 1):
+            turn(i, *picked[i])
 
         features(3, 0)
+        features(3, 1)
         quantise_tile(4)
         quantise_tile(5)
-        gate_sums(5)
-        w2_rounded = {}
+        w2_begun = {0: round_w2(0)}
         weight_sums(4, 0)
         weight_sums(5, 1)
         weight_sums(4, 1)
         weight_sums(5, 0)
         round_tile(6, [1])
         round_tile(7, [1])
-        w2_rounded[0] = round_w2(0)
         features(5, 1)
         gate_sums(6)
+        w2_rounded = {0: finish_w2(0, w2_begun[0])}
         pick_natural(3)
 
         features(4, 0)
@@ -477,15 +491,16 @@ def tile_list_pairwise_document_ranking_kernel(
         features(5, 0)
         quantise_tile(6)
         quantise_tile(7)
-        w2_rounded[1] = round_w2(1)
+        w2_begun[1] = round_w2(1)
+        gate_sums(7)
         both_weight_sums(6)
         features(6, 1)
-        gate_sums(7)
         both_weight_sums(7)
         features(7, 1)
-        for i in range(NATURAL):
+        for i in (2, 3):
             turn(i, *picked[i])
         z_natural = turn_z_back()
+        w2_rounded[1] = finish_w2(1, w2_begun[1])
         pick_plain(4, picks("first_4", FIRST_AT[4]), picks("second_4", SECOND_AT[4]))
         second_5 = placed("second_5", [P, SECOND_5[1] * KIB // 4], F32, SECOND_5[0])
         pick_plain(5, picks("first_5", None), second_5[:, 0:PAIRS])
@@ -495,12 +510,20 @@ def tile_list_pairwise_document_ranking_kernel(
         for h, (j0, width) in enumerate(PIECES):
             round_differences(nc.scalar.copy, h, 0, low[:, :, j0 : j0 + width])
 
-        seconds = {}
+        def pick_seconds(h):
+            j0, width = PIECES[h]
+            entries = slice(j0 // 16, (j0 + width) // 16)
+            seconds = []
+            for t, i in enumerate((6, 7)):
+                start, span = LAST_SECONDS[h][t]
+                tile = placed("second_%d_%d" % (i, h), [P, span * KIB // 4], F32, start)
+                seconds.append(tile[:, 0:width])
+                nc.vector.tensor_copy(seconds[t], windows[i][:].indirect(pos2_t[:, entries]))
+            return seconds
+
         for i in (6, 7):
             features(i, 0)
-        for i in (6, 7):
-            seconds[i] = picks("second_%d" % i, None)
-            nc.vector.tensor_copy(seconds[i], windows[i][:].indirect(pos2_t[:]))
+        seconds = pick_seconds(0)
         w2_q = {}
         for b in range(2):
             w2_q[b] = quantise("w2_%d" % b, w2_rounded[b], N, work, (SECOND_5[0] + 2 + 2 * b) * KIB)
@@ -509,13 +532,15 @@ def tile_list_pairwise_document_ranking_kernel(
         open_scores(1)
         last = len(PIECES) - 1
         for h, (j0, width) in enumerate(PIECES):
+            if h > 0:
+                seconds = pick_seconds(h)
             start, span = HIGH[h]
             high = placed("differences_high_%d" % h, [P, span * KIB // (4 * width), width], F32, start)[:, 0:2, :]
             entries = slice(j0 // 16, (j0 + width) // 16)
             for t, i in enumerate((6, 7)):
                 firsts = windows[i][:].indirect(pos1_t[:, entries])
-                nc.vector.tensor_tensor(high[:, t, :], firsts, seconds[i][:, j0 : j0 + width], SUB)
-            round_differences(nc.vector.tensor_copy, h, 1, high)
+                nc.vector.tensor_tensor(high[:, t, :], firsts, seconds[t], SUB)
+            round_differences(nc.vector.tensor_copy if h == last else nc.scalar.copy, h, 1, high)
             quantise_z_dealt(h)
             if h == last:
                 open_scores(h)

@@ -24,9 +24,8 @@ KIB = 1024
 BANK = 512
 NATURAL = 4
 SHARED = (5, 6, 7)
-GPSIMD_ROUNDS = [(1, 0), (2, 0), (6, 0), (4, 1), (5, 1)]
+GPSIMD_ROUNDS = [(1, 0), (2, 0), (6, 0), (5, 0), (5, 1)]
 W2_SHARED = [128, 384]
-WARM_UPS = 4
 PIECES = [(0, 256), (256, 128), (384, 128)]
 
 TURN_BANK = 0
@@ -274,15 +273,6 @@ def tile_list_pairwise_document_ranking_kernel(
                 bank = bank_tile("g_bank_%d_%d" % (i, d), [P, BANK], GATE_BANK[i] + d)
                 first_stage_sum(bank, gate_w, FP4X4, i, d)
                 copy_gate(i, d, bank)
-
-        def warm_up():
-            words = v_words[(0, 0)]
-            for k in range(WARM_UPS):
-                unread = bank_tile("warm_up_%d" % k, [P, BANK], SUM_BANK[2] + k % 2)
-                nc.tensor.matmul_mx(
-                    out=unread[:], lhsT=words[:, 0:P].bitcast(FP8X4), lhsT_scale=v_sc[0][:, 0:P],
-                    rhs=words.bitcast(FP8X4), rhs_scale=v_sc[0][:, 0:BANK], start=True, stop=True,
-                )
 
         def first_sums():
             banks = [bank_tile("g_bank_0_%d" % d, [P, BANK], GATE_BANK[0] + d) for d in range(2)]

@@ -23,9 +23,9 @@ P = 128
 KIB = 1024
 BANK = 512
 NATURAL = 4
-SHARED = (5, 6, 7)
+SHARED = (5, 6)
 GPSIMD_ROUNDS = [(1, 0), (2, 0), (6, 0), (5, 0), (5, 1)]
-W2_SHARED = [128, 384]
+W2_SHARED = [256, 384]
 PIECES = [(0, 256), (256, 128), (384, 128)]
 
 TURN_BANK = 0
@@ -289,8 +289,8 @@ def tile_list_pairwise_document_ranking_kernel(
             w1_sums[(i, d)] = bank_tile("a_bank_%d_%d" % (i, d), [P, BANK], SUM_BANK[i] + d)
             first_stage_sum(w1_sums[(i, d)], w1_q, FP8X4, i, d)
             if d == 1 and i in SHARED:
-                if i == 7:
-                    shared_sums[i] = placed("shared_sums_7", [P, BANK], F32, LAST_SUMS_AT)
+                if i == SHARED[-1]:
+                    shared_sums[i] = placed("shared_sums_last", [P, BANK], F32, LAST_SUMS_AT)
                 else:
                     shared_sums[i] = keep.tile([P, BANK], F32, name="shared_sums_%d" % i)
                 nc.scalar.copy(out=shared_sums[i][:], in_=w1_sums[(i, d)][:])
@@ -486,7 +486,6 @@ def tile_list_pairwise_document_ranking_kernel(
         both_weight_sums(6)
         features(6, 1)
         both_weight_sums(7)
-        features(7, 1)
         for i in (2, 3):
             turn(i, *picked[i])
         z_natural = turn_z_back()
@@ -511,8 +510,9 @@ def tile_list_pairwise_document_ranking_kernel(
                 nc.vector.tensor_copy(seconds[t], windows[i][:].indirect(pos2_t[:, entries]))
             return seconds
 
-        for i in (6, 7):
-            features(i, 0)
+        features(6, 0)
+        features(7, 0)
+        features(7, 1)
         seconds = pick_seconds(0)
         w2_q = {}
         for b in range(2):

@@ -165,7 +165,8 @@ def tile_list_pairwise_document_ranking_kernel(
 
         def round_w1(dst, i, a):
             if (i, a) in GPSIMD_ROUNDS:
-                gpsimd_round(dst.rearrange("p (q e) j -> p q e j", e=8), w1_raw[(i, a)].rearrange("p j q e -> p q e j"))
+                raw = w1_raw[(i, a)].rearrange("p j q e -> p q e j")
+                gpsimd_round(dst.rearrange("p (q e) j -> p q e j", e=8), raw)
             else:
                 nc.scalar.copy(
                     out=dst.rearrange("p (q g i) j -> p q g j i", g=4, i=2),
@@ -197,7 +198,7 @@ def tile_list_pairwise_document_ranking_kernel(
             for a in range(2):
                 w1_q[(i, a)] = (codes[:, P * a : P * (a + 1)], scales[:, P * a : P * (a + 1)])
 
-        def round_w2(b):
+        def begin_w2(b):
             rounded = placed("w2_rounded%d" % b, [P, N, 4], BF16, W2_ROUNDED_AT[b])
             shared = W2_SHARED[b]
             gpsimd_round(rounded[:, 0:shared, :], w2_raw[b][:, :, 0:shared].rearrange("p t n -> p n t"))
@@ -232,7 +233,7 @@ def tile_list_pairwise_document_ranking_kernel(
             words = placed("wg_dealt", [P, 2, 4, 2 * P], U8, WG_DEALT_AT)
             nc.gpsimd.tensor_copy(
                 words[:].bitcast(I32).rearrange("p a t (q w) -> p a t q w", w=4),
-                wg_rest[:, :, H - 2 * P : 2 * H - 2 * P].bitcast(I32).rearrange("p a (q t w) -> p a t q w", t=4, w=4),
+                wg_high[:].bitcast(I32).rearrange("p a (q t w) -> p a t q w", t=4, w=4),
             )
             for a in range(2):
                 for t in range(4):
@@ -420,8 +421,10 @@ def tile_list_pairwise_document_ranking_kernel(
         gather_scales()
         gather_first_pass()
         load_w1(1, 1, TABLE_0_AT)
-        wg_rest = load_wg("wg_rest", P, H - P, TABLE_0_AT + 12 * KIB)
-        load_w1(2, 2, TABLE_0_AT + 4 * KIB)
+        wg_rest = load_wg("wg_rest", P, H // 2 - P, TABLE_0_AT + 12 * KIB)
+        load_w1(2, 1, TABLE_0_AT + 4 * KIB)
+        wg_high = load_wg("wg_high", H // 2, H // 2, TABLE_0_AT + 14 * KIB)
+        load_w1(3, 1, TABLE_0_AT + 8 * KIB)
         gather_second_pass()
         load_w1(NATURAL, 4, 0)
         w2_raw = load_w2(16 * KIB)
@@ -443,8 +446,8 @@ def tile_list_pairwise_document_ranking_kernel(
                 gate_sums(1)
             both_weight_sums(i + 1)
             if i == 0:
-                deal_wg_words(wg_scales_dealt)
                 round_tile(2)
+                deal_wg_words(wg_scales_dealt)
                 gate_sums(2)
                 round_tile(3)
                 gate_sums(3)
@@ -464,7 +467,7 @@ def tile_list_pairwise_document_ranking_kernel(
         features(3, 1)
         quantise_tile(4)
         quantise_tile(5)
-        w2_begun = {0: round_w2(0)}
+        w2_begun = {0: begin_w2(0)}
         weight_sums(4, 0)
         weight_sums(5, 1)
         weight_sums(4, 1)
@@ -481,7 +484,7 @@ def tile_list_pairwise_document_ranking_kernel(
         features(5, 0)
         quantise_tile(6)
         quantise_tile(7)
-        w2_begun[1] = round_w2(1)
+        w2_begun[1] = begin_w2(1)
         gate_sums(7)
         both_weight_sums(6)
         features(6, 1)

@@ -419,6 +419,8 @@ def tile_list_pairwise_document_ranking_kernel(
         wg_first = load_wg("wg_first", 0, P, TABLE_1_SPAN)
         load_w1(0, 1, TABLE_1_SPAN + 4 * KIB)
         gather_scales()
+        warm = keep.tile([P, 8], F32, name="warm")
+        nc.scalar.activation(warm[:, 0:1], ident[:, 0:1], SIGMOID)
         gather_first_pass()
         load_w1(1, 1, TABLE_0_AT)
         wg_rest = load_wg("wg_rest", P, H // 2 - P, TABLE_0_AT + 12 * KIB)

@@ -35,6 +35,8 @@ SCORE_BANKS = [(6, 7, 4, 5), (2, 3, 0, 1), (6, 7, 4, 5)]
 
 ZEROS_SPAN = 48 * KIB
 TABLE_1_SPAN = 40 * KIB
+FIRST_W1_AT = TABLE_1_SPAN + KIB
+FIRST_GATE_AT = FIRST_W1_AT + 2 * KIB
 TABLE_0_AT = 48 * KIB
 TABLE_SCALES_AT = 64 * KIB
 
@@ -113,16 +115,17 @@ def tile_list_pairwise_document_ranking_kernel(
 
         def load_w1(first, count, offset):
             for a in range(2):
+                rows = 8 if (first, a) == (0, 1) else 4
                 raw = loads.tile(
-                    [P, 4, count * P], F32, name="w1_raw_%d_%d" % (first, a),
+                    [P, rows, count * P], F32, name="w1_raw_%d_%d" % (first, a),
                     offset=offset + a * count * 2 * KIB, align_bytes=64,
-                )
+                )[:, 0:4, :]
                 cols = w1[512 * a : 512 * (a + 1), first * P : (first + count) * P]
-                nc.sync.dma_start(out=raw[:], in_=cols.rearrange("(p j) c -> p j c", j=4))
+                nc.sync.dma_start(out=raw, in_=cols.rearrange("(p j) c -> p j c", j=4))
                 if first < NATURAL:
-                    tiles = raw[:].rearrange("p j (t q e) -> p t j q e", t=count, e=8)
+                    tiles = raw.rearrange("p j (t q e) -> p t j q e", t=count, e=8)
                 else:
-                    tiles = raw[:].rearrange("p j (q t e) -> p t j q e", t=count, e=8)
+                    tiles = raw.rearrange("p j (q t e) -> p t j q e", t=count, e=8)
                 for t in range(count):
                     w1_raw[(first + t, a)] = tiles[:, t]
 
@@ -194,7 +197,10 @@ def tile_list_pairwise_document_ranking_kernel(
 
         def quantise_tile(i):
             flat = w1_rounded[i].rearrange("p a c j -> p (a c j)")
-            codes, scales = quantise("w1_%d" % i, flat, 2 * P, work, CODES_AT[i] * KIB)
+            if i == 1:
+                codes, scales = quantise("w1_1", flat, 2 * P, loads, FIRST_GATE_AT)
+            else:
+                codes, scales = quantise("w1_%d" % i, flat, 2 * P, work, CODES_AT[i] * KIB)
             for a in range(2):
                 w1_q[(i, a)] = (codes[:, P * a : P * (a + 1)], scales[:, P * a : P * (a + 1)])
 
@@ -266,7 +272,11 @@ def tile_list_pairwise_document_ranking_kernel(
             return (1, 0) if i in SHARED else (0, 1)
 
         def copy_gate(i, d, bank):
-            gates[(i, d)] = placed("gate_%d_%d" % (i, d), [P, BANK], F32, GATE_AT[i] + 2 * d)
+            if i == 0:
+                offset = FIRST_GATE_AT + 2 * KIB * d
+                gates[(i, d)] = loads.tile([P, BANK], F32, name="gate_0_%d" % d, offset=offset, align_bytes=64)
+            else:
+                gates[(i, d)] = placed("gate_%d_%d" % (i, d), [P, BANK], F32, GATE_AT[i] + 2 * d)
             nc.scalar.copy(out=gates[(i, d)][:], in_=bank[:])
 
         def gate_sums(i):
@@ -417,7 +427,7 @@ def tile_list_pairwise_document_ranking_kernel(
         tab.append(loads.tile([P, TABLE_1_SPAN // 4], I32, name="tab1", offset=0, align_bytes=64))
         load_table(1)
         wg_first = load_wg("wg_first", 0, P, TABLE_1_SPAN)
-        load_w1(0, 1, TABLE_1_SPAN + 4 * KIB)
+        load_w1(0, 1, FIRST_W1_AT)
         gather_scales()
         warm = keep.tile([P, 8], F32, name="warm")
         nc.scalar.activation(warm[:, 0:1], ident[:, 0:1], SIGMOID)

@@ -24,14 +24,14 @@ KIB = 1024
 BANK = 512
 NATURAL = 4
 SHARED = (5, 6)
-GPSIMD_ROUNDS = [(1, 0), (2, 0), (6, 0), (5, 0), (5, 1)]
-W2_SHARED = [256, 384]
+GPSIMD_ROUNDS = [(1, 0), (2, 0), (6, 0), (5, 0), (5, 1), (7, 0)]
+W2_SHARED = [0, 384]
 PIECES = [(0, 256), (256, 128), (384, 128)]
 
 TURN_BANK = 0
-GATE_BANK = [0, 6, 6, 6, 6, 0, 6, 6]
-SUM_BANK = [6, 4, 2, 4, 0, 2, 4, 2]
-SCORE_BANKS = [(6, 7, 4, 5), (2, 3, 0, 1), (6, 7, 4, 5)]
+GATE_BANK = [(0, 1), (6, 7), (6, 7), (6, 7), (6, 7), (0, 1), (6, 7), (5, 7)]
+SUM_BANK = [(6, 7), (4, 5), (2, 3), (4, 5), (1, 5), (2, 0), (4, 5), (2, 3)]
+SCORE_BANKS = [(6, 7), (4, 5), (2, 3, 0, 1)]
 
 ZEROS_SPAN = 48 * KIB
 TABLE_1_SPAN = 40 * KIB
@@ -40,13 +40,13 @@ FIRST_GATE_AT = FIRST_W1_AT + 2 * KIB
 TABLE_0_AT = 48 * KIB
 TABLE_SCALES_AT = 64 * KIB
 
-ROUNDED = {1: (0, 28), 2: (4, 10), 3: (14, 14), 4: (16, 2), 5: (18, 10), 6: (6, 2), 7: (8, 6)}
+ROUNDED = {1: (0, 28), 2: (4, 10), 3: (14, 14), 4: (16, 2), 5: (18, 12), 6: (6, 6), 7: (20, 6)}
 WG_DEALT_AT = 2
-GATE_AT = {0: 28, 1: 32, 2: 36, 3: 40, 4: 48, 5: 44, 6: 20, 7: 52}
-CODES_AT = {1: 28, 2: 32, 3: 36, 4: 40, 5: 41, 6: 48, 7: 49}
+GATE_AT = {1: 32, 2: 36, 3: 40, 4: 48, 5: 44, 6: 26, 7: 52}
+CODES_AT = {2: 32, 3: 36, 4: 40, 5: 41, 6: 48, 7: 49}
 FIRST_AT = {3: 16, 4: 6}
-SECOND_AT = {0: 0, 1: 4, 2: 14, 3: 18, 4: 8}
-W2_ROUNDED_AT = [24, 10]
+SECOND_AT = {0: 0, 1: 4, 2: 14, 3: 18, 4: 20}
+W2_ROUNDED_AT = [8, 22]
 WIDE_WINDOWS_AT = 56
 WINDOWS_AT = 72
 LAST_SUMS_AT = 88
@@ -207,7 +207,8 @@ def tile_list_pairwise_document_ranking_kernel(
         def begin_w2(b):
             rounded = placed("w2_rounded%d" % b, [P, N, 4], BF16, W2_ROUNDED_AT[b])
             shared = W2_SHARED[b]
-            gpsimd_round(rounded[:, 0:shared, :], w2_raw[b][:, :, 0:shared].rearrange("p t n -> p n t"))
+            if shared:
+                gpsimd_round(rounded[:, 0:shared, :], w2_raw[b][:, :, 0:shared].rearrange("p t n -> p n t"))
             return rounded
 
         def finish_w2(b, rounded):
@@ -281,14 +282,14 @@ def tile_list_pairwise_document_ranking_kernel(
 
         def gate_sums(i):
             for d in halves(i):
-                bank = bank_tile("g_bank_%d_%d" % (i, d), [P, BANK], GATE_BANK[i] + d)
+                bank = bank_tile("g_bank_%d_%d" % (i, d), [P, BANK], GATE_BANK[i][d])
                 first_stage_sum(bank, gate_w, FP4X4, i, d)
                 copy_gate(i, d, bank)
 
         def first_sums():
-            banks = [bank_tile("g_bank_0_%d" % d, [P, BANK], GATE_BANK[0] + d) for d in range(2)]
+            banks = [bank_tile("g_bank_0_%d" % d, [P, BANK], GATE_BANK[0][d]) for d in range(2)]
             for d in range(2):
-                w1_sums[(0, d)] = bank_tile("a_bank_0_%d" % d, [P, BANK], SUM_BANK[0] + d)
+                w1_sums[(0, d)] = bank_tile("a_bank_0_%d" % d, [P, BANK], SUM_BANK[0][d])
                 first_stage_sum(banks[d], gate_w, FP4X4, 0, d, [0])
             for d in range(2):
                 first_stage_sum(banks[d], gate_w, FP4X4, 0, d, [1])
@@ -297,7 +298,7 @@ def tile_list_pairwise_document_ranking_kernel(
             first_stage_sum(w1_sums[(0, 1)], w1_q, FP8X4, 0, 1)
 
         def weight_sums(i, d):
-            w1_sums[(i, d)] = bank_tile("a_bank_%d_%d" % (i, d), [P, BANK], SUM_BANK[i] + d)
+            w1_sums[(i, d)] = bank_tile("a_bank_%d_%d" % (i, d), [P, BANK], SUM_BANK[i][d])
             first_stage_sum(w1_sums[(i, d)], w1_q, FP8X4, i, d)
             if d == 1 and i in SHARED:
                 if i == SHARED[-1]:
@@ -393,20 +394,24 @@ def tile_list_pairwise_document_ranking_kernel(
         def second_stage_pass(h, nt, b):
             w_codes, w_scales = w2_q[b]
             z_codes, z_scales = z_q[(b, h)]
+            shared = N // P // len(SCORE_BANKS[h])
             nc.tensor.matmul_mx(
-                out=y_banks[(h, nt)][:],
+                out=y_banks[(h, nt)],
                 lhsT=w_codes[:, P * nt : P * (nt + 1)].bitcast(FP8X4),
                 lhsT_scale=w_scales[:, P * nt : P * (nt + 1)],
                 rhs=z_codes.bitcast(FP8X4),
                 rhs_scale=z_scales,
-                start=(b == 0),
-                stop=(b == 1),
+                start=(b == 0 and nt % shared == 0),
+                stop=(b == 1 and nt % shared == shared - 1),
             )
 
         def open_scores(h):
-            for nt in range(N // P):
-                y_banks[(h, nt)] = bank_tile("y_bank_%d_%d" % (h, nt), [P, PIECES[h][1]], SCORE_BANKS[h][nt])
-                second_stage_pass(h, nt, 0)
+            shared = N // P // len(SCORE_BANKS[h])
+            for k, bank in enumerate(SCORE_BANKS[h]):
+                sums = bank_tile("y_bank_%d_%d" % (h, k), [P, shared, PIECES[h][1]], bank)
+                for u in range(shared):
+                    y_banks[(h, shared * k + u)] = sums[:, u, :]
+                    second_stage_pass(h, shared * k + u, 0)
 
         out_view = out.rearrange("(t p) j -> p t j", p=P)
 
@@ -415,9 +420,10 @@ def tile_list_pairwise_document_ranking_kernel(
             for first in range(0, N // P, group):
                 result = keep.tile([P, group, width], F32, name="result_%d_%d" % (h, first))
                 for k in range(group):
+                    second_stage_pass(h, first + k, 1)
+                for k in range(group):
                     nt = first + k
-                    second_stage_pass(h, nt, 1)
-                    nc.scalar.activation(result[:, k, :], y_banks[(h, nt)][:], SIGMOID, bias=c_t[:, nt : nt + 1])
+                    nc.scalar.activation(result[:, k, :], y_banks[(h, nt)], SIGMOID, bias=c_t[:, nt : nt + 1])
                 nc.sync.dma_start(out=out_view[:, first : first + group, j0 : j0 + width], in_=result[:])
 
         nc.sync.dma_start(offs_t[:], offs)
@@ -467,10 +473,10 @@ def tile_list_pairwise_document_ranking_kernel(
                 gate_sums(4)
                 gate_sums(5)
                 round_tile(6, [0])
-                round_tile(7, [0])
             if i == 2:
                 round_tile(4)
                 round_tile(5)
+                round_tile(6, [1])
             pick_natural(i)
         for i in (0, 1):
             turn(i, *picked[i])
@@ -479,16 +485,14 @@ def tile_list_pairwise_document_ranking_kernel(
         features(3, 1)
         quantise_tile(4)
         quantise_tile(5)
-        w2_begun = {0: begin_w2(0)}
         weight_sums(4, 0)
         weight_sums(5, 1)
         weight_sums(4, 1)
         weight_sums(5, 0)
-        round_tile(6, [1])
-        round_tile(7, [1])
+        round_tile(7)
         features(5, 1)
         gate_sums(6)
-        w2_rounded = {0: finish_w2(0, w2_begun[0])}
+        turn(2, *picked[2])
         pick_natural(3)
 
         features(4, 0)
@@ -496,15 +500,14 @@ def tile_list_pairwise_document_ranking_kernel(
         features(5, 0)
         quantise_tile(6)
         quantise_tile(7)
-        w2_begun[1] = begin_w2(1)
-        gate_sums(7)
+        w2_begun = [begin_w2(b) for b in range(2)]
         both_weight_sums(6)
         features(6, 1)
+        gate_sums(7)
         both_weight_sums(7)
-        for i in (2, 3):
-            turn(i, *picked[i])
+        turn(3, *picked[3])
         z_natural = turn_z_back()
-        w2_rounded[1] = finish_w2(1, w2_begun[1])
+        w2_rounded = [finish_w2(b, w2_begun[b]) for b in range(2)]
         pick_plain(4, picks("first_4", FIRST_AT[4]), picks("second_4", SECOND_AT[4]))
         second_5 = placed("second_5", [P, SECOND_5[1] * KIB // 4], F32, SECOND_5[0])
         pick_plain(5, picks("first_5", None), second_5[:, 0:PAIRS])
@@ -533,8 +536,8 @@ def tile_list_pairwise_document_ranking_kernel(
         for b in range(2):
             w2_q[b] = quantise("w2_%d" % b, w2_rounded[b], N, work, (SECOND_5[0] + 2 + 2 * b) * KIB)
         quantise_z_natural(z_natural)
-        open_scores(0)
-        open_scores(1)
+        for h in range(len(PIECES)):
+            open_scores(h)
         last = len(PIECES) - 1
         for h, (j0, width) in enumerate(PIECES):
             if h > 0:
@@ -547,6 +550,4 @@ def tile_list_pairwise_document_ranking_kernel(
                 nc.vector.tensor_tensor(high[:, t, :], firsts, seconds[t], SUB)
             round_differences(nc.vector.tensor_copy if h == last else nc.scalar.copy, h, 1, high)
             quantise_z_dealt(h)
-            if h == last:
-                open_scores(h)
             close_scores(h, 1 if h == last else 2)

@@ -23,9 +23,9 @@ P = 128
 KIB = 1024
 BANK = 512
 NATURAL = 4
-SHARED = (5, 6)
+SHARED = (5, 6, 7)
 GPSIMD_ROUNDS = [(1, 0), (2, 0), (6, 0), (5, 0), (5, 1), (7, 0)]
-W2_SHARED = [0, 384]
+W2_SHARED = [0, 128]
 PIECES = [(0, 256), (256, 128), (384, 128)]
 
 TURN_BANK = 0
@@ -54,7 +54,7 @@ SECOND_5 = (92, 8)
 Z_NATURAL_AT = 100
 Z_DEALT_AT = 105
 HIGH = [(98, 4), (102, 1), (110, 1)]
-LAST_SECONDS = [[(109, 1), (104, 1)], [(109, 1), (104, 1)], [(109, 1), (104, 2)]]
+LAST_SECONDS = [[(109, 1), (104, 1)], [(111, 1), (112, 1)], [(109, 1), (104, 2)]]
 
 
 def tile_list_pairwise_document_ranking_kernel(
@@ -83,14 +83,12 @@ def tile_list_pairwise_document_ranking_kernel(
         pos2_t = keep.tile([P, PAIRS // 16], U16, name="pos2_t")
         tab_sc = loads.tile([P, T], U8, name="tab_sc", offset=TABLE_SCALES_AT, align_bytes=64)
         v_sc = [keep.tile([P, S], U8, name="v_sc%d" % a, align_bytes=64) for a in range(2)]
-        ident = keep.tile([P, P], F32, name="ident")
         zeros = loads.tile([P, ZEROS_SPAN // 4], I32, name="zeros", offset=0, align_bytes=64)
         tab = [loads.tile([P, T], I32, name="tab0", offset=TABLE_0_AT, align_bytes=64)]
-        make_identity(nc, ident[:])
 
         nc.vector.memset(tab_sc[:].bitcast(I32), 0)
         wg_sc = keep.tile([P, 2, H], U8, name="wg_sc", align_bytes=64)
-        nc.vector.memset(wg_sc[:].bitcast(I32), 0)
+        nc.gpsimd.memset(wg_sc[:].bitcast(I32), 0)
         nc.vector.memset(zeros[:, 0 : S // 4], 0)
         nc.vector.tensor_copy(v_sc[1][:].bitcast(I32), zeros[:, 0 : S // 4])
         scale_rows = tab_scales.bitcast(I32).rearrange("a (q r) t -> r q a t", r=4)
@@ -436,8 +434,11 @@ def tile_list_pairwise_document_ranking_kernel(
         load_w1(0, 1, FIRST_W1_AT)
         gather_scales()
         warm = keep.tile([P, 8], F32, name="warm")
-        nc.scalar.activation(warm[:, 0:1], ident[:, 0:1], SIGMOID)
+        nc.vector.memset(warm[:, 0:1], 0.0)
+        nc.scalar.activation(warm[:, 4:5], warm[:, 0:1], SIGMOID)
         gather_first_pass()
+        ident = loads.tile([P, P], F32, name="ident", offset=TABLE_0_AT + 13 * KIB + KIB // 2, align_bytes=64)
+        make_identity(nc, ident[:])
         load_w1(1, 1, TABLE_0_AT)
         wg_rest = load_wg("wg_rest", P, H // 2 - P, TABLE_0_AT + 12 * KIB)
         load_w1(2, 1, TABLE_0_AT + 4 * KIB)
@@ -492,7 +493,6 @@ def tile_list_pairwise_document_ranking_kernel(
         round_tile(7)
         features(5, 1)
         gate_sums(6)
-        turn(2, *picked[2])
         pick_natural(3)
 
         features(4, 0)
@@ -501,10 +501,14 @@ def tile_list_pairwise_document_ranking_kernel(
         quantise_tile(6)
         quantise_tile(7)
         w2_begun = [begin_w2(b) for b in range(2)]
-        both_weight_sums(6)
+        weight_sums(6, 1)
+        weight_sums(7, 1)
         features(6, 1)
         gate_sums(7)
-        both_weight_sums(7)
+        features(7, 1)
+        weight_sums(6, 0)
+        weight_sums(7, 0)
+        turn(2, *picked[2])
         turn(3, *picked[3])
         z_natural = turn_z_back()
         w2_rounded = [finish_w2(b, w2_begun[b]) for b in range(2)]
@@ -530,8 +534,7 @@ def tile_list_pairwise_document_ranking_kernel(
 
         features(6, 0)
         features(7, 0)
-        features(7, 1)
-        seconds = pick_seconds(0)
+        seconds = {h: pick_seconds(h) for h in range(2)}
         w2_q = {}
         for b in range(2):
             w2_q[b] = quantise("w2_%d" % b, w2_rounded[b], N, work, (SECOND_5[0] + 2 + 2 * b) * KIB)
@@ -540,14 +543,14 @@ def tile_list_pairwise_document_ranking_kernel(
             open_scores(h)
         last = len(PIECES) - 1
         for h, (j0, width) in enumerate(PIECES):
-            if h > 0:
-                seconds = pick_seconds(h)
+            if h == last:
+                seconds[h] = pick_seconds(h)
             start, span = HIGH[h]
             high = placed("differences_high_%d" % h, [P, span * KIB // (4 * width), width], F32, start)[:, 0:2, :]
             entries = slice(j0 // 16, (j0 + width) // 16)
             for t, i in enumerate((6, 7)):
                 firsts = windows[i][:].indirect(pos1_t[:, entries])
-                nc.vector.tensor_tensor(high[:, t, :], firsts, seconds[t], SUB)
+                nc.vector.tensor_tensor(high[:, t, :], firsts, seconds[h][t], SUB)
             round_differences(nc.vector.tensor_copy if h == last else nc.scalar.copy, h, 1, high)
             quantise_z_dealt(h)
             close_scores(h, 1 if h == last else 2)

@@ -24,7 +24,7 @@ KIB = 1024
 BANK = 512
 NATURAL = 4
 SHARED = (5, 6, 7)
-GPSIMD_ROUNDS = [(1, 0), (2, 0), (6, 0), (5, 0), (5, 1), (7, 0)]
+GPSIMD_ROUNDS = [(1, 0), (2, 0), (5, 0), (5, 1), (7, 0)]
 W2_SHARED = [0, 128]
 PIECES = [(0, 256), (256, 128), (384, 128)]
 
@@ -89,19 +89,21 @@ def tile_list_pairwise_document_ranking_kernel(
         nc.vector.memset(tab_sc[:].bitcast(I32), 0)
         wg_sc = keep.tile([P, 2, H], U8, name="wg_sc", align_bytes=64)
         nc.gpsimd.memset(wg_sc[:].bitcast(I32), 0)
-        nc.vector.memset(zeros[:, 0 : S // 4], 0)
-        nc.vector.tensor_copy(v_sc[1][:].bitcast(I32), zeros[:, 0 : S // 4])
+        half = S // 8
+        nc.vector.memset(tab[0][:, T - half : T], 0)
+        nc.vector.memset(zeros[:, 0:half], 0)
+        nc.vector.tensor_copy(v_sc[1][:].bitcast(I32)[:, 0:half], tab[0][:, T - half : T])
+        nc.vector.tensor_copy(v_sc[1][:].bitcast(I32)[:, half : 2 * half], zeros[:, 0:half])
         scale_rows = tab_scales.bitcast(I32).rearrange("a (q r) t -> r q a t", r=4)
-        for r in range(4):
-            nc.scalar.dma_start(out=tab_sc[r:P:16, :].bitcast(I32), in_=scale_rows[r])
         for q in range(4):
             nc.gpsimd.dma_start(
                 out=wg_sc[32 * q : 32 * q + 4, :, :].bitcast(I32),
                 in_=wg_scales[:, 4 * q : 4 * q + 4, :].rearrange("a r t -> r a t").bitcast(I32),
             )
 
-        def load_table(a):
-            nc.sync.dma_start(out=tab[a][:, 0:T], in_=tab_words[a].rearrange("p t i -> p (t i)").bitcast(I32))
+        def load_table(a, first=0, last=T):
+            words = tab_words[a].rearrange("p t i -> p (t i)").bitcast(I32)
+            nc.sync.dma_start(out=tab[a][:, first:last], in_=words[:, first:last])
 
         def load_wg(name, first, count, offset):
             words = loads.tile([P, 2, 2 * count], U8, name=name, offset=offset, align_bytes=64)
@@ -425,9 +427,12 @@ def tile_list_pairwise_document_ranking_kernel(
                 nc.sync.dma_start(out=out_view[:, first : first + group, j0 : j0 + width], in_=result[:])
 
         nc.sync.dma_start(offs_t[:], offs)
-        load_table(0)
+        load_table(0, 0, T // 2)
         nc.sync.dma_start(pos1_t[:], pos1)
         nc.sync.dma_start(pos2_t[:], pos2)
+        for r in range(4):
+            nc.sync.dma_start(out=tab_sc[r:P:16, :].bitcast(I32), in_=scale_rows[r])
+        load_table(0, T // 2, T)
         tab.append(loads.tile([P, TABLE_1_SPAN // 4], I32, name="tab1", offset=0, align_bytes=64))
         load_table(1)
         wg_first = load_wg("wg_first", 0, P, TABLE_1_SPAN)

@@ -23,38 +23,45 @@ P = 128
 KIB = 1024
 BANK = 512
 NATURAL = 4
-SHARED = (5, 6, 7)
-GPSIMD_ROUNDS = [(1, 0), (2, 0), (5, 0), (5, 1), (7, 0)]
-W2_SHARED = [0, 128]
+SHARED = (3, 4, 5, 6, 7)
 PIECES = [(0, 256), (256, 128), (384, 128)]
+W2_SHARED = 128
 
-TURN_BANK = 0
-GATE_BANK = [(0, 1), (6, 7), (6, 7), (6, 7), (6, 7), (0, 1), (6, 7), (5, 7)]
-SUM_BANK = [(6, 7), (4, 5), (2, 3), (4, 5), (1, 5), (2, 0), (4, 5), (2, 3)]
-SCORE_BANKS = [(6, 7), (4, 5), (2, 3, 0, 1)]
+GATE_BANK = [(4, 5), (6, 7), (4, 5), (7, 6), (7, 5), (5, 4), (5, 4), (5, 4)]
+SUM_BANK = [(0, 1), (2, 3), (0, 1), (2, 4), (0, 6), (1, 7), (2, 6), (0, 7)]
+TURN_BANK = [1, 3, 3, 3]
+BACK_BANK = [4, 5]
+SCORE_BANKS = [(6, 7), (4, 5), (0, 1, 2, 3)]
 
-ZEROS_SPAN = 48 * KIB
-TABLE_1_SPAN = 40 * KIB
-FIRST_W1_AT = TABLE_1_SPAN + KIB
-FIRST_GATE_AT = FIRST_W1_AT + 2 * KIB
-TABLE_0_AT = 48 * KIB
-TABLE_SCALES_AT = 64 * KIB
-
-ROUNDED = {1: (0, 28), 2: (4, 10), 3: (14, 14), 4: (16, 2), 5: (18, 12), 6: (6, 6), 7: (20, 6)}
-WG_DEALT_AT = 2
-GATE_AT = {1: 32, 2: 36, 3: 40, 4: 48, 5: 44, 6: 26, 7: 52}
-CODES_AT = {2: 32, 3: 36, 4: 40, 5: 41, 6: 48, 7: 49}
-FIRST_AT = {3: 16, 4: 6}
-SECOND_AT = {0: 0, 1: 4, 2: 14, 3: 18, 4: 20}
-W2_ROUNDED_AT = [8, 22]
-WIDE_WINDOWS_AT = 56
-WINDOWS_AT = 72
-LAST_SUMS_AT = 88
-SECOND_5 = (92, 8)
-Z_NATURAL_AT = 100
-Z_DEALT_AT = 105
-HIGH = [(98, 4), (102, 1), (110, 1)]
-LAST_SECONDS = [[(109, 1), (104, 1)], [(111, 1), (112, 1)], [(109, 1), (104, 2)]]
+TABLE_AT = [26, 49]
+TABLE_SPAN = [(0, 48.5), (49, 66.5)]
+TABLE_CUT = [T // 4, 3 * T // 4]
+TABLE_SCALES_AT, TABLE_SCALES_SPAN = 200, 7
+W1_AT = {0: 4.5, 1: 10.5, 2: 32.5, 4: 16.5}
+W1_SPAN = {0: 4, 1: 4, 2: 8, 4: 8}
+W2_AT = [49, 57]
+WG_AT = {2: 3.5, 4: 10.5}
+WG_DEALT_AT = 74
+BIAS_AT = 65
+IDENT_AT = 206
+ROUNDED = {1: (72, 76, 78), 2: (76, 76, 80), 4: (76, 76, 86.0625), 6: (86, 86, 98)}
+FIRST_ROUNDED_AT = 76
+CODES_AT = {1: 6.5, 2: 11.5, 4: 144, 6: 148}
+FIRST_CODES_AT = 65.5
+WINDOW_AT = [207, 108, 207, 120, 162, 100, 104, 116]
+GATE_AT = [6.5, 12.5, 44.5, 40.5] + [128 + 4 * i for i in range(4)]
+SHARED_AT = {3: (144, 2), 4: (146, 2), 5: (148, 6), 6: (154, 2), 7: (166, 2)}
+FIRST_AT = [158, 36.5, 11.5, 82, 150, 168]
+SECOND_AT = [(72, 2), (38.5, 2), (80, 2), (84, 2), (152, 2), (172, 8), (182, 2), (196, 2)]
+W2_CODES_AT = [174, 176]
+Z_CODES_AT = 172
+HIGH_AT = [(178, 4), (180, 1), (181, 1)]
+LOW_AT = 156
+W2_ROUNDED_AT = [90, 94]
+Z_TURNED_AT = 184
+Z_ROUNDED_AT = 188
+Z_DEALT_AT = 192
+RESULT_AT = 108
 
 
 def tile_list_pairwise_document_ranking_kernel(
@@ -63,7 +70,6 @@ def tile_list_pairwise_document_ranking_kernel(
     nc = tc.nc
     with ExitStack() as ctx:
         keep = ctx.enter_context(tc.tile_pool(name="keep", bufs=1))
-        loads = ctx.enter_context(tc.tile_pool(name="loads", bufs=1))
         work = ctx.enter_context(tc.tile_pool(name="work", bufs=1))
         psum = ctx.enter_context(tc.psum_pool(name="psum", bufs=1))
 
@@ -71,270 +77,238 @@ def tile_list_pairwise_document_ranking_kernel(
             return psum.tile(shape, F32, name=name, offset=2 * KIB * bank)
 
         def placed(name, shape, dtype, kib):
-            return work.tile(shape, dtype, name=name, offset=kib * KIB, align_bytes=64)
-
-        def picks(name, kib):
-            if kib is None:
-                return keep.tile([P, PAIRS], F32, name=name)[:]
-            return placed(name, [P, PAIRS], F32, kib)[:]
+            return work.tile(shape, dtype, name=name, offset=int(kib * KIB), align_bytes=64)
 
         offs_t = keep.tile([P, S // 16], U16, name="offs_t")
         pos1_t = keep.tile([P, PAIRS // 16], U16, name="pos1_t")
         pos2_t = keep.tile([P, PAIRS // 16], U16, name="pos2_t")
-        tab_sc = loads.tile([P, T], U8, name="tab_sc", offset=TABLE_SCALES_AT, align_bytes=64)
-        v_sc = [keep.tile([P, S], U8, name="v_sc%d" % a, align_bytes=64) for a in range(2)]
-        zeros = loads.tile([P, ZEROS_SPAN // 4], I32, name="zeros", offset=0, align_bytes=64)
-        tab = [loads.tile([P, T], I32, name="tab0", offset=TABLE_0_AT, align_bytes=64)]
 
-        nc.vector.memset(tab_sc[:].bitcast(I32), 0)
-        wg_sc = keep.tile([P, 2, H], U8, name="wg_sc", align_bytes=64)
-        nc.gpsimd.memset(wg_sc[:].bitcast(I32), 0)
-        half = S // 8
-        nc.vector.memset(tab[0][:, T - half : T], 0)
-        nc.vector.memset(zeros[:, 0:half], 0)
-        nc.vector.tensor_copy(v_sc[1][:].bitcast(I32)[:, 0:half], tab[0][:, T - half : T])
-        nc.vector.tensor_copy(v_sc[1][:].bitcast(I32)[:, half : 2 * half], zeros[:, 0:half])
-        scale_rows = tab_scales.bitcast(I32).rearrange("a (q r) t -> r q a t", r=4)
-        for q in range(4):
-            nc.gpsimd.dma_start(
-                out=wg_sc[32 * q : 32 * q + 4, :, :].bitcast(I32),
-                in_=wg_scales[:, 4 * q : 4 * q + 4, :].rearrange("a r t -> r a t").bitcast(I32),
-            )
+        tab = []
+        for a, (start, end) in enumerate(TABLE_SPAN):
+            span = placed("tab%d" % a, [P, int((end - start) * KIB) // 4], I32, start)
+            skip = (TABLE_AT[a] - start) * KIB // 4
+            tab.append(span[:, skip : skip + T])
 
-        def load_table(a, first=0, last=T):
+        def load_table(a, first, last):
             words = tab_words[a].rearrange("p t i -> p (t i)").bitcast(I32)
             nc.sync.dma_start(out=tab[a][:, first:last], in_=words[:, first:last])
 
-        def load_wg(name, first, count, offset):
-            words = loads.tile([P, 2, 2 * count], U8, name=name, offset=offset, align_bytes=64)
+        gate_w = {}
+        gate_sc = {}
+
+        def load_wg(first, count):
+            shape = [P, 2, 2 * P * count]
+            if first == 0:
+                words = keep.tile(shape, U8, name="wg_0", align_bytes=64)
+            else:
+                words = placed("wg_%d" % first, shape, U8, WG_AT[first])
             rows = wg_words.bitcast(I32).rearrange("a p n -> p a n")
-            nc.sync.dma_start(out=words[:].bitcast(I32), in_=rows[:, :, first // 2 : (first + count) // 2])
+            nc.sync.dma_start(out=words[:].bitcast(I32), in_=rows[:, :, first * P // 2 : (first + count) * P // 2])
+            for a in range(2):
+                for t in range(count):
+                    gate_w[(first + t, a)] = words[:, a, 2 * P * t : 2 * P * (t + 1)]
             return words
+
+        def deal_wg_scales(plane):
+            scales = keep.tile([P, 2, 4, P], U8, name="wg_sc_dealt", align_bytes=64)
+            nc.gpsimd.tensor_copy(
+                scales[:].bitcast(I32).rearrange("p a t (q w) -> p a t q w", w=2),
+                plane[:, :, H // 2 : H].bitcast(I32).rearrange("p a (q t w) -> p a t q w", t=4, w=2),
+            )
+            for a in range(2):
+                for t in range(4):
+                    gate_sc[(NATURAL + t, a)] = scales[:, a, t, :]
+
+        def deal_wg_words(loaded):
+            words = placed("wg_dealt", [P, 2, 4, 2 * P], U8, WG_DEALT_AT)
+            nc.gpsimd.tensor_copy(
+                words[:].bitcast(I32).rearrange("p a t (q w) -> p a t q w", w=4),
+                loaded[:].bitcast(I32).rearrange("p a (q t w) -> p a t q w", t=4, w=4),
+            )
+            for a in range(2):
+                for t in range(4):
+                    gate_w[(NATURAL + t, a)] = words[:, a, t, :]
+
+        def load_wg_scales(engine, plane, first, count):
+            for q in range(4):
+                rows = wg_scales[:, 4 * q : 4 * q + 4, first * P : (first + count) * P]
+                engine.dma_start(
+                    out=plane[32 * q : 32 * q + 4, :, :].bitcast(I32),
+                    in_=rows.rearrange("a r t -> r a t").bitcast(I32),
+                )
+            for a in range(2):
+                for t in range(count):
+                    gate_sc[(first + t, a)] = plane[:, a, P * t : P * (t + 1)]
 
         w1_raw = {}
 
-        def load_w1(first, count, offset):
+        def load_w1(first, count):
             for a in range(2):
-                rows = 8 if (first, a) == (0, 1) else 4
-                raw = loads.tile(
-                    [P, rows, count * P], F32, name="w1_raw_%d_%d" % (first, a),
-                    offset=offset + a * count * 2 * KIB, align_bytes=64,
-                )[:, 0:4, :]
+                rows = W1_SPAN[first] * 2 // count if a == 1 else 4
+                raw = placed("w1_raw_%d_%d" % (first, a), [P, rows, count * P], F32, W1_AT[first] + 2 * count * a)
                 cols = w1[512 * a : 512 * (a + 1), first * P : (first + count) * P]
-                nc.sync.dma_start(out=raw, in_=cols.rearrange("(p j) c -> p j c", j=4))
-                if first < NATURAL:
-                    tiles = raw.rearrange("p j (t q e) -> p t j q e", t=count, e=8)
-                else:
-                    tiles = raw.rearrange("p j (q t e) -> p t j q e", t=count, e=8)
-                for t in range(count):
-                    w1_raw[(first + t, a)] = tiles[:, t]
+                nc.sync.dma_start(out=raw[:, 0:4, :], in_=cols.rearrange("(p j) c -> p j c", j=4))
+                w1_raw[(first, a)] = raw[:, 0:4, :]
 
-        def load_w2(offset):
-            natural = loads.tile([P, 4, N], F32, name="w2_raw0", offset=offset, align_bytes=64)
-            nc.sync.dma_start(out=natural[:], in_=w2[0:512, :].rearrange("(p t) n -> p t n", t=4))
-            dealt = loads.tile([P, 4, N], F32, name="w2_raw1", offset=offset + 8 * KIB, align_bytes=64)
-            rows = w2[512:1024, :].rearrange("(q t e) n -> t q e n", t=4, e=8)
-            for t in range(4):
-                nc.sync.dma_start(out=dealt[:, t, :], in_=rows[t])
-            return natural, dealt
+        w2_raw = {}
 
-        def gather_scales():
-            nc.vector.tensor_copy(v_sc[0][:], tab_sc[:].indirect(offs_t[:]))
-            nc.scalar.dma_start(out=v_sc[1][0 : P - 16, :].bitcast(I32), in_=v_sc[0][16:P, :].bitcast(I32))
+        def load_w2(b):
+            w2_raw[b] = placed("w2_raw%d" % b, [P, 4, N], F32, W2_AT[b])
+            if b == 0:
+                nc.sync.dma_start(out=w2_raw[b][:], in_=w2[0:512, :].rearrange("(p t) n -> p t n", t=4))
+            else:
+                rows = w2[512:1024, :].rearrange("(q t e) n -> t q e n", t=4, e=8)
+                for t in range(4):
+                    nc.sync.dma_start(out=w2_raw[b][:, t, :], in_=rows[t])
 
         v_words = {}
 
         def gather_first_pass():
-            words = loads.tile([P, S], U32, name="v_words_0", offset=TABLE_SCALES_AT, align_bytes=64)
+            words = placed("v_words_0", [P, S], U32, TABLE_SCALES_AT)
             nc.vector.tensor_copy(words[:], tab[0][:, 0:T].bitcast(U32).indirect(offs_t[:]))
             for d in range(2):
                 v_words[(0, d)] = words[:, BANK * d : BANK * (d + 1)]
 
-        def gather_second_pass():
-            for d in range(2):
-                words = keep.tile([P, BANK], U32, name="v_words_1_%d" % d, align_bytes=64)
-                entries = offs_t[:, BANK * d // 16 : BANK * (d + 1) // 16]
-                nc.vector.tensor_copy(words[:], tab[1][:, 0:T].bitcast(U32).indirect(entries))
-                v_words[(1, d)] = words[:]
+        def gather_second_pass(d):
+            words = keep.tile([P, BANK], U32, name="v_words_1_%d" % d, align_bytes=64)
+            entries = offs_t[:, BANK * d // 16 : BANK * (d + 1) // 16]
+            nc.vector.tensor_copy(words[:], tab[1][:, 0:T].bitcast(U32).indirect(entries))
+            v_words[(1, d)] = words[:]
 
-        def quantise(name, rounded, width, pool=keep, offset=None):
-            codes = pool.tile([P, width], U32, name="codes_" + name, offset=offset, align_bytes=64)
+        def quantise(name, rounded, width, kib=None):
+            if kib is None:
+                codes = keep.tile([P, width], U32, name="codes_" + name, align_bytes=64)
+            else:
+                codes = placed("codes_" + name, [P, width], U32, kib)
             scales = keep.tile([P, width], U8, name="scales_" + name, align_bytes=64)
             nc.vector.quantize_mx(out=codes[:].bitcast(FP8X4), scales=scales[:], in_=rounded)
             return codes, scales
 
-        def gpsimd_round(out, in_):
-            nc.gpsimd.tensor_scalar(out, in_, 1.0, 0.0, MULT, ADD)
+        def gpsimd_round(dst, raw):
+            nc.gpsimd.tensor_scalar(dst, raw.rearrange("p j c -> p c j"), 1.0, 0.0, MULT, ADD)
 
-        def round_w1(dst, i, a):
-            if (i, a) in GPSIMD_ROUNDS:
-                raw = w1_raw[(i, a)].rearrange("p j q e -> p q e j")
-                gpsimd_round(dst.rearrange("p (q e) j -> p q e j", e=8), raw)
+        def scalar_round(dst, raw):
+            nc.scalar.copy(
+                out=dst.rearrange("p (g i) j -> p g j i", i=2), in_=raw.rearrange("p j (g i) -> p g j i", i=2)
+            )
+
+        w1_q = {}
+        w1_rounded = {}
+
+        def prepare_first_w1(a):
+            if a == 0:
+                rounded = keep.tile([P, P, 4], BF16, name="w1_rounded_0_0", align_bytes=64)
+            else:
+                rounded = placed("w1_rounded_0_1", [P, P, 4], BF16, FIRST_ROUNDED_AT)
+            scalar_round(rounded[:], w1_raw[(0, a)])
+            codes, scales = quantise("w1_0_%d" % a, rounded[:].rearrange("p c j -> p (c j)"), P, FIRST_CODES_AT + a / 2)
+            w1_q[(0, a)] = (codes[:], scales[:])
+
+        def round_w1(rounder, first, count, a, lo, hi):
+            if first not in w1_rounded:
+                start, data, end = ROUNDED[first]
+                span = placed("w1_rounded_%d" % first, [P, int((end - start) * KIB) // 2], BF16, start)
+                skip = (data - start) * KIB // 2
+                w1_rounded[first] = span[:, skip : skip + count * KIB]
+            dst = w1_rounded[first].rearrange("p (a c j) -> p a c j", a=2, j=4)
+            rounder(dst[:, a, P * lo : P * hi, :], w1_raw[(first, a)][:, :, P * lo : P * hi])
+
+        def round_dealt(on_gpsimd, i, a):
+            first = i - i % 2
+            if first not in w1_rounded:
+                start, data, end = ROUNDED[first]
+                span = placed("w1_rounded_%d" % first, [P, int((end - start) * KIB) // 2], BF16, start)
+                skip = (data - start) * KIB // 2
+                w1_rounded[first] = span[:, skip : skip + 2 * KIB]
+            dst = w1_rounded[first].rearrange("p (a t c j) -> p a t c j", a=2, t=2, j=4)[:, a, i % 2]
+            raw = w1_raw[(NATURAL, a)].rearrange("p j (q t e) -> p t j q e", t=4, e=8)[:, i - NATURAL]
+            if on_gpsimd:
+                out = dst.rearrange("p (q e) j -> p q e j", e=8)
+                nc.gpsimd.tensor_scalar(out, raw.rearrange("p j q e -> p q e j"), 1.0, 0.0, MULT, ADD)
             else:
                 nc.scalar.copy(
                     out=dst.rearrange("p (q g i) j -> p q g j i", g=4, i=2),
-                    in_=w1_raw[(i, a)].rearrange("p j q (g i) -> p q g j i", i=2),
+                    in_=raw.rearrange("p j q (g i) -> p q g j i", i=2),
                 )
 
-        w1_rounded = {}
-        w1_q = {}
-
-        def prepare_first_w1():
-            early = keep.tile([P, P, 4], BF16, name="w1_rounded_0_0", align_bytes=64)
-            late = placed("w1_rounded_0_1", [P, P, 4], BF16, ROUNDED[1][0])
-            for a, rounded in enumerate((early, late)):
-                round_w1(rounded[:], 0, a)
-                flat = rounded[:].rearrange("p c j -> p (c j)")
-                codes, scales = quantise("w1_0_%d" % a, flat, P, loads, TABLE_1_SPAN - (2 - a) * KIB)
-                w1_q[(0, a)] = (codes[:], scales[:])
-
-        def round_tile(i, passes=(0, 1)):
-            if i not in w1_rounded:
-                start, span = ROUNDED[i]
-                w1_rounded[i] = placed("w1_rounded_%d" % i, [P, span, P, 4], BF16, start)[:, 0:2, :, :]
-            for a in passes:
-                round_w1(w1_rounded[i][:, a, :, :], i, a)
-
-        def quantise_tile(i):
-            flat = w1_rounded[i].rearrange("p a c j -> p (a c j)")
-            if i == 1:
-                codes, scales = quantise("w1_1", flat, 2 * P, loads, FIRST_GATE_AT)
-            else:
-                codes, scales = quantise("w1_%d" % i, flat, 2 * P, work, CODES_AT[i] * KIB)
+        def quantise_w1(first, count):
+            codes, scales = quantise("w1_%d" % first, w1_rounded[first], 2 * count * P, CODES_AT[first])
             for a in range(2):
-                w1_q[(i, a)] = (codes[:, P * a : P * (a + 1)], scales[:, P * a : P * (a + 1)])
+                for t in range(count):
+                    cols = slice(P * (a * count + t), P * (a * count + t + 1))
+                    w1_q[(first + t, a)] = (codes[:, cols], scales[:, cols])
 
-        def begin_w2(b):
-            rounded = placed("w2_rounded%d" % b, [P, N, 4], BF16, W2_ROUNDED_AT[b])
-            shared = W2_SHARED[b]
-            if shared:
-                gpsimd_round(rounded[:, 0:shared, :], w2_raw[b][:, :, 0:shared].rearrange("p t n -> p n t"))
-            return rounded
-
-        def finish_w2(b, rounded):
-            for first in range(W2_SHARED[b], N, P):
-                cols = slice(first, first + P)
-                nc.scalar.copy(
-                    out=rounded[:, cols, :].rearrange("p (g i) t -> p g t i", i=2),
-                    in_=w2_raw[b][:, :, cols].rearrange("p t (g i) -> p g t i", i=2),
-                )
-            return rounded[:].rearrange("p n t -> p (n t)")
-
-        gate_w = {}
-
-        def name_natural_wg():
-            for a in range(2):
-                for i in range(NATURAL):
-                    words = wg_first[:, a, :] if i == 0 else wg_rest[:, a, 2 * P * (i - 1) : 2 * P * i]
-                    gate_w[(i, a)] = (words, wg_sc[:, a, P * i : P * (i + 1)])
-
-        def deal_wg_scales():
-            scales = keep.tile([P, 2, 4, P], U8, name="wg_sc_dealt", align_bytes=64)
-            nc.gpsimd.tensor_copy(
-                scales[:].bitcast(I32).rearrange("p a t (q w) -> p a t q w", w=2),
-                wg_sc[:, :, H // 2 : H].bitcast(I32).rearrange("p a (q t w) -> p a t q w", t=4, w=2),
+        def first_stage_pass(bank, codes, scales, fmt, d, a):
+            nc.tensor.matmul_mx(
+                out=bank[:],
+                lhsT=codes.bitcast(fmt),
+                lhsT_scale=scales,
+                rhs=v_words[(a, d)].bitcast(FP8X4),
+                rhs_scale=v_sc[:, a, BANK * d : BANK * (d + 1)],
+                start=(a == 0),
+                stop=(a == 1),
             )
-            return scales
 
-        def deal_wg_words(scales):
-            words = placed("wg_dealt", [P, 2, 4, 2 * P], U8, WG_DEALT_AT)
-            nc.gpsimd.tensor_copy(
-                words[:].bitcast(I32).rearrange("p a t (q w) -> p a t q w", w=4),
-                wg_high[:].bitcast(I32).rearrange("p a (q t w) -> p a t q w", t=4, w=4),
-            )
-            for a in range(2):
-                for t in range(4):
-                    gate_w[(NATURAL + t, a)] = (words[:, a, t, :], scales[:, a, t, :])
-
-        wide = [placed("wide_window_%d" % u, [P, 2 * S], F32, WIDE_WINDOWS_AT + 8 * u) for u in range(2)]
-        for window in wide:
-            nc.vector.memset(window[:, S : 2 * S], 0.0)
-        windows = {i: wide[i % 2] for i in range(NATURAL)}
-        for t in range(4):
-            windows[NATURAL + t] = placed("window_%d" % (NATURAL + t), [P, S], F32, WINDOWS_AT + 4 * t)
-        w1_sums = {}
+        gate_banks = {}
         gates = {}
+        w1_sums = {}
         shared_sums = {}
+        windows = {}
 
-        def first_stage_sum(bank, weights, fmt, i, d, passes=(0, 1)):
-            for a in passes:
-                codes, scales = weights[(i, a)]
-                nc.tensor.matmul_mx(
-                    out=bank[:],
-                    lhsT=codes.bitcast(fmt),
-                    lhsT_scale=scales,
-                    rhs=v_words[(a, d)].bitcast(FP8X4),
-                    rhs_scale=v_sc[a][:, BANK * d : BANK * (d + 1)],
-                    start=(a == 0),
-                    stop=(a == 1),
-                )
+        def gate_pass(i, d, a):
+            if a == 0:
+                gate_banks[(i, d)] = bank_tile("g_bank_%d_%d" % (i, d), [P, BANK], GATE_BANK[i][d])
+            first_stage_pass(gate_banks[(i, d)], gate_w[(i, a)], gate_sc[(i, a)], FP4X4, d, a)
 
-        def halves(i):
-            return (1, 0) if i in SHARED else (0, 1)
+        def copy_gate(i, d):
+            gates[(i, d)] = placed("gate_%d_%d" % (i, d), [P, BANK], F32, GATE_AT[i] + 2 * d)
+            nc.scalar.copy(out=gates[(i, d)][:], in_=gate_banks[(i, d)][:])
 
-        def copy_gate(i, d, bank):
-            if i == 0:
-                offset = FIRST_GATE_AT + 2 * KIB * d
-                gates[(i, d)] = loads.tile([P, BANK], F32, name="gate_0_%d" % d, offset=offset, align_bytes=64)
-            else:
-                gates[(i, d)] = placed("gate_%d_%d" % (i, d), [P, BANK], F32, GATE_AT[i] + 2 * d)
-            nc.scalar.copy(out=gates[(i, d)][:], in_=bank[:])
+        def gate_sum(i, d):
+            gate_pass(i, d, 0)
+            gate_pass(i, d, 1)
+            copy_gate(i, d)
 
-        def gate_sums(i):
-            for d in halves(i):
-                bank = bank_tile("g_bank_%d_%d" % (i, d), [P, BANK], GATE_BANK[i][d])
-                first_stage_sum(bank, gate_w, FP4X4, i, d)
-                copy_gate(i, d, bank)
-
-        def first_sums():
-            banks = [bank_tile("g_bank_0_%d" % d, [P, BANK], GATE_BANK[0][d]) for d in range(2)]
-            for d in range(2):
-                w1_sums[(0, d)] = bank_tile("a_bank_0_%d" % d, [P, BANK], SUM_BANK[0][d])
-                first_stage_sum(banks[d], gate_w, FP4X4, 0, d, [0])
-            for d in range(2):
-                first_stage_sum(banks[d], gate_w, FP4X4, 0, d, [1])
-                copy_gate(0, d, banks[d])
-            first_stage_sum(w1_sums[(0, 0)], w1_q, FP8X4, 0, 0)
-            first_stage_sum(w1_sums[(0, 1)], w1_q, FP8X4, 0, 1)
-
-        def weight_sums(i, d):
+        def weight_sum(i, d):
             w1_sums[(i, d)] = bank_tile("a_bank_%d_%d" % (i, d), [P, BANK], SUM_BANK[i][d])
-            first_stage_sum(w1_sums[(i, d)], w1_q, FP8X4, i, d)
+            for a in range(2):
+                first_stage_pass(w1_sums[(i, d)], *w1_q[(i, a)], FP8X4, d, a)
             if d == 1 and i in SHARED:
-                if i == SHARED[-1]:
-                    shared_sums[i] = placed("shared_sums_last", [P, BANK], F32, LAST_SUMS_AT)
-                else:
-                    shared_sums[i] = keep.tile([P, BANK], F32, name="shared_sums_%d" % i)
-                nc.scalar.copy(out=shared_sums[i][:], in_=w1_sums[(i, d)][:])
-
-        def both_weight_sums(i):
-            for d in halves(i):
-                weight_sums(i, d)
+                start, span = SHARED_AT[i]
+                shared_sums[i] = placed("shared_sums_%d" % i, [P, span * KIB // 4], F32, start)[:, 0:BANK]
+                nc.scalar.copy(out=shared_sums[i], in_=w1_sums[(i, d)][:])
 
         def features(i, d):
+            if i not in windows:
+                windows[i] = placed("window_%d" % i, [P, 2 * S if i < NATURAL else S], F32, WINDOW_AT[i])
             dst = windows[i][:, BANK * d : BANK * (d + 1)]
             if d == 1 and i in SHARED:
-                nc.gpsimd.tensor_tensor(dst, shared_sums[i][:], gates[(i, d)][:], MULT)
+                nc.gpsimd.tensor_tensor(dst, shared_sums[i], gates[(i, d)][:], MULT)
             else:
                 nc.vector.tensor_tensor(dst, w1_sums[(i, d)][:], gates[(i, d)][:], MULT)
 
+        firsts = {}
+        seconds = {}
 
-        picked = {}
+        def pick_first(i):
+            firsts[i] = placed("first_%d" % i, [P, PAIRS], F32, FIRST_AT[i])[:]
+            nc.vector.tensor_copy(firsts[i], windows[i][:, 0:S].indirect(pos1_t[:]))
 
-        def pick_natural(i):
-            first = picks("first_%d" % i, FIRST_AT.get(i))
-            negated_second = picks("second_%d" % i, SECOND_AT.get(i))
-            nc.vector.tensor_copy(first, windows[i][:, 0:S].indirect(pos1_t[:]))
-            nc.vector.tensor_scalar(negated_second, windows[i][:].indirect(pos2_t[:]), -1.0, 0.0, MULT, ADD)
-            picked[i] = (first, negated_second)
+        def pick_second(i):
+            start, span = SECOND_AT[i]
+            seconds[i] = placed("second_%d" % i, [P, span * KIB // 4], F32, start)[:, 0:PAIRS]
+            if i < NATURAL:
+                nc.vector.tensor_scalar(seconds[i], windows[i][:].indirect(pos2_t[:]), -1.0, 0.0, MULT, ADD)
+            else:
+                nc.vector.tensor_copy(seconds[i], windows[i][:].indirect(pos2_t[:]))
 
-        z_turned = placed("z_turned", [P, 4, 2, 2 * P], BF16, Z_DEALT_AT)
+        z_turned = placed("z_turned", [P, 4, 2, 2 * P], BF16, Z_TURNED_AT)
 
-        def turn(i, first, negated_second):
-            bank = bank_tile("zt_bank_%d" % i, [P, 4, P], TURN_BANK + i % 2)
+        def turn(i):
+            bank = bank_tile("zt_bank_%d" % i, [P, 4, P], TURN_BANK[i])
             for jb in range(4):
                 cols = slice(P * jb, P * (jb + 1))
-                for term, last in ((first, False), (negated_second, True)):
+                for term, last in ((firsts[i], False), (seconds[i], True)):
                     nc.tensor.matmul(
                         bank[:, jb, :], term[:, cols], ident[:], start=not last, stop=last, is_transpose=True
                     )
@@ -343,51 +317,59 @@ def tile_list_pairwise_document_ranking_kernel(
                 in_=bank[:].rearrange("j b (m u e) -> j b u m e", u=2, e=2),
             )
 
-        def turn_z_back():
+        z_q = {}
+
+        def turn_back():
             words = z_turned[:].bitcast(F32)
-            rounded = []
+            rounded = placed("z_rounded_0", [P, PAIRS, 4], BF16, Z_ROUNDED_AT)
             for g in range(2):
-                rounded.append(placed("z_rounded_0_%d" % g, [P, PAIRS // 2, 4], BF16, Z_NATURAL_AT + 2 * g)[:])
-                bank = bank_tile("back_bank_%d" % g, [P, 2, 2, P], TURN_BANK + g)
+                bank = bank_tile("back_bank_%d" % g, [P, 2, 2, P], BACK_BANK[g])
                 for jb in range(2):
                     for u in range(2):
                         nc.tensor.transpose(bank[:, jb, u, :], words[:, 2 * g + jb, u, :], ident[:])
                 nc.scalar.copy(
-                    out=rounded[g].bitcast(F32).rearrange("p (b j) u -> p b j u", b=2),
+                    out=rounded[:, 2 * P * g : 2 * P * (g + 1), :].bitcast(F32).rearrange("p (b j) u -> p b j u", b=2),
                     in_=bank[:].rearrange("p b u j -> p b j u"),
                 )
-            return rounded
-
-        z_q = {}
-
-        def quantise_z_natural(rounded):
-            half = PAIRS // 2
-            for g in range(2):
-                flat = rounded[g].rearrange("p j t -> p (j t)")
-                codes, scales = quantise("z_0_%d" % g, flat, half, work, (SECOND_5[0] + g) * KIB)
-                for h, (j0, width) in enumerate(PIECES):
-                    if j0 // half == g:
-                        cols = slice(j0 - half * g, j0 - half * g + width)
-                        z_q[(0, h)] = (codes[:, cols], scales[:, cols])
-
+            return rounded[:].rearrange("p j t -> p (j t)")
 
         z_dealt = [
             placed("z_rounded_1_%d" % h, [P, width, 4], BF16, Z_DEALT_AT + j0 // P)
             for h, (j0, width) in enumerate(PIECES)
         ]
+        low = placed("differences_low", [P, 2, PAIRS], F32, LOW_AT)
 
-        def pick_plain(i, first, second):
-            nc.vector.tensor_copy(first, windows[i][:].indirect(pos1_t[:]))
-            nc.vector.tensor_copy(second, windows[i][:].indirect(pos2_t[:]))
-            picked[i] = (first, second)
+        def subtract(i):
+            nc.gpsimd.tensor_tensor(low[:, i - NATURAL, :], firsts[i], seconds[i], SUB)
 
         def round_differences(copy, h, u, differences):
             copy(out=z_dealt[h][:, :, 2 * u : 2 * u + 2], in_=differences.rearrange("p t j -> p j t"))
 
-        def quantise_z_dealt(h):
+        def pick_last_differences(h):
+            j0, width = PIECES[h]
+            start, span = HIGH_AT[h]
+            high = placed("differences_high_%d" % h, [P, span * KIB // (4 * width), width], F32, start)[:, 0:2, :]
+            entries = slice(j0 // 16, (j0 + width) // 16)
+            for t in range(2):
+                firsts_now = windows[6 + t][:].indirect(pos1_t[:, entries])
+                nc.vector.tensor_tensor(high[:, t, :], firsts_now, seconds[6 + t][:, j0 : j0 + width], SUB)
+            last = h == len(PIECES) - 1
+            round_differences(nc.vector.tensor_copy if last else nc.scalar.copy, h, 1, high)
+
+        def quantise_piece(h):
             codes, scales = quantise("z_1_%d" % h, z_dealt[h][:].rearrange("p j t -> p (j t)"), PIECES[h][1])
             z_q[(1, h)] = (codes[:], scales[:])
 
+        w2_rounded = {}
+        w2_q = {}
+
+        def round_w2(rounder, b, lo, hi):
+            if b not in w2_rounded:
+                w2_rounded[b] = placed("w2_rounded%d" % b, [P, N, 4], BF16, W2_ROUNDED_AT[b])
+            rounder(w2_rounded[b][:, lo:hi, :], w2_raw[b][:, :, lo:hi])
+
+        def quantise_w2(b):
+            w2_q[b] = quantise("w2_%d" % b, w2_rounded[b][:].rearrange("p n t -> p (n t)"), N, W2_CODES_AT[b])
 
         y_banks = {}
 
@@ -418,7 +400,7 @@ def tile_list_pairwise_document_ranking_kernel(
         def close_scores(h, group):
             j0, width = PIECES[h]
             for first in range(0, N // P, group):
-                result = keep.tile([P, group, width], F32, name="result_%d_%d" % (h, first))
+                result = placed("result_%d_%d" % (h, first), [P, group, width], F32, RESULT_AT + (4 * j0 + first * width) / 256)
                 for k in range(group):
                     second_stage_pass(h, first + k, 1)
                 for k in range(group):
@@ -426,136 +408,171 @@ def tile_list_pairwise_document_ranking_kernel(
                     nc.scalar.activation(result[:, k, :], y_banks[(h, nt)], SIGMOID, bias=c_t[:, nt : nt + 1])
                 nc.sync.dma_start(out=out_view[:, first : first + group, j0 : j0 + width], in_=result[:])
 
+        tab_sc = placed("tab_sc", [P, TABLE_SCALES_SPAN * KIB], U8, TABLE_SCALES_AT)
+        nc.vector.memset(tab_sc[:, 0:T].bitcast(I32), 0)
+        wg_sc = keep.tile([P, 2, H], U8, name="wg_sc", align_bytes=64)
+        nc.gpsimd.memset(wg_sc[:].bitcast(I32), 0)
+        v_sc = keep.tile([P, 2, S], U8, name="v_sc", align_bytes=64)
+        nc.vector.memset(v_sc[:].bitcast(I32), 0)
+
         nc.sync.dma_start(offs_t[:], offs)
-        load_table(0, 0, T // 2)
+        load_table(0, 0, TABLE_CUT[0])
         nc.sync.dma_start(pos1_t[:], pos1)
         nc.sync.dma_start(pos2_t[:], pos2)
-        for r in range(4):
-            nc.sync.dma_start(out=tab_sc[r:P:16, :].bitcast(I32), in_=scale_rows[r])
-        load_table(0, T // 2, T)
-        tab.append(loads.tile([P, TABLE_1_SPAN // 4], I32, name="tab1", offset=0, align_bytes=64))
-        load_table(1)
-        wg_first = load_wg("wg_first", 0, P, TABLE_1_SPAN)
-        load_w1(0, 1, FIRST_W1_AT)
-        gather_scales()
+        load_wg(0, 2)
+        for a in range(2):
+            nc.sync.dma_start(out=tab_sc[4 * a : P : 8, 0:T].bitcast(I32), in_=tab_scales[a].bitcast(I32))
+        load_table(0, TABLE_CUT[0], T)
+        load_table(1, 0, TABLE_CUT[1])
+        load_wg_scales(nc.gpsimd, wg_sc, 0, 8)
+        deal_wg_scales(wg_sc)
         warm = keep.tile([P, 8], F32, name="warm")
         nc.vector.memset(warm[:, 0:1], 0.0)
         nc.scalar.activation(warm[:, 4:5], warm[:, 0:1], SIGMOID)
+
+        gathered_sc = keep.tile([P, S], U8, name="gathered_sc", align_bytes=64)
+        nc.vector.tensor_copy(gathered_sc[:], tab_sc[:, 0:T].indirect(offs_t[:]))
+        for q in range(4):
+            nc.sync.dma_start(
+                out=v_sc[32 * q : 32 * q + 4, :, :].bitcast(I32),
+                in_=gathered_sc[32 * q : 32 * q + 32 : 4, :].bitcast(I32),
+            )
+        load_table(1, TABLE_CUT[1], T)
         gather_first_pass()
-        ident = loads.tile([P, P], F32, name="ident", offset=TABLE_0_AT + 13 * KIB + KIB // 2, align_bytes=64)
+        load_w1(0, 1)
+        load_w1(1, 1)
+        load_wg(2, 2)
+        load_w1(2, 2)
+        wg_high = load_wg(4, 4)
+        load_w1(4, 4)
+        ident = placed("ident", [P, P], F32, IDENT_AT)
         make_identity(nc, ident[:])
-        load_w1(1, 1, TABLE_0_AT)
-        wg_rest = load_wg("wg_rest", P, H // 2 - P, TABLE_0_AT + 12 * KIB)
-        load_w1(2, 1, TABLE_0_AT + 4 * KIB)
-        wg_high = load_wg("wg_high", H // 2, H // 2, TABLE_0_AT + 14 * KIB)
-        load_w1(3, 1, TABLE_0_AT + 8 * KIB)
-        gather_second_pass()
-        load_w1(NATURAL, 4, 0)
-        w2_raw = load_w2(16 * KIB)
-        c_t = loads.tile([P, N // P], F32, name="c_t", offset=32 * KIB, align_bytes=64)
+        for i in range(2):
+            for d in range(2):
+                gate_pass(i, d, 0)
+        gather_second_pass(0)
+        gather_second_pass(1)
+        load_w2(0)
+        load_w2(1)
+        c_t = placed("c_t", [P, N // P], F32, BIAS_AT)
         with nc.allow_non_contiguous_dma(reason="one bias value for each partition"):
             nc.sync.dma_start(out=c_t[:], in_=c.rearrange("(t p) -> p t", p=P))
 
-        wg_scales_dealt = deal_wg_scales()
-        prepare_first_w1()
-        name_natural_wg()
-        first_sums()
-        round_tile(1)
+        prepare_first_w1(0)
+        prepare_first_w1(1)
+        for d in range(2):
+            gate_pass(0, d, 1)
+            copy_gate(0, d)
+        weight_sum(0, 0)
+        weight_sum(0, 1)
+        round_w1(gpsimd_round, 1, 1, 0, 0, 1)
+        round_w1(scalar_round, 1, 1, 1, 0, 1)
+        for d in range(2):
+            gate_pass(1, d, 1)
+            copy_gate(1, d)
+        features(0, 0)
+        features(0, 1)
+        gate_sum(2, 0)
+        gate_sum(2, 1)
+        quantise_w1(1, 1)
+        weight_sum(1, 0)
+        weight_sum(1, 1)
+        round_w1(gpsimd_round, 2, 2, 0, 0, 2)
+        deal_wg_words(wg_high)
+        round_w1(scalar_round, 2, 2, 1, 0, 1)
+        round_w1(scalar_round, 2, 2, 1, 1, 2)
+        pick_first(0)
+        pick_second(0)
+        gate_sum(3, 1)
+        gate_sum(3, 0)
+        turn(0)
 
-        for i in range(3):
-            features(i, 0)
-            features(i, 1)
-            quantise_tile(i + 1)
-            if i == 0:
-                gate_sums(1)
-            both_weight_sums(i + 1)
-            if i == 0:
-                round_tile(2)
-                deal_wg_words(wg_scales_dealt)
-                gate_sums(2)
-                round_tile(3)
-                gate_sums(3)
-            if i == 1:
-                gate_sums(4)
-                gate_sums(5)
-                round_tile(6, [0])
-            if i == 2:
-                round_tile(4)
-                round_tile(5)
-                round_tile(6, [1])
-            pick_natural(i)
-        for i in (0, 1):
-            turn(i, *picked[i])
-
-        features(3, 0)
+        features(1, 0)
+        features(1, 1)
+        quantise_w1(2, 2)
+        weight_sum(3, 1)
+        weight_sum(2, 0)
+        weight_sum(2, 1)
+        weight_sum(3, 0)
+        round_dealt(True, 4, 0)
+        round_dealt(True, 5, 0)
         features(3, 1)
-        quantise_tile(4)
-        quantise_tile(5)
-        weight_sums(4, 0)
-        weight_sums(5, 1)
-        weight_sums(4, 1)
-        weight_sums(5, 0)
-        round_tile(7)
-        features(5, 1)
-        gate_sums(6)
-        pick_natural(3)
+        round_dealt(False, 4, 1)
+        round_dealt(False, 5, 1)
+        gate_sum(4, 1)
+        gate_sum(4, 0)
+        pick_first(1)
+        pick_second(1)
+        turn(1)
+        gate_sum(5, 1)
+        gate_sum(5, 0)
 
-        features(4, 0)
+        features(2, 0)
+        features(2, 1)
+        features(3, 0)
+        pick_first(2)
+        quantise_w1(4, 2)
+        weight_sum(4, 1)
+        weight_sum(4, 0)
+        weight_sum(5, 1)
+        weight_sum(5, 0)
+        gate_sum(6, 1)
+        gate_sum(6, 0)
+        round_dealt(True, 6, 0)
+        round_dealt(True, 7, 0)
         features(4, 1)
-        features(5, 0)
-        quantise_tile(6)
-        quantise_tile(7)
-        w2_begun = [begin_w2(b) for b in range(2)]
-        weight_sums(6, 1)
-        weight_sums(7, 1)
+        features(5, 1)
+        round_dealt(False, 6, 1)
+        round_dealt(False, 7, 1)
+        pick_second(2)
+        turn(2)
+        gate_sum(7, 1)
+        gate_sum(7, 0)
+
+        pick_first(3)
+        features(4, 0)
+        pick_second(3)
+        turn(3)
+        quantise_w1(6, 2)
+        weight_sum(6, 1)
+        weight_sum(7, 1)
+        weight_sum(6, 0)
+        weight_sum(7, 0)
+        round_w2(gpsimd_round, 0, 0, W2_SHARED)
+        z_first = turn_back()
+
+        pick_first(4)
+        pick_second(4)
         features(6, 1)
-        gate_sums(7)
         features(7, 1)
-        weight_sums(6, 0)
-        weight_sums(7, 0)
-        turn(2, *picked[2])
-        turn(3, *picked[3])
-        z_natural = turn_z_back()
-        w2_rounded = [finish_w2(b, w2_begun[b]) for b in range(2)]
-        pick_plain(4, picks("first_4", FIRST_AT[4]), picks("second_4", SECOND_AT[4]))
-        second_5 = placed("second_5", [P, SECOND_5[1] * KIB // 4], F32, SECOND_5[0])
-        pick_plain(5, picks("first_5", None), second_5[:, 0:PAIRS])
-        low = placed("differences_low", [P, 2, PAIRS], F32, LAST_SUMS_AT)
-        for t in range(2):
-            nc.gpsimd.tensor_tensor(low[:, t, :], *picked[NATURAL + t], SUB)
+        subtract(4)
+        features(5, 0)
+        for first in range(W2_SHARED, N, P):
+            round_w2(scalar_round, 0, first, first + P)
+        for first in range(0, N, P):
+            round_w2(scalar_round, 1, first, first + P)
+        pick_first(5)
+        pick_second(5)
+        subtract(5)
         for h, (j0, width) in enumerate(PIECES):
             round_differences(nc.scalar.copy, h, 0, low[:, :, j0 : j0 + width])
 
-        def pick_seconds(h):
-            j0, width = PIECES[h]
-            entries = slice(j0 // 16, (j0 + width) // 16)
-            seconds = []
-            for t, i in enumerate((6, 7)):
-                start, span = LAST_SECONDS[h][t]
-                tile = placed("second_%d_%d" % (i, h), [P, span * KIB // 4], F32, start)
-                seconds.append(tile[:, 0:width])
-                nc.vector.tensor_copy(seconds[t], windows[i][:].indirect(pos2_t[:, entries]))
-            return seconds
-
         features(6, 0)
         features(7, 0)
-        seconds = {h: pick_seconds(h) for h in range(2)}
-        w2_q = {}
-        for b in range(2):
-            w2_q[b] = quantise("w2_%d" % b, w2_rounded[b], N, work, (SECOND_5[0] + 2 + 2 * b) * KIB)
-        quantise_z_natural(z_natural)
-        for h in range(len(PIECES)):
-            open_scores(h)
-        last = len(PIECES) - 1
+        pick_second(6)
+        pick_second(7)
+        quantise_w2(0)
+        z_codes, z_scales = quantise("z_0", z_first, PAIRS, Z_CODES_AT)
         for h, (j0, width) in enumerate(PIECES):
-            if h == last:
-                seconds[h] = pick_seconds(h)
-            start, span = HIGH[h]
-            high = placed("differences_high_%d" % h, [P, span * KIB // (4 * width), width], F32, start)[:, 0:2, :]
-            entries = slice(j0 // 16, (j0 + width) // 16)
-            for t, i in enumerate((6, 7)):
-                firsts = windows[i][:].indirect(pos1_t[:, entries])
-                nc.vector.tensor_tensor(high[:, t, :], firsts, seconds[h][t], SUB)
-            round_differences(nc.vector.tensor_copy if h == last else nc.scalar.copy, h, 1, high)
-            quantise_z_dealt(h)
-            close_scores(h, 1 if h == last else 2)
+            z_q[(0, h)] = (z_codes[:, j0 : j0 + width], z_scales[:, j0 : j0 + width])
+            open_scores(h)
+        pick_last_differences(0)
+        quantise_w2(1)
+        quantise_piece(0)
+        pick_last_differences(1)
+        close_scores(0, 2)
+        quantise_piece(1)
+        pick_last_differences(2)
+        close_scores(1, 2)
+        quantise_piece(2)
+        close_scores(2, 1)

@@ -25,13 +25,12 @@ BANK = 512
 NATURAL = 4
 SHARED = (3, 4, 5, 6, 7)
 PIECES = [(0, 256), (256, 128), (384, 128)]
-W2_SHARED = 128
 
-GATE_BANK = [(4, 5), (6, 7), (4, 5), (7, 6), (7, 5), (5, 4), (5, 4), (5, 4)]
+GATE_BANK = [(4, 5), (6, 7), (4, 5), (7, 6), (7, 5), (5, 4), (1, 4), (6, 4)]
 SUM_BANK = [(0, 1), (2, 3), (0, 1), (2, 4), (0, 6), (1, 7), (2, 6), (0, 7)]
 TURN_BANK = [1, 3, 3, 3]
-BACK_BANK = [4, 5]
-SCORE_BANKS = [(6, 7), (4, 5), (0, 1, 2, 3)]
+BACK_BANK = [6, 0]
+SCORE_BANKS = [(4, 5), (6, 7), (0, 1, 2, 3)]
 
 TABLE_AT = [26, 49]
 TABLE_SPAN = [(0, 48.5), (49, 66.5)]
@@ -42,22 +41,20 @@ W1_SPAN = {0: 4, 1: 4, 2: 8, 4: 8}
 W2_AT = [49, 57]
 WG_AT = {2: 3.5, 4: 10.5}
 WG_DEALT_AT = 74
-BIAS_AT = 65
 IDENT_AT = 206
-ROUNDED = {1: (72, 76, 78), 2: (76, 76, 80), 4: (76, 76, 86.0625), 6: (86, 86, 98)}
+ROUNDED = {1: (72, 76, 78), 2: (76, 76, 80), 4: (76, 76, 86.0625), 6: (86, 86, 98.0625)}
 FIRST_ROUNDED_AT = 76
-CODES_AT = {1: 6.5, 2: 11.5, 4: 144, 6: 148}
+CODES_AT = {1: 6.5, 2: 11.5, 4: 144, 6: 146}
 FIRST_CODES_AT = 65.5
-WINDOW_AT = [207, 108, 207, 120, 162, 100, 104, 116]
+WINDOW_AT = [207, 108, 207, 120, 162, 98, 104, 116]
 GATE_AT = [6.5, 12.5, 44.5, 40.5] + [128 + 4 * i for i in range(4)]
-SHARED_AT = {3: (144, 2), 4: (146, 2), 5: (148, 6), 6: (154, 2), 7: (166, 2)}
-FIRST_AT = [158, 36.5, 11.5, 82, 150, 168]
-SECOND_AT = [(72, 2), (38.5, 2), (80, 2), (84, 2), (152, 2), (172, 8), (182, 2), (196, 2)]
-W2_CODES_AT = [174, 176]
-Z_CODES_AT = 172
-HIGH_AT = [(178, 4), (180, 1), (181, 1)]
-LOW_AT = 156
-W2_ROUNDED_AT = [90, 94]
+SHARED_AT = {3: (144, 2), 4: (146, 4), 5: (150, 2), 6: (152, 2), 7: (166, 2)}
+FIRST_AT = [158, 36.5, 11.5, 82]
+SECOND_AT = [72, 38.5, 80, 84, 148, 154, 198, 196]
+W2_CODES_AT = [57, 59]
+Z_CODES_AT = [61, 70]
+DIFFERENCES_AT = [(62, 10), (66, 2), (68, 2)]
+W2_ROUNDED_AT = [170, 94]
 Z_TURNED_AT = 184
 Z_ROUNDED_AT = 188
 Z_DEALT_AT = 192
@@ -295,8 +292,7 @@ def tile_list_pairwise_document_ranking_kernel(
             nc.vector.tensor_copy(firsts[i], windows[i][:, 0:S].indirect(pos1_t[:]))
 
         def pick_second(i):
-            start, span = SECOND_AT[i]
-            seconds[i] = placed("second_%d" % i, [P, span * KIB // 4], F32, start)[:, 0:PAIRS]
+            seconds[i] = placed("second_%d" % i, [P, PAIRS], F32, SECOND_AT[i])[:]
             if i < NATURAL:
                 nc.vector.tensor_scalar(seconds[i], windows[i][:].indirect(pos2_t[:]), -1.0, 0.0, MULT, ADD)
             else:
@@ -333,28 +329,34 @@ def tile_list_pairwise_document_ranking_kernel(
                 )
             return rounded[:].rearrange("p j t -> p (j t)")
 
+        def quantise_first_pass(g):
+            half = PAIRS // 2
+            rounded = z_first[:, 4 * half * g : 4 * half * (g + 1)]
+            codes, scales = quantise("z_0_%d" % g, rounded, half, Z_CODES_AT[g])
+            for h, (j0, width) in enumerate(PIECES):
+                if j0 // half == g:
+                    cols = slice(j0 - half * g, j0 - half * g + width)
+                    z_q[(0, h)] = (codes[:, cols], scales[:, cols])
+
         z_dealt = [
             placed("z_rounded_1_%d" % h, [P, width, 4], BF16, Z_DEALT_AT + j0 // P)
             for h, (j0, width) in enumerate(PIECES)
         ]
-        low = placed("differences_low", [P, 2, PAIRS], F32, LOW_AT)
 
-        def subtract(i):
-            nc.gpsimd.tensor_tensor(low[:, i - NATURAL, :], firsts[i], seconds[i], SUB)
-
-        def round_differences(copy, h, u, differences):
-            copy(out=z_dealt[h][:, :, 2 * u : 2 * u + 2], in_=differences.rearrange("p t j -> p j t"))
-
-        def pick_last_differences(h):
+        def pick_differences(h):
             j0, width = PIECES[h]
-            start, span = HIGH_AT[h]
-            high = placed("differences_high_%d" % h, [P, span * KIB // (4 * width), width], F32, start)[:, 0:2, :]
+            start, span = DIFFERENCES_AT[h]
+            rows = span * KIB // (4 * width)
+            differences = placed("differences_%d" % h, [P, rows, width], F32, start)[:, 0:4, :]
             entries = slice(j0 // 16, (j0 + width) // 16)
-            for t in range(2):
-                firsts_now = windows[6 + t][:].indirect(pos1_t[:, entries])
-                nc.vector.tensor_tensor(high[:, t, :], firsts_now, seconds[6 + t][:, j0 : j0 + width], SUB)
-            last = h == len(PIECES) - 1
-            round_differences(nc.vector.tensor_copy if last else nc.scalar.copy, h, 1, high)
+            for t in range(4):
+                picked = windows[NATURAL + t][:].indirect(pos1_t[:, entries])
+                nc.vector.tensor_tensor(differences[:, t, :], picked, seconds[NATURAL + t][:, j0 : j0 + width], SUB)
+            copy = nc.vector.tensor_copy if h > 0 else nc.scalar.copy
+            copy(
+                out=z_dealt[h][:].rearrange("p (g i) t -> p g t i", i=2),
+                in_=differences.rearrange("p t (g i) -> p g t i", i=2),
+            )
 
         def quantise_piece(h):
             codes, scales = quantise("z_1_%d" % h, z_dealt[h][:].rearrange("p j t -> p (j t)"), PIECES[h][1])
@@ -454,7 +456,7 @@ def tile_list_pairwise_document_ranking_kernel(
         gather_second_pass(1)
         load_w2(0)
         load_w2(1)
-        c_t = placed("c_t", [P, N // P], F32, BIAS_AT)
+        c_t = keep.tile([P, N // P], F32, name="c_t")
         with nc.allow_non_contiguous_dma(reason="one bias value for each partition"):
             nc.sync.dma_start(out=c_t[:], in_=c.rearrange("(t p) -> p t", p=P))
 
@@ -498,7 +500,7 @@ def tile_list_pairwise_document_ranking_kernel(
         round_dealt(True, 5, 0)
         features(3, 1)
         round_dealt(False, 4, 1)
-        round_dealt(False, 5, 1)
+        round_dealt(True, 5, 1)
         gate_sum(4, 1)
         gate_sum(4, 0)
         pick_first(1)
@@ -515,64 +517,59 @@ def tile_list_pairwise_document_ranking_kernel(
         weight_sum(4, 1)
         weight_sum(4, 0)
         weight_sum(5, 1)
-        weight_sum(5, 0)
         gate_sum(6, 1)
-        gate_sum(6, 0)
+        weight_sum(5, 0)
         round_dealt(True, 6, 0)
         round_dealt(True, 7, 0)
         features(4, 1)
-        features(5, 1)
         round_dealt(False, 6, 1)
-        round_dealt(False, 7, 1)
+        round_dealt(True, 7, 1)
         pick_second(2)
         turn(2)
         gate_sum(7, 1)
-        gate_sum(7, 0)
 
         pick_first(3)
-        features(4, 0)
         pick_second(3)
+        features(4, 0)
         turn(3)
         quantise_w1(6, 2)
+        features(5, 1)
+        features(5, 0)
         weight_sum(6, 1)
         weight_sum(7, 1)
+        gate_sum(6, 0)
         weight_sum(6, 0)
+        gate_sum(7, 0)
         weight_sum(7, 0)
-        round_w2(gpsimd_round, 0, 0, W2_SHARED)
-        z_first = turn_back()
-
-        pick_first(4)
-        pick_second(4)
+        round_w2(gpsimd_round, 1, 0, P)
         features(6, 1)
         features(7, 1)
-        subtract(4)
-        features(5, 0)
-        for first in range(W2_SHARED, N, P):
-            round_w2(scalar_round, 0, first, first + P)
+        round_w2(gpsimd_round, 1, P, 2 * P)
         for first in range(0, N, P):
+            round_w2(scalar_round, 0, first, first + P)
+        for first in range(2 * P, N, P):
             round_w2(scalar_round, 1, first, first + P)
-        pick_first(5)
-        pick_second(5)
-        subtract(5)
-        for h, (j0, width) in enumerate(PIECES):
-            round_differences(nc.scalar.copy, h, 0, low[:, :, j0 : j0 + width])
 
+        pick_second(4)
+        pick_second(5)
         features(6, 0)
         features(7, 0)
+        z_first = turn_back()
         pick_second(6)
         pick_second(7)
+        pick_differences(0)
         quantise_w2(0)
-        z_codes, z_scales = quantise("z_0", z_first, PAIRS, Z_CODES_AT)
-        for h, (j0, width) in enumerate(PIECES):
-            z_q[(0, h)] = (z_codes[:, j0 : j0 + width], z_scales[:, j0 : j0 + width])
-            open_scores(h)
-        pick_last_differences(0)
+        quantise_first_pass(0)
+        open_scores(0)
         quantise_w2(1)
         quantise_piece(0)
-        pick_last_differences(1)
+        pick_differences(1)
+        quantise_first_pass(1)
         close_scores(0, 2)
+        open_scores(1)
+        open_scores(2)
         quantise_piece(1)
-        pick_last_differences(2)
+        pick_differences(2)
         close_scores(1, 2)
         quantise_piece(2)
         close_scores(2, 1)

@@ -33,13 +33,13 @@ BACK_BANK = [6, 0]
 SCORE_BANKS = [(4, 5), (6, 7), (0, 1, 2, 3)]
 
 TABLE_AT = [26, 49]
-TABLE_SPAN = [(0, 48.5), (49, 66.5)]
+TABLE_SPAN = [(10.5, 48.5), (49, 66.5)]
 TABLE_CUT = [T // 4, 3 * T // 4]
 TABLE_SCALES_AT, TABLE_SCALES_SPAN = 200, 7
-W1_AT = {0: 4.5, 1: 10.5, 2: 32.5, 4: 16.5}
+W1_AT = {0: (4.5, 6.5), 1: (0, 12.5), 2: (32.5, 36.5), 4: (16.5, 24.5)}
 W1_SPAN = {0: 4, 1: 4, 2: 8, 4: 8}
-W2_AT = [49, 57]
-WG_AT = {2: 3.5, 4: 10.5}
+W2_AT = {(0, 0): 61, (0, 256): 170, (1, 0): 49}
+WG_AT = {4: 10.5}
 WG_DEALT_AT = 74
 IDENT_AT = 206
 ROUNDED = {1: (72, 76, 78), 2: (76, 76, 80), 4: (76, 76, 86.0625), 6: (86, 86, 98.0625)}
@@ -47,17 +47,18 @@ FIRST_ROUNDED_AT = 76
 CODES_AT = {1: 6.5, 2: 11.5, 4: 144, 6: 146}
 FIRST_CODES_AT = 65.5
 WINDOW_AT = [207, 108, 207, 120, 162, 98, 104, 116]
-GATE_AT = [6.5, 12.5, 44.5, 40.5] + [128 + 4 * i for i in range(4)]
-SHARED_AT = {3: (144, 2), 4: (146, 4), 5: (150, 2), 6: (152, 2), 7: (166, 2)}
+GATE_AT = [6.5, 12.5, 44.5, 40.5] + [128, 132, 136, 190]
+SHARED_AT = {3: (144, 2), 4: (146, 4), 5: (150, 2), 6: (152, 2), 7: (188, 2)}
 FIRST_AT = [158, 36.5, 11.5, 82]
 SECOND_AT = [72, 38.5, 80, 84, 148, 154, 198, 196]
-W2_CODES_AT = [57, 59]
-Z_CODES_AT = [61, 70]
-DIFFERENCES_AT = [(62, 10), (66, 2), (68, 2)]
-W2_ROUNDED_AT = [170, 94]
-Z_TURNED_AT = 184
-Z_ROUNDED_AT = 188
-Z_DEALT_AT = 192
+LATE_CODES_AT = 191
+SECOND_Z_CODES_AT = 187.5
+DIFFERENCES_AT = (180.5, 10)
+LATE_DIFFERENCES_AT = 184.5
+W2_ROUNDED_AT = {(0, 0): 94, (0, 256): 174, (1, 0): 136}
+Z_TURNED_AT = 57
+Z_ROUNDED_AT = 66.5
+Z_DEALT_AT = 140
 RESULT_AT = 108
 
 
@@ -83,7 +84,7 @@ def tile_list_pairwise_document_ranking_kernel(
         tab = []
         for a, (start, end) in enumerate(TABLE_SPAN):
             span = placed("tab%d" % a, [P, int((end - start) * KIB) // 4], I32, start)
-            skip = (TABLE_AT[a] - start) * KIB // 4
+            skip = int((TABLE_AT[a] - start) * KIB) // 4
             tab.append(span[:, skip : skip + T])
 
         def load_table(a, first, last):
@@ -105,6 +106,13 @@ def tile_list_pairwise_document_ranking_kernel(
                 for t in range(count):
                     gate_w[(first + t, a)] = words[:, a, 2 * P * t : 2 * P * (t + 1)]
             return words
+
+        def load_wg_pass(a, first, count):
+            words = keep.tile([P, 2 * P * count], U8, name="wg_%d_%d" % (a, first), align_bytes=64)
+            cols = slice(first * P // 2, (first + count) * P // 2)
+            nc.sync.dma_start(out=words[:].bitcast(I32), in_=wg_words[a].bitcast(I32)[:, cols])
+            for t in range(count):
+                gate_w[(first + t, a)] = words[:, 2 * P * t : 2 * P * (t + 1)]
 
         def deal_wg_scales(plane):
             scales = keep.tile([P, 2, 4, P], U8, name="wg_sc_dealt", align_bytes=64)
@@ -139,24 +147,26 @@ def tile_list_pairwise_document_ranking_kernel(
 
         w1_raw = {}
 
-        def load_w1(first, count):
-            for a in range(2):
+        def load_w1(first, count, passes=(0, 1)):
+            for a in passes:
                 rows = W1_SPAN[first] * 2 // count if a == 1 else 4
-                raw = placed("w1_raw_%d_%d" % (first, a), [P, rows, count * P], F32, W1_AT[first] + 2 * count * a)
+                raw = placed("w1_raw_%d_%d" % (first, a), [P, rows, count * P], F32, W1_AT[first][a])
                 cols = w1[512 * a : 512 * (a + 1), first * P : (first + count) * P]
                 nc.sync.dma_start(out=raw[:, 0:4, :], in_=cols.rearrange("(p j) c -> p j c", j=4))
                 w1_raw[(first, a)] = raw[:, 0:4, :]
 
         w2_raw = {}
 
-        def load_w2(b):
-            w2_raw[b] = placed("w2_raw%d" % b, [P, 4, N], F32, W2_AT[b])
-            if b == 0:
-                nc.sync.dma_start(out=w2_raw[b][:], in_=w2[0:512, :].rearrange("(p t) n -> p t n", t=4))
-            else:
-                rows = w2[512:1024, :].rearrange("(q t e) n -> t q e n", t=4, e=8)
-                for t in range(4):
-                    nc.sync.dma_start(out=w2_raw[b][:, t, :], in_=rows[t])
+        def load_w2_natural(first, span):
+            raw = placed("w2_raw_0_%d" % first, [P, span, N // 2], F32, W2_AT[(0, first)])[:, 0:4, :]
+            nc.sync.dma_start(out=raw, in_=w2[0:512, first : first + N // 2].rearrange("(p t) n -> p t n", t=4))
+            w2_raw[(0, first)] = raw
+
+        def load_w2_dealt():
+            w2_raw[(1, 0)] = placed("w2_raw_1", [P, 4, N], F32, W2_AT[(1, 0)])[:]
+            rows = w2[512:1024, :].rearrange("(q t e) n -> t q e n", t=4, e=8)
+            for t in range(4):
+                nc.sync.dma_start(out=w2_raw[(1, 0)][:, t, :], in_=rows[t])
 
         v_words = {}
 
@@ -172,8 +182,10 @@ def tile_list_pairwise_document_ranking_kernel(
             nc.vector.tensor_copy(words[:], tab[1][:, 0:T].bitcast(U32).indirect(entries))
             v_words[(1, d)] = words[:]
 
-        def quantise(name, rounded, width, kib=None):
-            if kib is None:
+        def quantise(name, rounded, width, kib=None, codes=None):
+            if codes is not None:
+                pass
+            elif kib is None:
                 codes = keep.tile([P, width], U32, name="codes_" + name, align_bytes=64)
             else:
                 codes = placed("codes_" + name, [P, width], U32, kib)
@@ -314,6 +326,7 @@ def tile_list_pairwise_document_ranking_kernel(
             )
 
         z_q = {}
+        late_codes = placed("late_codes", [P, 2 * N + PAIRS // 2], U32, LATE_CODES_AT)
 
         def turn_back():
             words = z_turned[:].bitcast(F32)
@@ -332,7 +345,10 @@ def tile_list_pairwise_document_ranking_kernel(
         def quantise_first_pass(g):
             half = PAIRS // 2
             rounded = z_first[:, 4 * half * g : 4 * half * (g + 1)]
-            codes, scales = quantise("z_0_%d" % g, rounded, half, Z_CODES_AT[g])
+            if g == 0:
+                codes, scales = quantise("z_0_0", rounded, half, codes=late_codes[:, 2 * N : 2 * N + half])
+            else:
+                codes, scales = quantise("z_0_1", rounded, half, SECOND_Z_CODES_AT)
             for h, (j0, width) in enumerate(PIECES):
                 if j0 // half == g:
                     cols = slice(j0 - half * g, j0 - half * g + width)
@@ -342,17 +358,21 @@ def tile_list_pairwise_document_ranking_kernel(
             placed("z_rounded_1_%d" % h, [P, width, 4], BF16, Z_DEALT_AT + j0 // P)
             for h, (j0, width) in enumerate(PIECES)
         ]
+        late_differences = placed("late_differences", [P, 6, P], F32, LATE_DIFFERENCES_AT)
 
         def pick_differences(h):
             j0, width = PIECES[h]
-            start, span = DIFFERENCES_AT[h]
-            rows = span * KIB // (4 * width)
-            differences = placed("differences_%d" % h, [P, rows, width], F32, start)[:, 0:4, :]
+            if h == 0:
+                start, span = DIFFERENCES_AT
+                rows = span * KIB // (4 * width)
+                differences = placed("differences", [P, rows, width], F32, start)[:, 0:4, :]
+            else:
+                differences = late_differences[:, 4 - 2 * h : 8 - 2 * h, :]
             entries = slice(j0 // 16, (j0 + width) // 16)
             for t in range(4):
                 picked = windows[NATURAL + t][:].indirect(pos1_t[:, entries])
                 nc.vector.tensor_tensor(differences[:, t, :], picked, seconds[NATURAL + t][:, j0 : j0 + width], SUB)
-            copy = nc.vector.tensor_copy if h > 0 else nc.scalar.copy
+            copy = nc.vector.tensor_copy if h == len(PIECES) - 1 else nc.scalar.copy
             copy(
                 out=z_dealt[h][:].rearrange("p (g i) t -> p g t i", i=2),
                 in_=differences.rearrange("p t (g i) -> p g t i", i=2),
@@ -365,24 +385,29 @@ def tile_list_pairwise_document_ranking_kernel(
         w2_rounded = {}
         w2_q = {}
 
-        def round_w2(rounder, b, lo, hi):
-            if b not in w2_rounded:
-                w2_rounded[b] = placed("w2_rounded%d" % b, [P, N, 4], BF16, W2_ROUNDED_AT[b])
-            rounder(w2_rounded[b][:, lo:hi, :], w2_raw[b][:, :, lo:hi])
+        def round_w2(rounder, b, first, width, lo):
+            if (b, first) not in w2_rounded:
+                at = W2_ROUNDED_AT[(b, first)]
+                w2_rounded[(b, first)] = placed("w2_rounded_%d_%d" % (b, first), [P, width, 4], BF16, at)
+            rounder(w2_rounded[(b, first)][:, lo : lo + P, :], w2_raw[(b, first)][:, :, lo : lo + P])
 
-        def quantise_w2(b):
-            w2_q[b] = quantise("w2_%d" % b, w2_rounded[b][:].rearrange("p n t -> p (n t)"), N, W2_CODES_AT[b])
+        def quantise_w2(b, first, width):
+            flat = w2_rounded[(b, first)][:].rearrange("p n t -> p (n t)")
+            place = late_codes[:, N * b + first : N * b + first + width]
+            codes, scales = quantise("w2_%d_%d" % (b, first), flat, width, codes=place)
+            for lo in range(0, width, P):
+                w2_q[(b, (first + lo) // P)] = (codes[:, lo : lo + P], scales[:, lo : lo + P])
 
         y_banks = {}
 
         def second_stage_pass(h, nt, b):
-            w_codes, w_scales = w2_q[b]
+            w_codes, w_scales = w2_q[(b, nt)]
             z_codes, z_scales = z_q[(b, h)]
             shared = N // P // len(SCORE_BANKS[h])
             nc.tensor.matmul_mx(
                 out=y_banks[(h, nt)],
-                lhsT=w_codes[:, P * nt : P * (nt + 1)].bitcast(FP8X4),
-                lhsT_scale=w_scales[:, P * nt : P * (nt + 1)],
+                lhsT=w_codes.bitcast(FP8X4),
+                lhsT_scale=w_scales,
                 rhs=z_codes.bitcast(FP8X4),
                 rhs_scale=z_scales,
                 start=(b == 0 and nt % shared == 0),
@@ -421,7 +446,8 @@ def tile_list_pairwise_document_ranking_kernel(
         load_table(0, 0, TABLE_CUT[0])
         nc.sync.dma_start(pos1_t[:], pos1)
         nc.sync.dma_start(pos2_t[:], pos2)
-        load_wg(0, 2)
+        load_wg_pass(0, 0, 2)
+        load_wg_pass(1, 0, 1)
         for a in range(2):
             nc.sync.dma_start(out=tab_sc[4 * a : P : 8, 0:T].bitcast(I32), in_=tab_scales[a].bitcast(I32))
         load_table(0, TABLE_CUT[0], T)
@@ -443,10 +469,13 @@ def tile_list_pairwise_document_ranking_kernel(
         gather_first_pass()
         load_w1(0, 1)
         load_w1(1, 1)
-        load_wg(2, 2)
+        load_wg_pass(1, 1, 3)
+        load_wg_pass(0, 2, 2)
         load_w1(2, 2)
         wg_high = load_wg(4, 4)
-        load_w1(4, 4)
+        load_w1(4, 4, [0])
+        load_w2_natural(N // 2, 4)
+        load_w1(4, 4, [1])
         ident = placed("ident", [P, P], F32, IDENT_AT)
         make_identity(nc, ident[:])
         for i in range(2):
@@ -454,8 +483,8 @@ def tile_list_pairwise_document_ranking_kernel(
                 gate_pass(i, d, 0)
         gather_second_pass(0)
         gather_second_pass(1)
-        load_w2(0)
-        load_w2(1)
+        load_w2_natural(0, 4)
+        load_w2_dealt()
         c_t = keep.tile([P, N // P], F32, name="c_t")
         with nc.allow_non_contiguous_dma(reason="one bias value for each partition"):
             nc.sync.dma_start(out=c_t[:], in_=c.rearrange("(t p) -> p t", p=P))
@@ -496,10 +525,10 @@ def tile_list_pairwise_document_ranking_kernel(
         weight_sum(2, 0)
         weight_sum(2, 1)
         weight_sum(3, 0)
-        round_dealt(True, 4, 0)
+        round_dealt(False, 4, 0)
         round_dealt(True, 5, 0)
         features(3, 1)
-        round_dealt(False, 4, 1)
+        round_dealt(True, 4, 1)
         round_dealt(True, 5, 1)
         gate_sum(4, 1)
         gate_sum(4, 0)
@@ -508,6 +537,8 @@ def tile_list_pairwise_document_ranking_kernel(
         turn(1)
         gate_sum(5, 1)
         gate_sum(5, 0)
+        for lo in range(0, N // 2, P):
+            round_w2(scalar_round, 0, N // 2, N // 2, lo)
 
         features(2, 0)
         features(2, 1)
@@ -541,27 +572,26 @@ def tile_list_pairwise_document_ranking_kernel(
         weight_sum(6, 0)
         gate_sum(7, 0)
         weight_sum(7, 0)
-        round_w2(gpsimd_round, 1, 0, P)
+        round_w2(gpsimd_round, 0, 0, N // 2, 0)
         features(6, 1)
+        round_w2(gpsimd_round, 0, 0, N // 2, P)
         features(7, 1)
-        round_w2(gpsimd_round, 1, P, 2 * P)
-        for first in range(0, N, P):
-            round_w2(scalar_round, 0, first, first + P)
-        for first in range(2 * P, N, P):
-            round_w2(scalar_round, 1, first, first + P)
 
         pick_second(4)
         pick_second(5)
         features(6, 0)
         features(7, 0)
         z_first = turn_back()
+        for lo in range(0, N, P):
+            round_w2(scalar_round, 1, 0, N, lo)
         pick_second(6)
         pick_second(7)
         pick_differences(0)
-        quantise_w2(0)
+        quantise_w2(0, 0, N // 2)
+        quantise_w2(0, N // 2, N // 2)
         quantise_first_pass(0)
         open_scores(0)
-        quantise_w2(1)
+        quantise_w2(1, 0, N)
         quantise_piece(0)
         pick_differences(1)
         quantise_first_pass(1)

@@ -53,8 +53,8 @@ FIRST_AT = [158, 36.5, 11.5, 82]
 SECOND_AT = [72, 38.5, 80, 84, 148, 154, 198, 196]
 LATE_CODES_AT = 191
 SECOND_Z_CODES_AT = 187.5
-DIFFERENCES_AT = (180.5, 10)
-LATE_DIFFERENCES_AT = 184.5
+DIFFERENCES_AT = (179.5, 11)
+LATE_DIFFERENCES_AT = 183.5
 W2_ROUNDED_AT = {(0, 0): 94, (0, 256): 174, (1, 0): 136}
 Z_TURNED_AT = 57
 Z_ROUNDED_AT = 66.5
@@ -358,7 +358,7 @@ def tile_list_pairwise_document_ranking_kernel(
             placed("z_rounded_1_%d" % h, [P, width, 4], BF16, Z_DEALT_AT + j0 // P)
             for h, (j0, width) in enumerate(PIECES)
         ]
-        late_differences = placed("late_differences", [P, 6, P], F32, LATE_DIFFERENCES_AT)
+        late_differences = placed("late_differences", [P, 8, P], F32, LATE_DIFFERENCES_AT)
 
         def pick_differences(h):
             j0, width = PIECES[h]
@@ -367,12 +367,12 @@ def tile_list_pairwise_document_ranking_kernel(
                 rows = span * KIB // (4 * width)
                 differences = placed("differences", [P, rows, width], F32, start)[:, 0:4, :]
             else:
-                differences = late_differences[:, 4 - 2 * h : 8 - 2 * h, :]
+                differences = late_differences[:, 4 * h - 4 : 4 * h, :]
             entries = slice(j0 // 16, (j0 + width) // 16)
             for t in range(4):
                 picked = windows[NATURAL + t][:].indirect(pos1_t[:, entries])
                 nc.vector.tensor_tensor(differences[:, t, :], picked, seconds[NATURAL + t][:, j0 : j0 + width], SUB)
-            copy = nc.vector.tensor_copy if h == len(PIECES) - 1 else nc.scalar.copy
+            copy = nc.vector.tensor_copy if h > 0 else nc.scalar.copy
             copy(
                 out=z_dealt[h][:].rearrange("p (g i) t -> p g t i", i=2),
                 in_=differences.rearrange("p t (g i) -> p g t i", i=2),
@@ -444,13 +444,13 @@ def tile_list_pairwise_document_ranking_kernel(
 
         nc.sync.dma_start(offs_t[:], offs)
         load_table(0, 0, TABLE_CUT[0])
-        nc.sync.dma_start(pos1_t[:], pos1)
-        nc.sync.dma_start(pos2_t[:], pos2)
         load_wg_pass(0, 0, 2)
         load_wg_pass(1, 0, 1)
         for a in range(2):
             nc.sync.dma_start(out=tab_sc[4 * a : P : 8, 0:T].bitcast(I32), in_=tab_scales[a].bitcast(I32))
         load_table(0, TABLE_CUT[0], T)
+        nc.sync.dma_start(pos1_t[:], pos1)
+        nc.sync.dma_start(pos2_t[:], pos2)
         load_table(1, 0, TABLE_CUT[1])
         load_wg_scales(nc.gpsimd, wg_sc, 0, 8)
         deal_wg_scales(wg_sc)

@@ -23,11 +23,11 @@ P = 128
 KIB = 1024
 BANK = 512
 NATURAL = 4
-SHARED = (3, 4, 5, 6, 7)
+SHARED = (3, 4, 6, 7)
 PIECES = [(0, 256), (256, 128), (384, 128)]
 
 GATE_BANK = [(4, 5), (6, 7), (4, 5), (7, 6), (7, 5), (5, 4), (1, 4), (6, 4)]
-SUM_BANK = [(0, 1), (2, 3), (0, 1), (2, 4), (0, 6), (1, 7), (2, 6), (0, 7)]
+SUM_BANK = [(0, 1), (2, 3), (0, 1), (2, 4), (0, 6), (1, 7), (2, 6), (0, 5)]
 TURN_BANK = [1, 3, 3, 3]
 BACK_BANK = [6, 0]
 SCORE_BANKS = [(4, 5), (6, 7), (0, 1, 2, 3)]
@@ -38,7 +38,7 @@ TABLE_CUT = [T // 4, 3 * T // 4]
 TABLE_SCALES_AT, TABLE_SCALES_SPAN = 200, 7
 W1_AT = {0: (4.5, 6.5), 1: (0, 12.5), 2: (32.5, 36.5), 4: (16.5, 24.5)}
 W1_SPAN = {0: 4, 1: 4, 2: 8, 4: 8}
-W2_AT = {(0, 0): 61, (0, 256): 170, (1, 0): 49}
+W2_AT = {(0, 0): 168, (1, 0): 49}
 WG_AT = {4: 10.5}
 WG_DEALT_AT = 74
 IDENT_AT = 206
@@ -55,7 +55,7 @@ LATE_CODES_AT = 191
 SECOND_Z_CODES_AT = 187.5
 DIFFERENCES_AT = (179.5, 11)
 LATE_DIFFERENCES_AT = 183.5
-W2_ROUNDED_AT = {(0, 0): 94, (0, 256): 174, (1, 0): 136}
+W2_ROUNDED_AT = {(0, 0): 94, (1, 0): 136}
 Z_TURNED_AT = 57
 Z_ROUNDED_AT = 66.5
 Z_DEALT_AT = 140
@@ -157,10 +157,9 @@ def tile_list_pairwise_document_ranking_kernel(
 
         w2_raw = {}
 
-        def load_w2_natural(first, span):
-            raw = placed("w2_raw_0_%d" % first, [P, span, N // 2], F32, W2_AT[(0, first)])[:, 0:4, :]
-            nc.sync.dma_start(out=raw, in_=w2[0:512, first : first + N // 2].rearrange("(p t) n -> p t n", t=4))
-            w2_raw[(0, first)] = raw
+        def load_w2_natural():
+            w2_raw[(0, 0)] = placed("w2_raw_0", [P, 4, N], F32, W2_AT[(0, 0)])[:]
+            nc.sync.dma_start(out=w2_raw[(0, 0)], in_=w2[0:512, :].rearrange("(p t) n -> p t n", t=4))
 
         def load_w2_dealt():
             w2_raw[(1, 0)] = placed("w2_raw_1", [P, 4, N], F32, W2_AT[(1, 0)])[:]
@@ -385,11 +384,11 @@ def tile_list_pairwise_document_ranking_kernel(
         w2_rounded = {}
         w2_q = {}
 
-        def round_w2(rounder, b, first, width, lo):
+        def round_w2(rounder, b, first, width, lo, count=P):
             if (b, first) not in w2_rounded:
                 at = W2_ROUNDED_AT[(b, first)]
                 w2_rounded[(b, first)] = placed("w2_rounded_%d_%d" % (b, first), [P, width, 4], BF16, at)
-            rounder(w2_rounded[(b, first)][:, lo : lo + P, :], w2_raw[(b, first)][:, :, lo : lo + P])
+            rounder(w2_rounded[(b, first)][:, lo : lo + count, :], w2_raw[(b, first)][:, :, lo : lo + count])
 
         def quantise_w2(b, first, width):
             flat = w2_rounded[(b, first)][:].rearrange("p n t -> p (n t)")
@@ -473,9 +472,7 @@ def tile_list_pairwise_document_ranking_kernel(
         load_wg_pass(0, 2, 2)
         load_w1(2, 2)
         wg_high = load_wg(4, 4)
-        load_w1(4, 4, [0])
-        load_w2_natural(N // 2, 4)
-        load_w1(4, 4, [1])
+        load_w1(4, 4)
         ident = placed("ident", [P, P], F32, IDENT_AT)
         make_identity(nc, ident[:])
         for i in range(2):
@@ -483,7 +480,7 @@ def tile_list_pairwise_document_ranking_kernel(
                 gate_pass(i, d, 0)
         gather_second_pass(0)
         gather_second_pass(1)
-        load_w2_natural(0, 4)
+        load_w2_natural()
         load_w2_dealt()
         c_t = keep.tile([P, N // P], F32, name="c_t")
         with nc.allow_non_contiguous_dma(reason="one bias value for each partition"):
@@ -537,8 +534,6 @@ def tile_list_pairwise_document_ranking_kernel(
         turn(1)
         gate_sum(5, 1)
         gate_sum(5, 0)
-        for lo in range(0, N // 2, P):
-            round_w2(scalar_round, 0, N // 2, N // 2, lo)
 
         features(2, 0)
         features(2, 1)
@@ -564,17 +559,18 @@ def tile_list_pairwise_document_ranking_kernel(
         features(4, 0)
         turn(3)
         quantise_w1(6, 2)
-        features(5, 1)
+        round_w2(gpsimd_round, 0, 0, N, 0, 2 * P)
         features(5, 0)
+        features(5, 1)
         weight_sum(6, 1)
         weight_sum(7, 1)
         gate_sum(6, 0)
         weight_sum(6, 0)
         gate_sum(7, 0)
         weight_sum(7, 0)
-        round_w2(gpsimd_round, 0, 0, N // 2, 0)
+        round_w2(gpsimd_round, 0, 0, N, 2 * P)
         features(6, 1)
-        round_w2(gpsimd_round, 0, 0, N // 2, P)
+        round_w2(gpsimd_round, 0, 0, N, 3 * P)
         features(7, 1)
 
         pick_second(4)
@@ -587,8 +583,7 @@ def tile_list_pairwise_document_ranking_kernel(
         pick_second(6)
         pick_second(7)
         pick_differences(0)
-        quantise_w2(0, 0, N // 2)
-        quantise_w2(0, N // 2, N // 2)
+        quantise_w2(0, 0, N)
         quantise_first_pass(0)
         open_scores(0)
         quantise_w2(1, 0, N)

@@ -35,18 +35,18 @@ SCORE_BANKS = [(4, 5), (6, 7), (0, 1, 2, 3)]
 TABLE_AT = [26, 49]
 TABLE_SPAN = [(10.5, 48.5), (49, 66.5)]
 TABLE_CUT = [T // 4, 3 * T // 4]
-TABLE_SCALES_AT, TABLE_SCALES_SPAN = 200, 7
+TABLE_SCALES_AT, TABLE_SCALES_SPAN = 200, 5
 W1_AT = {0: (4.5, 6.5), 1: (0, 12.5), 2: (32.5, 36.5), 4: (16.5, 24.5)}
 W1_SPAN = {0: 4, 1: 4, 2: 8, 4: 8}
 W2_AT = {(0, 0): 168, (1, 0): 49}
 WG_AT = {4: 10.5}
 WG_DEALT_AT = 74
-IDENT_AT = 206
+IDENT_AT = 204
 ROUNDED = {1: (72, 76, 78), 2: (76, 76, 80), 4: (76, 76, 86.0625), 6: (86, 86, 98.0625)}
 FIRST_ROUNDED_AT = 76
 CODES_AT = {1: 6.5, 2: 11.5, 4: 144, 6: 146}
 FIRST_CODES_AT = 65.5
-WINDOW_AT = [207, 108, 207, 120, 162, 98, 104, 116]
+WINDOW_AT = [205, 108, 205, 120, 162, 98, 104, 116]
 GATE_AT = [6.5, 12.5, 44.5, 40.5] + [128, 132, 136, 190]
 SHARED_AT = {3: (144, 2), 4: (146, 4), 5: (150, 2), 6: (152, 2), 7: (188, 2)}
 FIRST_AT = [158, 36.5, 11.5, 82]
@@ -75,7 +75,7 @@ def tile_list_pairwise_document_ranking_kernel(
             return psum.tile(shape, F32, name=name, offset=2 * KIB * bank)
 
         def placed(name, shape, dtype, kib):
-            return work.tile(shape, dtype, name=name, offset=int(kib * KIB), align_bytes=64)
+            return work.tile(shape, dtype, name=name, offset=int(kib * KIB), align_bytes=256)
 
         offs_t = keep.tile([P, S // 16], U16, name="offs_t")
         pos1_t = keep.tile([P, PAIRS // 16], U16, name="pos1_t")
@@ -97,7 +97,7 @@ def tile_list_pairwise_document_ranking_kernel(
         def load_wg(first, count):
             shape = [P, 2, 2 * P * count]
             if first == 0:
-                words = keep.tile(shape, U8, name="wg_0", align_bytes=64)
+                words = keep.tile(shape, U8, name="wg_0", align_bytes=256)
             else:
                 words = placed("wg_%d" % first, shape, U8, WG_AT[first])
             rows = wg_words.bitcast(I32).rearrange("a p n -> p a n")
@@ -108,14 +108,14 @@ def tile_list_pairwise_document_ranking_kernel(
             return words
 
         def load_wg_pass(a, first, count):
-            words = keep.tile([P, 2 * P * count], U8, name="wg_%d_%d" % (a, first), align_bytes=64)
+            words = keep.tile([P, 2 * P * count], U8, name="wg_%d_%d" % (a, first), align_bytes=256)
             cols = slice(first * P // 2, (first + count) * P // 2)
             nc.sync.dma_start(out=words[:].bitcast(I32), in_=wg_words[a].bitcast(I32)[:, cols])
             for t in range(count):
                 gate_w[(first + t, a)] = words[:, 2 * P * t : 2 * P * (t + 1)]
 
         def deal_wg_scales(plane):
-            scales = keep.tile([P, 2, 4, P], U8, name="wg_sc_dealt", align_bytes=64)
+            scales = keep.tile([P, 2, 4, P], U8, name="wg_sc_dealt", align_bytes=256)
             nc.gpsimd.tensor_copy(
                 scales[:].bitcast(I32).rearrange("p a t (q w) -> p a t q w", w=2),
                 plane[:, :, H // 2 : H].bitcast(I32).rearrange("p a (q t w) -> p a t q w", t=4, w=2),
@@ -176,7 +176,7 @@ def tile_list_pairwise_document_ranking_kernel(
                 v_words[(0, d)] = words[:, BANK * d : BANK * (d + 1)]
 
         def gather_second_pass(d):
-            words = keep.tile([P, BANK], U32, name="v_words_1_%d" % d, align_bytes=64)
+            words = keep.tile([P, BANK], U32, name="v_words_1_%d" % d, align_bytes=256)
             entries = offs_t[:, BANK * d // 16 : BANK * (d + 1) // 16]
             nc.vector.tensor_copy(words[:], tab[1][:, 0:T].bitcast(U32).indirect(entries))
             v_words[(1, d)] = words[:]
@@ -185,10 +185,10 @@ def tile_list_pairwise_document_ranking_kernel(
             if codes is not None:
                 pass
             elif kib is None:
-                codes = keep.tile([P, width], U32, name="codes_" + name, align_bytes=64)
+                codes = keep.tile([P, width], U32, name="codes_" + name, align_bytes=256)
             else:
                 codes = placed("codes_" + name, [P, width], U32, kib)
-            scales = keep.tile([P, width], U8, name="scales_" + name, align_bytes=64)
+            scales = keep.tile([P, width], U8, name="scales_" + name, align_bytes=256)
             nc.vector.quantize_mx(out=codes[:].bitcast(FP8X4), scales=scales[:], in_=rounded)
             return codes, scales
 
@@ -205,7 +205,7 @@ def tile_list_pairwise_document_ranking_kernel(
 
         def prepare_first_w1(a):
             if a == 0:
-                rounded = keep.tile([P, P, 4], BF16, name="w1_rounded_0_0", align_bytes=64)
+                rounded = keep.tile([P, P, 4], BF16, name="w1_rounded_0_0", align_bytes=256)
             else:
                 rounded = placed("w1_rounded_0_1", [P, P, 4], BF16, FIRST_ROUNDED_AT)
             scalar_round(rounded[:], w1_raw[(0, a)])
@@ -436,9 +436,9 @@ def tile_list_pairwise_document_ranking_kernel(
 
         tab_sc = placed("tab_sc", [P, TABLE_SCALES_SPAN * KIB], U8, TABLE_SCALES_AT)
         nc.vector.memset(tab_sc[:, 0:T].bitcast(I32), 0)
-        wg_sc = keep.tile([P, 2, H], U8, name="wg_sc", align_bytes=64)
+        wg_sc = keep.tile([P, 2, H], U8, name="wg_sc", align_bytes=256)
         nc.gpsimd.memset(wg_sc[:].bitcast(I32), 0)
-        v_sc = keep.tile([P, 2, S], U8, name="v_sc", align_bytes=64)
+        v_sc = keep.tile([P, 2, S], U8, name="v_sc", align_bytes=256)
         nc.vector.memset(v_sc[:].bitcast(I32), 0)
 
         nc.sync.dma_start(offs_t[:], offs)
@@ -457,7 +457,7 @@ def tile_list_pairwise_document_ranking_kernel(
         nc.vector.memset(warm[:, 0:1], 0.0)
         nc.scalar.activation(warm[:, 4:5], warm[:, 0:1], SIGMOID)
 
-        gathered_sc = keep.tile([P, S], U8, name="gathered_sc", align_bytes=64)
+        gathered_sc = keep.tile([P, S], U8, name="gathered_sc", align_bytes=256)
         nc.vector.tensor_copy(gathered_sc[:], tab_sc[:, 0:T].indirect(offs_t[:]))
         for q in range(4):
             nc.sync.dma_start(

@@ -50,11 +50,10 @@ WINDOW_AT = [205, 108, 205, 120, 162, 98, 104, 116]
 GATE_AT = [6.5, 12.5, 44.5, 40.5] + [128, 132, 136, 190]
 SHARED_AT = {3: (144, 2), 4: (146, 4), 5: (150, 2), 6: (152, 2), 7: (188, 2)}
 FIRST_AT = [158, 36.5, 11.5, 82]
-SECOND_AT = [72, 38.5, 80, 84, 148, 154, 198, 196]
-LATE_CODES_AT = 191
-SECOND_Z_CODES_AT = 187.5
-DIFFERENCES_AT = (179.5, 11)
-LATE_DIFFERENCES_AT = 183.5
+SECOND_AT = [72, 38.5, 80, 84, 148, 154, 198, 166]
+LATE_CODES_AT = 190.5
+DIFFERENCES_AT, DIFFERENCES_SPAN = 185.5, 5
+DIFFERENCES_START = [P, 0, 4 * P]
 W2_ROUNDED_AT = {(0, 0): 94, (1, 0): 136}
 Z_TURNED_AT = 57
 Z_ROUNDED_AT = 66.5
@@ -325,7 +324,7 @@ def tile_list_pairwise_document_ranking_kernel(
             )
 
         z_q = {}
-        late_codes = placed("late_codes", [P, 2 * N + PAIRS // 2], U32, LATE_CODES_AT)
+        late_codes = placed("late_codes", [P, 2 * N + PAIRS], U32, LATE_CODES_AT)
 
         def turn_back():
             words = z_turned[:].bitcast(F32)
@@ -341,32 +340,21 @@ def tile_list_pairwise_document_ranking_kernel(
                 )
             return rounded[:].rearrange("p j t -> p (j t)")
 
-        def quantise_first_pass(g):
-            half = PAIRS // 2
-            rounded = z_first[:, 4 * half * g : 4 * half * (g + 1)]
-            if g == 0:
-                codes, scales = quantise("z_0_0", rounded, half, codes=late_codes[:, 2 * N : 2 * N + half])
-            else:
-                codes, scales = quantise("z_0_1", rounded, half, SECOND_Z_CODES_AT)
+        def quantise_first_pass():
+            codes, scales = quantise("z_0", z_first, PAIRS, codes=late_codes[:, 2 * N : 2 * N + PAIRS])
             for h, (j0, width) in enumerate(PIECES):
-                if j0 // half == g:
-                    cols = slice(j0 - half * g, j0 - half * g + width)
-                    z_q[(0, h)] = (codes[:, cols], scales[:, cols])
+                z_q[(0, h)] = (codes[:, j0 : j0 + width], scales[:, j0 : j0 + width])
 
         z_dealt = [
             placed("z_rounded_1_%d" % h, [P, width, 4], BF16, Z_DEALT_AT + j0 // P)
             for h, (j0, width) in enumerate(PIECES)
         ]
-        late_differences = placed("late_differences", [P, 8, P], F32, LATE_DIFFERENCES_AT)
+        all_differences = placed("differences", [P, DIFFERENCES_SPAN * KIB // 4], F32, DIFFERENCES_AT)
 
         def pick_differences(h):
             j0, width = PIECES[h]
-            if h == 0:
-                start, span = DIFFERENCES_AT
-                rows = span * KIB // (4 * width)
-                differences = placed("differences", [P, rows, width], F32, start)[:, 0:4, :]
-            else:
-                differences = late_differences[:, 4 * h - 4 : 4 * h, :]
+            start = DIFFERENCES_START[h]
+            differences = all_differences[:, start : start + 4 * width].rearrange("p (t j) -> p t j", t=4)
             entries = slice(j0 // 16, (j0 + width) // 16)
             for t in range(4):
                 picked = windows[NATURAL + t][:].indirect(pos1_t[:, entries])
@@ -584,12 +572,11 @@ def tile_list_pairwise_document_ranking_kernel(
         pick_second(7)
         pick_differences(0)
         quantise_w2(0, 0, N)
-        quantise_first_pass(0)
+        quantise_first_pass()
         open_scores(0)
         quantise_w2(1, 0, N)
         quantise_piece(0)
         pick_differences(1)
-        quantise_first_pass(1)
         close_scores(0, 2)
         open_scores(1)
         open_scores(2)

@@ -26,7 +26,7 @@ NATURAL = 4
 SHARED = (3, 4, 6, 7)
 PIECES = [(0, 256), (256, 128), (384, 128)]
 
-GATE_BANK = [(4, 5), (6, 7), (4, 5), (7, 6), (7, 5), (5, 4), (1, 4), (6, 4)]
+GATE_BANK = [(4, 5), (6, 7), (4, 5), (7, 6), (7, 5), (5, 4), (5, 4), (5, 4)]
 SUM_BANK = [(0, 1), (2, 3), (0, 1), (2, 4), (0, 6), (1, 7), (2, 6), (0, 5)]
 TURN_BANK = [1, 3, 3, 3]
 BACK_BANK = [6, 0]
@@ -42,7 +42,7 @@ W2_AT = {(0, 0): 168, (1, 0): 49}
 WG_AT = {4: 10.5}
 WG_DEALT_AT = 74
 IDENT_AT = 204
-ROUNDED = {1: (72, 76, 78), 2: (76, 76, 80), 4: (76, 76, 86.0625), 6: (86, 86, 98.0625)}
+ROUNDED = {1: (72, 76, 78), 2: (76, 76, 80), 4: (76, 76, 86.0625), 6: (86, 86, 102.0625)}
 FIRST_ROUNDED_AT = 76
 CODES_AT = {1: 6.5, 2: 11.5, 4: 144, 6: 146}
 FIRST_CODES_AT = 65.5
@@ -50,7 +50,7 @@ WINDOW_AT = [205, 108, 205, 120, 162, 98, 104, 116]
 GATE_AT = [6.5, 12.5, 44.5, 40.5] + [128, 132, 136, 190]
 SHARED_AT = {3: (144, 2), 4: (146, 4), 5: (150, 2), 6: (152, 2), 7: (188, 2)}
 FIRST_AT = [158, 36.5, 11.5, 82]
-SECOND_AT = [72, 38.5, 80, 84, 148, 154, 198, 166]
+SECOND_AT = [72, 38.5, 80, 84, 102, 154, 146, 166]
 LATE_CODES_AT = 190.5
 DIFFERENCES_AT, DIFFERENCES_SPAN = 185.5, 5
 DIFFERENCES_START = [P, 0, 4 * P]
@@ -114,14 +114,14 @@ def tile_list_pairwise_document_ranking_kernel(
                 gate_w[(first + t, a)] = words[:, 2 * P * t : 2 * P * (t + 1)]
 
         def deal_wg_scales(plane):
-            scales = keep.tile([P, 2, 4, P], U8, name="wg_sc_dealt", align_bytes=256)
+            scales = keep.tile([P, 2, 4, 2 * P], U8, name="wg_sc_dealt", align_bytes=256)
             nc.gpsimd.tensor_copy(
-                scales[:].bitcast(I32).rearrange("p a t (q w) -> p a t q w", w=2),
+                scales[:].bitcast(I32)[:, :, :, 0 : P // 4].rearrange("p a t (q w) -> p a t q w", w=2),
                 plane[:, :, H // 2 : H].bitcast(I32).rearrange("p a (q t w) -> p a t q w", t=4, w=2),
             )
             for a in range(2):
                 for t in range(4):
-                    gate_sc[(NATURAL + t, a)] = scales[:, a, t, :]
+                    gate_sc[(NATURAL + t, a)] = scales[:, a, t, 0:P]
 
         def deal_wg_words(loaded):
             words = placed("wg_dealt", [P, 2, 4, 2 * P], U8, WG_DEALT_AT)
@@ -533,6 +533,7 @@ def tile_list_pairwise_document_ranking_kernel(
         weight_sum(5, 1)
         gate_sum(6, 1)
         weight_sum(5, 0)
+        gate_sum(6, 0)
         round_dealt(True, 6, 0)
         round_dealt(True, 7, 0)
         features(4, 1)
@@ -541,6 +542,7 @@ def tile_list_pairwise_document_ranking_kernel(
         pick_second(2)
         turn(2)
         gate_sum(7, 1)
+        gate_sum(7, 0)
 
         pick_first(3)
         pick_second(3)
@@ -548,17 +550,14 @@ def tile_list_pairwise_document_ranking_kernel(
         turn(3)
         quantise_w1(6, 2)
         round_w2(gpsimd_round, 0, 0, N, 0, 2 * P)
+        round_w2(gpsimd_round, 0, 0, N, 2 * P, 2 * P)
         features(5, 0)
         features(5, 1)
         weight_sum(6, 1)
         weight_sum(7, 1)
-        gate_sum(6, 0)
         weight_sum(6, 0)
-        gate_sum(7, 0)
         weight_sum(7, 0)
-        round_w2(gpsimd_round, 0, 0, N, 2 * P)
         features(6, 1)
-        round_w2(gpsimd_round, 0, 0, N, 3 * P)
         features(7, 1)
 
         pick_second(4)

@@ -23,41 +23,42 @@ P = 128
 KIB = 1024
 BANK = 512
 NATURAL = 4
-SHARED = (3, 4, 6, 7)
+SHARED = (3, 4, 5, 6, 7)
 PIECES = [(0, 256), (256, 128), (384, 128)]
 
-GATE_BANK = [(4, 5), (6, 7), (4, 5), (7, 6), (7, 5), (5, 4), (5, 4), (5, 4)]
+GATE_BANK = [(4, 5), (6, 7), (4, 5), (7, 6), (7, 5), (5, 4), (5, 4), (1, 4)]
 SUM_BANK = [(0, 1), (2, 3), (0, 1), (2, 4), (0, 6), (1, 7), (2, 6), (0, 5)]
 TURN_BANK = [1, 3, 3, 3]
-BACK_BANK = [6, 0]
+BACK_BANK = [3, 6]
 SCORE_BANKS = [(4, 5), (6, 7), (0, 1, 2, 3)]
 
 TABLE_AT = [26, 49]
 TABLE_SPAN = [(10.5, 48.5), (49, 66.5)]
 TABLE_CUT = [T // 4, 3 * T // 4]
-TABLE_SCALES_AT, TABLE_SCALES_SPAN = 200, 5
+TABLE_SCALES_AT, TABLE_SCALES_SPAN = 199.5, 5
 W1_AT = {0: (4.5, 6.5), 1: (0, 12.5), 2: (32.5, 36.5), 4: (16.5, 24.5)}
 W1_SPAN = {0: 4, 1: 4, 2: 8, 4: 8}
 W2_AT = {(0, 0): 168, (1, 0): 49}
 WG_AT = {4: 10.5}
 WG_DEALT_AT = 74
-IDENT_AT = 204
+IDENT_AT = 203.5
 ROUNDED = {1: (72, 76, 78), 2: (76, 76, 80), 4: (76, 76, 86.0625), 6: (86, 86, 102.0625)}
 FIRST_ROUNDED_AT = 76
-CODES_AT = {1: 6.5, 2: 11.5, 4: 144, 6: 146}
+CODES_AT = {1: 6.5, 2: 11.5, 4: 144, 6: 147}
 FIRST_CODES_AT = 65.5
-WINDOW_AT = [205, 108, 205, 120, 162, 98, 104, 116]
+WINDOW_AT = [204.5, 108, 204.5, 120, 162, 98, 104, 116]
 GATE_AT = [6.5, 12.5, 44.5, 40.5] + [128, 132, 136, 190]
-SHARED_AT = {3: (144, 2), 4: (146, 4), 5: (150, 2), 6: (152, 2), 7: (188, 2)}
+SHARED_AT = {3: (144, 2), 4: (147, 2), 5: (150, 2), 6: (152, 2), 7: (188, 2)}
 FIRST_AT = [158, 36.5, 11.5, 82]
-SECOND_AT = [72, 38.5, 80, 84, 102, 154, 146, 166]
+SECOND_AT = [72, 38.5, 80, 84, 102, 154, 147.5, 166]
 LATE_CODES_AT = 190.5
 DIFFERENCES_AT, DIFFERENCES_SPAN = 185.5, 5
-DIFFERENCES_START = [P, 0, 4 * P]
-W2_ROUNDED_AT = {(0, 0): 94, (1, 0): 136}
+DIFFERENCES_START = [2 * P, 0, 4 * P]
+W2_EARLY = 256
+W2_EARLY_AT, W2_LATE_AT = 94, 141.25
 Z_TURNED_AT = 57
 Z_ROUNDED_AT = 66.5
-Z_DEALT_AT = 140
+Z_DEALT_AT = 176
 RESULT_AT = 108
 
 
@@ -369,17 +370,20 @@ def tile_list_pairwise_document_ranking_kernel(
             codes, scales = quantise("z_1_%d" % h, z_dealt[h][:].rearrange("p j t -> p (j t)"), PIECES[h][1])
             z_q[(1, h)] = (codes[:], scales[:])
 
-        w2_rounded = {}
         w2_q = {}
+        w2_early = placed("w2_rounded_early", [P, W2_EARLY, 4], BF16, W2_EARLY_AT)
+        w2_late = placed("w2_rounded_late", [P, 2 * N - W2_EARLY, 4], BF16, W2_LATE_AT)
 
-        def round_w2(rounder, b, first, width, lo, count=P):
-            if (b, first) not in w2_rounded:
-                at = W2_ROUNDED_AT[(b, first)]
-                w2_rounded[(b, first)] = placed("w2_rounded_%d_%d" % (b, first), [P, width, 4], BF16, at)
-            rounder(w2_rounded[(b, first)][:, lo : lo + count, :], w2_raw[(b, first)][:, :, lo : lo + count])
+        def rounded_w2(b, first, width):
+            if (b, first) == (0, 0):
+                return w2_early[:]
+            return w2_late[:, N * b + first - W2_EARLY : N * b + first - W2_EARLY + width, :]
+
+        def round_w2(rounder, b, first, width=P):
+            rounder(rounded_w2(b, first, width), w2_raw[(b, 0)][:, :, first : first + width])
 
         def quantise_w2(b, first, width):
-            flat = w2_rounded[(b, first)][:].rearrange("p n t -> p (n t)")
+            flat = rounded_w2(b, first, width).rearrange("p n t -> p (n t)")
             place = late_codes[:, N * b + first : N * b + first + width]
             codes, scales = quantise("w2_%d_%d" % (b, first), flat, width, codes=place)
             for lo in range(0, width, P):
@@ -542,19 +546,18 @@ def tile_list_pairwise_document_ranking_kernel(
         pick_second(2)
         turn(2)
         gate_sum(7, 1)
-        gate_sum(7, 0)
 
         pick_first(3)
         pick_second(3)
         features(4, 0)
         turn(3)
         quantise_w1(6, 2)
-        round_w2(gpsimd_round, 0, 0, N, 0, 2 * P)
-        round_w2(gpsimd_round, 0, 0, N, 2 * P, 2 * P)
-        features(5, 0)
         features(5, 1)
+        round_w2(gpsimd_round, 0, 0, W2_EARLY)
+        features(5, 0)
         weight_sum(6, 1)
         weight_sum(7, 1)
+        gate_sum(7, 0)
         weight_sum(6, 0)
         weight_sum(7, 0)
         features(6, 1)
@@ -565,12 +568,13 @@ def tile_list_pairwise_document_ranking_kernel(
         features(6, 0)
         features(7, 0)
         z_first = turn_back()
-        for lo in range(0, N, P):
-            round_w2(scalar_round, 1, 0, N, lo)
+        for first in range(W2_EARLY, 2 * N, P):
+            round_w2(scalar_round, first // N, first % N)
         pick_second(6)
         pick_second(7)
         pick_differences(0)
-        quantise_w2(0, 0, N)
+        quantise_w2(0, 0, W2_EARLY)
+        quantise_w2(0, W2_EARLY, N - W2_EARLY)
         quantise_first_pass()
         open_scores(0)
         quantise_w2(1, 0, N)

from contextlib import ExitStack

import concourse.mybir as mybir
from concourse.masks import make_identity

T, S, PAIRS, K, H, N = 4096, 1024, 512, 1024, 1024, 512
FLOPS = 2 * (2 * K * H * S + H * N * PAIRS)

F32 = mybir.dt.float32
BF16 = mybir.dt.bfloat16
I32 = mybir.dt.int32
U32 = mybir.dt.uint32
U16 = mybir.dt.uint16
U8 = mybir.dt.uint8
FP8X4 = mybir.dt.float8_e4m3fn_x4
FP4X4 = mybir.dt.float4_e2m1fn_x4
MULT = mybir.AluOpType.mult
ADD = mybir.AluOpType.add
SUB = mybir.AluOpType.subtract
SIGMOID = mybir.ActivationFunctionType.Sigmoid

P = 128
KIB = 1024
BANK = 512
NATURAL = 4
SHARED = (3, 4, 5, 6, 7)
PIECES = [(0, 256), (256, 128), (384, 128)]

GATE_BANK = [(4, 5), (6, 7), (4, 5), (7, 6), (7, 5), (5, 4), (5, 4), (1, 4)]
SUM_BANK = [(0, 1), (2, 3), (0, 1), (2, 4), (0, 6), (1, 7), (2, 6), (0, 5)]
TURN_BANK = [1, 3, 3, 3]
BACK_BANK = [3, 6]
SCORE_BANKS = [(4, 5), (6, 7), (0, 1, 2, 3)]

TABLE_AT = [26, 49]
TABLE_SPAN = [(10.5, 48.5), (49, 66.5)]
TABLE_CUT = [T // 4, 3 * T // 4]
TABLE_SCALES_AT, TABLE_SCALES_SPAN = 199.5, 5
W1_AT = {0: (4.5, 6.5), 1: (0, 12.5), 2: (32.5, 36.5), 4: (16.5, 24.5)}
W1_SPAN = {0: 4, 1: 4, 2: 8, 4: 8}
W2_AT = {(0, 0): 168, (1, 0): 49}
WG_AT = {4: 10.5}
WG_DEALT_AT = 74
IDENT_AT = 203.5
ROUNDED = {1: (72, 76, 78), 2: (76, 76, 80), 4: (76, 76, 86.0625), 6: (86, 86, 102.0625)}
FIRST_ROUNDED_AT = 76
CODES_AT = {1: 6.5, 2: 11.5, 4: 144, 6: 147}
FIRST_CODES_AT = 65.5
WINDOW_AT = [204.5, 108, 204.5, 120, 162, 98, 104, 116]
GATE_AT = [6.5, 12.5, 44.5, 40.5] + [128, 132, 136, 190]
SHARED_AT = {3: (144, 2), 4: (147, 2), 5: (150, 2), 6: (152, 2), 7: (188, 2)}
FIRST_AT = [158, 36.5, 11.5, 82]
SECOND_AT = [72, 38.5, 80, 84, 102, 154, 147.5, 166]
LATE_CODES_AT = 190.5
DIFFERENCES_AT, DIFFERENCES_SPAN = 185.5, 5
DIFFERENCES_START = [2 * P, 0, 4 * P]
W2_EARLY = 256
W2_EARLY_AT, W2_LATE_AT = 94, 141.25
Z_TURNED_AT = 57
Z_ROUNDED_AT = 66.5
Z_DEALT_AT = 176
RESULT_AT = 108


def tile_list_pairwise_document_ranking_kernel(
    tc, tab_words, tab_scales, offs, pos1, pos2, w1, wg_words, wg_scales, w2, c, out
):
    nc = tc.nc
    with ExitStack() as ctx:
        keep = ctx.enter_context(tc.tile_pool(name="keep", bufs=1))
        work = ctx.enter_context(tc.tile_pool(name="work", bufs=1))
        psum = ctx.enter_context(tc.psum_pool(name="psum", bufs=1))

        def bank_tile(name, shape, bank):
            return psum.tile(shape, F32, name=name, offset=2 * KIB * bank)

        def placed(name, shape, dtype, kib):
            return work.tile(shape, dtype, name=name, offset=int(kib * KIB), align_bytes=256)

        offs_t = keep.tile([P, S // 16], U16, name="offs_t")
        pos1_t = keep.tile([P, PAIRS // 16], U16, name="pos1_t")
        pos2_t = keep.tile([P, PAIRS // 16], U16, name="pos2_t")

        tab = []
        for a, (start, end) in enumerate(TABLE_SPAN):
            span = placed("tab%d" % a, [P, int((end - start) * KIB) // 4], I32, start)
            skip = int((TABLE_AT[a] - start) * KIB) // 4
            tab.append(span[:, skip : skip + T])

        def load_table(a, first, last):
            words = tab_words[a].rearrange("p t i -> p (t i)").bitcast(I32)
            nc.sync.dma_start(out=tab[a][:, first:last], in_=words[:, first:last])

        gate_w = {}
        gate_sc = {}

        def load_wg(first, count):
            shape = [P, 2, 2 * P * count]
            if first == 0:
                words = keep.tile(shape, U8, name="wg_0", align_bytes=256)
            else:
                words = placed("wg_%d" % first, shape, U8, WG_AT[first])
            rows = wg_words.bitcast(I32).rearrange("a p n -> p a n")
            nc.sync.dma_start(out=words[:].bitcast(I32), in_=rows[:, :, first * P // 2 : (first + count) * P // 2])
            for a in range(2):
                for t in range(count):
                    gate_w[(first + t, a)] = words[:, a, 2 * P * t : 2 * P * (t + 1)]
            return words

        def load_wg_pass(a, first, count):
            words = keep.tile([P, 2 * P * count], U8, name="wg_%d_%d" % (a, first), align_bytes=256)
            cols = slice(first * P // 2, (first + count) * P // 2)
            nc.sync.dma_start(out=words[:].bitcast(I32), in_=wg_words[a].bitcast(I32)[:, cols])
            for t in range(count):
                gate_w[(first + t, a)] = words[:, 2 * P * t : 2 * P * (t + 1)]

        def deal_wg_scales(plane):
            scales = keep.tile([P, 2, 4, 2 * P], U8, name="wg_sc_dealt", align_bytes=256)
            nc.gpsimd.tensor_copy(
                scales[:].bitcast(I32)[:, :, :, 0 : P // 4].rearrange("p a t (q w) -> p a t q w", w=2),
                plane[:, :, H // 2 : H].bitcast(I32).rearrange("p a (q t w) -> p a t q w", t=4, w=2),
            )
            for a in range(2):
                for t in range(4):
                    gate_sc[(NATURAL + t, a)] = scales[:, a, t, 0:P]

        def deal_wg_words(loaded):
            words = placed("wg_dealt", [P, 2, 4, 2 * P], U8, WG_DEALT_AT)
            nc.gpsimd.tensor_copy(
                words[:].bitcast(I32).rearrange("p a t (q w) -> p a t q w", w=4),
                loaded[:].bitcast(I32).rearrange("p a (q t w) -> p a t q w", t=4, w=4),
            )
            for a in range(2):
                for t in range(4):
                    gate_w[(NATURAL + t, a)] = words[:, a, t, :]

        def load_wg_scales(engine, plane, first, count):
            for q in range(4):
                rows = wg_scales[:, 4 * q : 4 * q + 4, first * P : (first + count) * P]
                engine.dma_start(
                    out=plane[32 * q : 32 * q + 4, :, :].bitcast(I32),
                    in_=rows.rearrange("a r t -> r a t").bitcast(I32),
                )
            for a in range(2):
                for t in range(count):
                    gate_sc[(first + t, a)] = plane[:, a, P * t : P * (t + 1)]

        w1_raw = {}

        def load_w1(first, count, passes=(0, 1)):
            for a in passes:
                rows = W1_SPAN[first] * 2 // count if a == 1 else 4
                raw = placed("w1_raw_%d_%d" % (first, a), [P, rows, count * P], F32, W1_AT[first][a])
                cols = w1[512 * a : 512 * (a + 1), first * P : (first + count) * P]
                nc.sync.dma_start(out=raw[:, 0:4, :], in_=cols.rearrange("(p j) c -> p j c", j=4))
                w1_raw[(first, a)] = raw[:, 0:4, :]

        w2_raw = {}

        def load_w2_natural():
            w2_raw[(0, 0)] = placed("w2_raw_0", [P, 4, N], F32, W2_AT[(0, 0)])[:]
            nc.sync.dma_start(out=w2_raw[(0, 0)], in_=w2[0:512, :].rearrange("(p t) n -> p t n", t=4))

        def load_w2_dealt():
            w2_raw[(1, 0)] = placed("w2_raw_1", [P, 4, N], F32, W2_AT[(1, 0)])[:]
            rows = w2[512:1024, :].rearrange("(q t e) n -> t q e n", t=4, e=8)
            for t in range(4):
                nc.sync.dma_start(out=w2_raw[(1, 0)][:, t, :], in_=rows[t])

        v_words = {}

        def gather_first_pass():
            words = placed("v_words_0", [P, S], U32, TABLE_SCALES_AT)
            nc.vector.tensor_copy(words[:], tab[0][:, 0:T].bitcast(U32).indirect(offs_t[:]))
            for d in range(2):
                v_words[(0, d)] = words[:, BANK * d : BANK * (d + 1)]

        def gather_second_pass(d):
            words = keep.tile([P, BANK], U32, name="v_words_1_%d" % d, align_bytes=256)
            entries = offs_t[:, BANK * d // 16 : BANK * (d + 1) // 16]
            nc.vector.tensor_copy(words[:], tab[1][:, 0:T].bitcast(U32).indirect(entries))
            v_words[(1, d)] = words[:]

        def quantise(name, rounded, width, kib=None, codes=None):
            if codes is not None:
                pass
            elif kib is None:
                codes = keep.tile([P, width], U32, name="codes_" + name, align_bytes=256)
            else:
                codes = placed("codes_" + name, [P, width], U32, kib)
            scales = keep.tile([P, width], U8, name="scales_" + name, align_bytes=256)
            nc.vector.quantize_mx(out=codes[:].bitcast(FP8X4), scales=scales[:], in_=rounded)
            return codes, scales

        def gpsimd_round(dst, raw):
            nc.gpsimd.tensor_scalar(dst, raw.rearrange("p j c -> p c j"), 1.0, 0.0, MULT, ADD)

        def scalar_round(dst, raw):
            nc.scalar.copy(
                out=dst.rearrange("p (g i) j -> p g j i", i=2), in_=raw.rearrange("p j (g i) -> p g j i", i=2)
            )

        w1_q = {}
        w1_rounded = {}

        def prepare_first_w1(a):
            if a == 0:
                rounded = keep.tile([P, P, 4], BF16, name="w1_rounded_0_0", align_bytes=256)
            else:
                rounded = placed("w1_rounded_0_1", [P, P, 4], BF16, FIRST_ROUNDED_AT)
            scalar_round(rounded[:], w1_raw[(0, a)])
            codes, scales = quantise("w1_0_%d" % a, rounded[:].rearrange("p c j -> p (c j)"), P, FIRST_CODES_AT + a / 2)
            w1_q[(0, a)] = (codes[:], scales[:])

        def round_w1(rounder, first, count, a, lo, hi):
            if first not in w1_rounded:
                start, data, end = ROUNDED[first]
                span = placed("w1_rounded_%d" % first, [P, int((end - start) * KIB) // 2], BF16, start)
                skip = (data - start) * KIB // 2
                w1_rounded[first] = span[:, skip : skip + count * KIB]
            dst = w1_rounded[first].rearrange("p (a c j) -> p a c j", a=2, j=4)
            rounder(dst[:, a, P * lo : P * hi, :], w1_raw[(first, a)][:, :, P * lo : P * hi])

        def round_dealt(on_gpsimd, i, a):
            first = i - i % 2
            if first not in w1_rounded:
                start, data, end = ROUNDED[first]
                span = placed("w1_rounded_%d" % first, [P, int((end - start) * KIB) // 2], BF16, start)
                skip = (data - start) * KIB // 2
                w1_rounded[first] = span[:, skip : skip + 2 * KIB]
            dst = w1_rounded[first].rearrange("p (a t c j) -> p a t c j", a=2, t=2, j=4)[:, a, i % 2]
            raw = w1_raw[(NATURAL, a)].rearrange("p j (q t e) -> p t j q e", t=4, e=8)[:, i - NATURAL]
            if on_gpsimd:
                out = dst.rearrange("p (q e) j -> p q e j", e=8)
                nc.gpsimd.tensor_scalar(out, raw.rearrange("p j q e -> p q e j"), 1.0, 0.0, MULT, ADD)
            else:
                nc.scalar.copy(
                    out=dst.rearrange("p (q g i) j -> p q g j i", g=4, i=2),
                    in_=raw.rearrange("p j q (g i) -> p q g j i", i=2),
                )

        def quantise_w1(first, count):
            codes, scales = quantise("w1_%d" % first, w1_rounded[first], 2 * count * P, CODES_AT[first])
            for a in range(2):
                for t in range(count):
                    cols = slice(P * (a * count + t), P * (a * count + t + 1))
                    w1_q[(first + t, a)] = (codes[:, cols], scales[:, cols])

        def first_stage_pass(bank, codes, scales, fmt, d, a):
            nc.tensor.matmul_mx(
                out=bank[:],
                lhsT=codes.bitcast(fmt),
                lhsT_scale=scales,
                rhs=v_words[(a, d)].bitcast(FP8X4),
                rhs_scale=v_sc[:, a, BANK * d : BANK * (d + 1)],
                start=(a == 0),
                stop=(a == 1),
            )

        gate_banks = {}
        gates = {}
        w1_sums = {}
        shared_sums = {}
        windows = {}

        def gate_pass(i, d, a):
            if a == 0:
                gate_banks[(i, d)] = bank_tile("g_bank_%d_%d" % (i, d), [P, BANK], GATE_BANK[i][d])
            first_stage_pass(gate_banks[(i, d)], gate_w[(i, a)], gate_sc[(i, a)], FP4X4, d, a)

        def copy_gate(i, d):
            gates[(i, d)] = placed("gate_%d_%d" % (i, d), [P, BANK], F32, GATE_AT[i] + 2 * d)
            nc.scalar.copy(out=gates[(i, d)][:], in_=gate_banks[(i, d)][:])

        def gate_sum(i, d):
            gate_pass(i, d, 0)
            gate_pass(i, d, 1)
            copy_gate(i, d)

        def weight_sum(i, d):
            w1_sums[(i, d)] = bank_tile("a_bank_%d_%d" % (i, d), [P, BANK], SUM_BANK[i][d])
            for a in range(2):
                first_stage_pass(w1_sums[(i, d)], *w1_q[(i, a)], FP8X4, d, a)
            if d == 1 and i in SHARED:
                start, span = SHARED_AT[i]
                shared_sums[i] = placed("shared_sums_%d" % i, [P, span * KIB // 4], F32, start)[:, 0:BANK]
                nc.scalar.copy(out=shared_sums[i], in_=w1_sums[(i, d)][:])

        def features(i, d):
            if i not in windows:
                windows[i] = placed("window_%d" % i, [P, 2 * S if i < NATURAL else S], F32, WINDOW_AT[i])
            dst = windows[i][:, BANK * d : BANK * (d + 1)]
            if d == 1 and i in SHARED:
                nc.gpsimd.tensor_tensor(dst, shared_sums[i], gates[(i, d)][:], MULT)
            else:
                nc.vector.tensor_tensor(dst, w1_sums[(i, d)][:], gates[(i, d)][:], MULT)

        firsts = {}
        seconds = {}

        def pick_first(i):
            firsts[i] = placed("first_%d" % i, [P, PAIRS], F32, FIRST_AT[i])[:]
            nc.vector.tensor_copy(firsts[i], windows[i][:, 0:S].indirect(pos1_t[:]))

        def pick_second(i):
            seconds[i] = placed("second_%d" % i, [P, PAIRS], F32, SECOND_AT[i])[:]
            if i < NATURAL:
                nc.vector.tensor_scalar(seconds[i], windows[i][:].indirect(pos2_t[:]), -1.0, 0.0, MULT, ADD)
            else:
                nc.vector.tensor_copy(seconds[i], windows[i][:].indirect(pos2_t[:]))

        z_turned = placed("z_turned", [P, 4, 2, 2 * P], BF16, Z_TURNED_AT)

        def turn(i):
            bank = bank_tile("zt_bank_%d" % i, [P, 4, P], TURN_BANK[i])
            for jb in range(4):
                cols = slice(P * jb, P * (jb + 1))
                for term, last in ((firsts[i], False), (seconds[i], True)):
                    nc.tensor.matmul(
                        bank[:, jb, :], term[:, cols], ident[:], start=not last, stop=last, is_transpose=True
                    )
            nc.scalar.copy(
                out=z_turned[:, :, :, 64 * i : 64 * (i + 1)].rearrange("j b u (m e) -> j b u m e", e=2),
                in_=bank[:].rearrange("j b (m u e) -> j b u m e", u=2, e=2),
            )

        z_q = {}
        late_codes = placed("late_codes", [P, 2 * N + PAIRS], U32, LATE_CODES_AT)

        def turn_back():
            words = z_turned[:].bitcast(F32)
            rounded = placed("z_rounded_0", [P, PAIRS, 4], BF16, Z_ROUNDED_AT)
            for g in range(2):
                bank = bank_tile("back_bank_%d" % g, [P, 2, 2, P], BACK_BANK[g])
                for jb in range(2):
                    for u in range(2):
                        nc.tensor.transpose(bank[:, jb, u, :], words[:, 2 * g + jb, u, :], ident[:])
                nc.scalar.copy(
                    out=rounded[:, 2 * P * g : 2 * P * (g + 1), :].bitcast(F32).rearrange("p (b j) u -> p b j u", b=2),
                    in_=bank[:].rearrange("p b u j -> p b j u"),
                )
            return rounded[:].rearrange("p j t -> p (j t)")

        def quantise_first_pass():
            codes, scales = quantise("z_0", z_first, PAIRS, codes=late_codes[:, 2 * N : 2 * N + PAIRS])
            for h, (j0, width) in enumerate(PIECES):
                z_q[(0, h)] = (codes[:, j0 : j0 + width], scales[:, j0 : j0 + width])

        z_dealt = [
            placed("z_rounded_1_%d" % h, [P, width, 4], BF16, Z_DEALT_AT + j0 // P)
            for h, (j0, width) in enumerate(PIECES)
        ]
        all_differences = placed("differences", [P, DIFFERENCES_SPAN * KIB // 4], F32, DIFFERENCES_AT)

        def pick_differences(h):
            j0, width = PIECES[h]
            start = DIFFERENCES_START[h]
            differences = all_differences[:, start : start + 4 * width].rearrange("p (t j) -> p t j", t=4)
            entries = slice(j0 // 16, (j0 + width) // 16)
            for t in range(4):
                picked = windows[NATURAL + t][:].indirect(pos1_t[:, entries])
                nc.vector.tensor_tensor(differences[:, t, :], picked, seconds[NATURAL + t][:, j0 : j0 + width], SUB)
            copy = nc.vector.tensor_copy if h > 0 else nc.scalar.copy
            copy(
                out=z_dealt[h][:].rearrange("p (g i) t -> p g t i", i=2),
                in_=differences.rearrange("p t (g i) -> p g t i", i=2),
            )

        def quantise_piece(h):
            codes, scales = quantise("z_1_%d" % h, z_dealt[h][:].rearrange("p j t -> p (j t)"), PIECES[h][1])
            z_q[(1, h)] = (codes[:], scales[:])

        w2_q = {}
        w2_early = placed("w2_rounded_early", [P, W2_EARLY, 4], BF16, W2_EARLY_AT)
        w2_late = placed("w2_rounded_late", [P, 2 * N - W2_EARLY, 4], BF16, W2_LATE_AT)

        def rounded_w2(b, first, width):
            if (b, first) == (0, 0):
                return w2_early[:]
            return w2_late[:, N * b + first - W2_EARLY : N * b + first - W2_EARLY + width, :]

        def round_w2(rounder, b, first, width=P):
            rounder(rounded_w2(b, first, width), w2_raw[(b, 0)][:, :, first : first + width])

        def quantise_w2(b, first, width):
            flat = rounded_w2(b, first, width).rearrange("p n t -> p (n t)")
            place = late_codes[:, N * b + first : N * b + first + width]
            codes, scales = quantise("w2_%d_%d" % (b, first), flat, width, codes=place)
            for lo in range(0, width, P):
                w2_q[(b, (first + lo) // P)] = (codes[:, lo : lo + P], scales[:, lo : lo + P])

        y_banks = {}

        def second_stage_pass(h, nt, b):
            w_codes, w_scales = w2_q[(b, nt)]
            z_codes, z_scales = z_q[(b, h)]
            shared = N // P // len(SCORE_BANKS[h])
            nc.tensor.matmul_mx(
                out=y_banks[(h, nt)],
                lhsT=w_codes.bitcast(FP8X4),
                lhsT_scale=w_scales,
                rhs=z_codes.bitcast(FP8X4),
                rhs_scale=z_scales,
                start=(b == 0 and nt % shared == 0),
                stop=(b == 1 and nt % shared == shared - 1),
            )

        def open_scores(h):
            shared = N // P // len(SCORE_BANKS[h])
            for k, bank in enumerate(SCORE_BANKS[h]):
                sums = bank_tile("y_bank_%d_%d" % (h, k), [P, shared, PIECES[h][1]], bank)
                for u in range(shared):
                    y_banks[(h, shared * k + u)] = sums[:, u, :]
                    second_stage_pass(h, shared * k + u, 0)

        out_view = out.rearrange("(t p) j -> p t j", p=P)

        def close_scores(h, group):
            j0, width = PIECES[h]
            for first in range(0, N // P, group):
                result = placed("result_%d_%d" % (h, first), [P, group, width], F32, RESULT_AT + (4 * j0 + first * width) / 256)
                for k in range(group):
                    second_stage_pass(h, first + k, 1)
                for k in range(group):
                    nt = first + k
                    nc.scalar.activation(result[:, k, :], y_banks[(h, nt)], SIGMOID, bias=c_t[:, nt : nt + 1])
                nc.sync.dma_start(out=out_view[:, first : first + group, j0 : j0 + width], in_=result[:])

        tab_sc = placed("tab_sc", [P, TABLE_SCALES_SPAN * KIB], U8, TABLE_SCALES_AT)
        nc.vector.memset(tab_sc[:, 0:T].bitcast(I32), 0)
        wg_sc = keep.tile([P, 2, H], U8, name="wg_sc", align_bytes=256)
        nc.gpsimd.memset(wg_sc[:].bitcast(I32), 0)
        v_sc = keep.tile([P, 2, S], U8, name="v_sc", align_bytes=256)
        nc.vector.memset(v_sc[:].bitcast(I32), 0)

        nc.sync.dma_start(offs_t[:], offs)
        load_table(0, 0, TABLE_CUT[0])
        load_wg_pass(0, 0, 2)
        load_wg_pass(1, 0, 1)
        for a in range(2):
            nc.sync.dma_start(out=tab_sc[4 * a : P : 8, 0:T].bitcast(I32), in_=tab_scales[a].bitcast(I32))
        load_table(0, TABLE_CUT[0], T)
        nc.sync.dma_start(pos1_t[:], pos1)
        nc.sync.dma_start(pos2_t[:], pos2)
        load_table(1, 0, TABLE_CUT[1])
        load_wg_scales(nc.gpsimd, wg_sc, 0, 8)
        deal_wg_scales(wg_sc)
        warm = keep.tile([P, 8], F32, name="warm")
        nc.vector.memset(warm[:, 0:1], 0.0)
        nc.scalar.activation(warm[:, 4:5], warm[:, 0:1], SIGMOID)

        gathered_sc = keep.tile([P, S], U8, name="gathered_sc", align_bytes=256)
        nc.vector.tensor_copy(gathered_sc[:], tab_sc[:, 0:T].indirect(offs_t[:]))
        for q in range(4):
            nc.sync.dma_start(
                out=v_sc[32 * q : 32 * q + 4, :, :].bitcast(I32),
                in_=gathered_sc[32 * q : 32 * q + 32 : 4, :].bitcast(I32),
            )
        load_table(1, TABLE_CUT[1], T)
        gather_first_pass()
        load_w1(0, 1)
        load_w1(1, 1)
        load_wg_pass(1, 1, 3)
        load_wg_pass(0, 2, 2)
        load_w1(2, 2)
        wg_high = load_wg(4, 4)
        load_w1(4, 4)
        ident = placed("ident", [P, P], F32, IDENT_AT)
        make_identity(nc, ident[:])
        for i in range(2):
            for d in range(2):
                gate_pass(i, d, 0)
        gather_second_pass(0)
        gather_second_pass(1)
        load_w2_natural()
        load_w2_dealt()
        c_t = keep.tile([P, N // P], F32, name="c_t")
        with nc.allow_non_contiguous_dma(reason="one bias value for each partition"):
            nc.sync.dma_start(out=c_t[:], in_=c.rearrange("(t p) -> p t", p=P))

        prepare_first_w1(0)
        prepare_first_w1(1)
        for d in range(2):
            gate_pass(0, d, 1)
            copy_gate(0, d)
        weight_sum(0, 0)
        weight_sum(0, 1)
        round_w1(gpsimd_round, 1, 1, 0, 0, 1)
        round_w1(scalar_round, 1, 1, 1, 0, 1)
        for d in range(2):
            gate_pass(1, d, 1)
            copy_gate(1, d)
        features(0, 0)
        features(0, 1)
        gate_sum(2, 0)
        gate_sum(2, 1)
        quantise_w1(1, 1)
        weight_sum(1, 0)
        weight_sum(1, 1)
        round_w1(gpsimd_round, 2, 2, 0, 0, 2)
        deal_wg_words(wg_high)
        round_w1(scalar_round, 2, 2, 1, 0, 1)
        round_w1(scalar_round, 2, 2, 1, 1, 2)
        pick_first(0)
        pick_second(0)
        gate_sum(3, 1)
        gate_sum(3, 0)
        turn(0)

        features(1, 0)
        features(1, 1)
        quantise_w1(2, 2)
        weight_sum(3, 1)
        weight_sum(2, 0)
        weight_sum(2, 1)
        weight_sum(3, 0)
        round_dealt(False, 4, 0)
        round_dealt(True, 5, 0)
        features(3, 1)
        round_dealt(True, 4, 1)
        round_dealt(True, 5, 1)
        gate_sum(4, 1)
        gate_sum(4, 0)
        pick_first(1)
        pick_second(1)
        turn(1)
        gate_sum(5, 1)
        gate_sum(5, 0)

        features(2, 0)
        features(2, 1)
        features(3, 0)
        pick_first(2)
        quantise_w1(4, 2)
        weight_sum(4, 1)
        weight_sum(4, 0)
        weight_sum(5, 1)
        gate_sum(6, 1)
        weight_sum(5, 0)
        gate_sum(6, 0)
        round_dealt(True, 6, 0)
        round_dealt(True, 7, 0)
        features(4, 1)
        round_dealt(False, 6, 1)
        round_dealt(True, 7, 1)
        pick_second(2)
        turn(2)
        gate_sum(7, 1)

        pick_first(3)
        pick_second(3)
        features(4, 0)
        turn(3)
        quantise_w1(6, 2)
        features(5, 1)
        round_w2(gpsimd_round, 0, 0, W2_EARLY)
        features(5, 0)
        weight_sum(6, 1)
        weight_sum(7, 1)
        gate_sum(7, 0)
        weight_sum(6, 0)
        weight_sum(7, 0)
        features(6, 1)
        features(7, 1)

        pick_second(4)
        pick_second(5)
        features(6, 0)
        features(7, 0)
        z_first = turn_back()
        for first in range(W2_EARLY, 2 * N, P):
            round_w2(scalar_round, first // N, first % N)
        pick_second(6)
        pick_second(7)
        pick_differences(0)
        quantise_w2(0, 0, W2_EARLY)
        quantise_w2(0, W2_EARLY, N - W2_EARLY)
        quantise_first_pass()
        open_scores(0)
        quantise_w2(1, 0, N)
        quantise_piece(0)
        pick_differences(1)
        close_scores(0, 2)
        open_scores(1)
        open_scores(2)
        quantise_piece(1)
        pick_differences(2)
        close_scores(1, 2)
        quantise_piece(2)
        close_scores(2, 1)
